import numpy as np, ml_dtypes
CORES = [3,11,19,27,35,43,51,59]
N = 8
BF = ml_dtypes.bfloat16
W, L, S, H, CP = 4096, 1024, 3, 2, 96
def parts(rng):
    x = np.minimum((128 * rng.random((N, 8, 16, W), dtype=np.float32) * (0.25 + 0.75 * rng.random((N, 8, 1, W), dtype=np.float32))).astype(np.int64), 127)
    share = np.zeros((N, 8, W)) + rng.choice(np.array([0.01, 0.03, 0.06]), (N, 8, 1))
    for t in range(S):
        B = W - 256 * (t + 1)
        share[:, :, B:B + 256] = rng.choice(np.array([0.3, 0.6, 0.9]) if t == 0 else np.array([0.1, 0.3, 0.5]), (N, 8, 1))
    mk = (rng.random((N, 8, W)) < share).astype(np.int64)
    return x, mk, rng.integers(0, 4096, (N, 8, 16, L)), rng.integers(0, 4096, (N, 8, S * 256)), rng.integers(0, 256, (N, 8, 16)), rng.choice(np.array([1, 8, 20, 40, 80]), (N, 8))
def pack(x, mk, oc, dl, wt, th):
    return {"xc": x.reshape(N, 128, W).astype(np.float32).astype(BF), "mk": mk.astype(np.float32).astype(BF), "oc": oc.reshape(N, 128, L).astype(np.int32),
            "dl": dl.astype(np.int32), "wt": wt.reshape(N, 128, 1).astype(np.int32), "th": th.reshape(N, 8, 1).astype(np.int32)}
def setup_inputs(rng):
    return pack(*parts(rng))
def setup_inputs_spread(rng):
    x, mk, oc, dl, wt, th = parts(rng)
    x = np.minimum((np.exp2(8 * rng.random((N, 8, 1, W))) * rng.random((N, 8, 16, W))).astype(np.int64), 127)
    mk = (rng.random((N, 8, W)) < np.exp2(-6 * rng.random((N, 8, 1)))).astype(np.int64)
    oc = np.minimum((4096 * rng.random((N, 8, 16, L)) ** 3).astype(np.int64), 4095)
    flip = rng.integers(0, 2, (N, 8, 1, 1)); oc = np.where(flip == 1, 4095 - oc, oc)
    wt = np.minimum((np.exp2(8 * rng.random((N, 8, 16))) - 1).astype(np.int64), 255)
    th = np.minimum(np.exp2(11 * rng.random((N, 8))).astype(np.int64), 2032)
    th[:, rng.integers(0, 8)] = 1
    return pack(x, mk, oc, dl, wt, th)
def setup_inputs_ends(rng):
    x, mk, oc, dl, wt, th = parts(rng)
    kind = rng.integers(0, 3, (N, 8, 1, W)); x = 127 * np.where(kind == 2, rng.integers(0, 2, (N, 8, 16, W)), kind)
    mk = rng.integers(0, 2, (N, 8, W))
    E = np.array([0] + [W - 256 * (t + 1) - 1 for t in range(S)])
    c = rng.integers(0, 3, (N, 8)); c[:, 0] = 2; c[N - 1, 7] = 1; c[N - 2, 7] = 0; c[0, 5] = 2
    for q in range(N):
        for g in range(8):
            x[q, g][:, E] = 127 * rng.integers(0, 2, (16, len(E))) if c[q, g] == 2 else 127 * c[q, g]
    x[:, :, :, W - 1] = 127; mk[:, :, W - 1] = 1; mk[N - 1, 7, E] = 1
    oc = 4095 * rng.integers(0, 2, (N, 8, 16, L)); oc[:, :, :15, ::7] = 0; oc[:, :, 15, ::7] = 4095; oc[:, :, :, L - 1] = 4095
    dl = 4095 * rng.integers(0, 2, dl.shape)
    wt = 255 * rng.integers(0, 2, wt.shape); wt[N - 1, 7] = 255; wt[0, 5] = 0; wt[:, 2, 0] = 0; wt[:, 2, 15] = 255
    th = np.where(rng.integers(0, 2, (N, 8)) == 1, 2032, 1); th[:, 0] = 1; th[:, 1] = 2032; th[N - 2, 7] = 2032
    return pack(x, mk, oc, dl, wt, th)
def setup_inputs_corners(rng):
    x, mk, oc, dl, wt, th = parts(rng); B = W - 256
    u = np.arange(4096); lv = ((u * u >> 5) + 37 * u) & (L - 1); top = int(np.argmax(lv)); place = int(lv[top])
    for q in range(N):
        for g in range(8):
            n = int((0, 1, CP - 1, CP, CP + 1, 256)[int(rng.integers(0, 6))])
            if q == 0: n = (CP, CP + 1, 256, CP, CP + 1, 256, CP, CP)[g]
            if q == 1: n = 0
            if q == 2: n = 63 if g == 7 else 0
            if q == 3: n = (CP - 1, 1, 0, CP, CP + 1, 256, CP - 1, CP)[g]
            o = rng.permutation(256); e = B + o[:n]; rest = B + o[n:]; T = (1, 127)[int(rng.integers(0, 2))]; th[q, g] = T
            xg = x[q, g]; xg[15, :B] = 0; xg[15, e] = 127; xg[:15, e[::2]] = 0; xg[:, rest] = 0
            if T == 127: xg[15, rest[::2]] = 126
            if g == 4: mk[q, g, :B] = 0
            if g == 6: mk[q, g, :B] = 1
            mk[q, g, e] = 1; mk[q, g, rest] = rng.integers(0, 2, 256 - n)
            if g == 0: wt[q, g] = 0
            if g == 1: wt[q, g] = 255
            if g == 2: oc[q, g] = 4095 * rng.integers(0, 2, (16, L))
            if g == 5: oc[q, g] = oc[q, g, :1].copy()
            if g % 4 == 3:
                wt[q, g] = 0; wt[q, g, 0] = 1; wt[q, g, 1] = 128
                xg[0, e[1::2]] = top & 127; xg[1, e[1::2]] = top >> 7
                oc[q, g, :, place] = 4095 * rng.integers(0, 2, 16); oc[q, g, :, 0] = 4095 * rng.integers(0, 2, 16)
    return pack(x, mk, oc, dl, wt, th)
def setup_inputs_crowd(rng):
    x, mk, oc, dl, wt, th = parts(rng); s = int(rng.integers(0, 8)); low = W - 256 * S
    for q in range(N):
        for g in range(8):
            kind = (g + s) % 8; xg = x[q, g]; odd = [W - 256 * (t + 1) + int(rng.integers(0, 256)) for t in range(S)]
            if kind == 7: continue
            mk[q, g, low:] = 1; th[q, g] = 1
            if kind in (0, 1, 4):
                keep = xg[:, odd].copy(); xg[:, low:] = xg[:, W - 1:W].copy()
                if kind == 1: xg[:, odd] = keep
                if kind == 4: mk[q, g, odd] = 0
            if kind == 2:
                three = xg[:, W - 3:].copy(); xg[:, low:] = three[:, rng.integers(0, 3, 256 * S)]
            if kind == 3: oc[q, g] = int(rng.integers(0, 4096))
            if kind in (5, 6): wt[q, g] = 0
            if kind == 6:
                wt[q, g, 15] = 1; xg[15, :] = 0; xg[15, odd] = 64
    return pack(x, mk, oc, dl, wt, th)
def setup_inputs_edges(rng):
    x, mk, oc, dl, wt, th = parts(rng); B = W - 256; low = W - 256 * S
    p = [int(a) for a in rng.permutation(8)]; z = p[0]; e = int(rng.integers(0, N)); s = (e + 1) % N
    u = np.arange(4096); lv = ((u * u >> 5) + 37 * u) & (L - 1); pl, first = np.unique(lv, return_index=True); first = first[pl >= 64]
    x[:, z, :, low:] = rng.integers(64, 128, (N, 16, 256 * S)); x[:, z, :, 0] = 0; x[:, z, :, W // 8:W // 2] = 0
    mk[:, z, W // 8:W // 2] = 0; oc[:, z, :, :64] = 0; wt[:, z] = 0
    for t in range(S):
        Bt = W - 256 * (t + 1); c = W // 2 - 1 - t
        x[:, z, :, c] = 127; dl[:, z, t * 256:(t + 1) * 256] = -((-c * 4096) // Bt); mk[:, z, Bt + 255] = 1
    for q in range(N):
        for g, pair in ((p[1], (257, 385)), (p[2], (513, 1001))):
            T = pair[int(rng.integers(0, 2))]; th[q, g] = T
            x[q, g, 4:, :B] = 0; x[q, g, :, B:] = 0; mk[q, g, B:] = rng.integers(0, 2, 256)
            o = B + rng.permutation(256)[:40]; tot = T - (np.arange(40) & 1); dv = rng.integers(-20, 21, (6, 40))
            v = np.concatenate([dv, -dv]) + tot // 12; v[11] += tot % 12
            x[q, g][4:, o] = v; mk[q, g, o] = 1
        g = p[3]; two = [int(a) for a in rng.permutation(low)[:2]]
        for k, c in ((0, two[0]), (int(rng.integers(1, 16)), two[1])):
            oc[q, g, k] = -((-c * 4096) // B); x[q, g, :, c] = 127; mk[q, g, c] = 1
        x[q, g, int(rng.integers(0, 16)), two[0]] = 126 * int(rng.integers(0, 2)); x[q, g, :, B::2] = 127; mk[q, g, B::2] = 1
        g = p[4]; us = rng.permutation(first)[:256]
        wt[q, g] = 0; wt[q, g, 0] = 1; wt[q, g, 1] = 128; x[q, g, :2, :B] = 0
        x[q, g, 0, B:] = us & 127; x[q, g, 1, B:] = us >> 7; mk[q, g, B:] = 1
        oc[q, g] = oc[q, g] & 4094; dl[q, g, :256] = dl[q, g, :256] | 1
    mk[s, p[:1] + p[3:], B:] = 0
    x[e, :, :, W - 512:W - 256] = 0
    return pack(x, mk, oc, dl, wt, th)
def check_inputs(d):
    bad = []
    for k, lo, hi in (("xc", 0, 127), ("mk", 0, 1), ("oc", 0, 4095), ("dl", 0, 4095), ("wt", 0, 255), ("th", 1, 2032)):
        v = np.asarray(d[k]).astype(np.float64)
        if not (np.min(v) >= lo and np.max(v) <= hi): bad.append("range of " + k)
        elif np.any(v != np.floor(v)): bad.append("whole numbers of " + k)
    return bad
def hop(y, x, m, o, w, A, B):
    n = y.shape[2]
    u = np.add.reduce(w[:, :, None] * y, axis=1) & 4095
    l = ((u * u >> 5) + 37 * u + A) & (L - 1)
    c = (np.take_along_axis(o, l[:, None, :], 2) * B) >> 12
    cc = c.reshape(8, 16 * n)
    v = np.take_along_axis(x, cc[:, None, :], 2).reshape(8, 16, 16, n)
    s = np.add.reduce(np.minimum(v, y[:, :, None, :]), axis=1) + 256 * np.take_along_axis(m, cc, 1).reshape(8, 16, n)
    k = np.argmax(s, axis=1)
    return l, s, np.take_along_axis(c, k[:, None, :], 1)[:, 0]
def reference(xc, mk, oc, dl, wt, th):
    x = xc.astype(np.float32).astype(np.int64).reshape(N, 8, 16, W); m = mk.astype(np.float32).astype(np.int64).reshape(N, 8, W)
    o = oc.astype(np.int64).reshape(N, 8, 16, L); w = wt.astype(np.int64).reshape(N, 8, 16); d = dl.astype(np.int64); lim = th.astype(np.int64).reshape(N, 8, 1)
    A = [0] * N; ya = np.full((N, 8, S, H, 256), -1, np.int64)
    for t in range(S):
        B = W - 256 * (t + 1)
        box = np.zeros((N, 8, 16, CP), np.int64); full = np.zeros((N, 8, CP), bool)
        for r in range(N):
            y = x[r, :, :, B:B + 256]; live = m[r, :, B:B + 256] == 1
            for h in range(H):
                l, s, a = hop(y, x[r], m[r], o[r], w[r], A[r], B)
                ya[r, :, t, h] = np.where(live, a, -1)
                for g in range(8): m[r, g, a[g][live[g]]] = 1
                y = np.maximum(y - np.take_along_axis(x[r], a[:, None, :], 2), 0)
            k = np.argmin(s, axis=1)
            go = live & (np.add.reduce(y, axis=1) >= lim[r])
            for g in range(8):
                i = np.flatnonzero(live[g]); i = i[np.unique(l[g, i], return_index=True)[1]]
                o[r, g, k[g, i], l[g, i]] = d[r, g, t * 256 + i]
                j = np.flatnonzero(go[g])[:CP]
                box[r, g, :, :len(j)] = y[g][:, j]; full[r, g, :len(j)] = True
        for r in range(N):
            q = (r - 1 - t % (N - 1)) % N
            l, s, a = hop(box[q], x[r], m[r], o[r], w[r], A[r], B)
            for g in range(8): m[r, g, a[g][full[q, g]]] = 1
            A[r] = int(np.count_nonzero(full[q])) & 63
    return {"ya": ya.reshape(N, 8, S * H * 256).astype(np.float32), "ym": m.astype(np.float32).astype(BF), "yo": o.reshape(N, 128, L).astype(np.float32)}

@@ -1,0 +1,721 @@
+from concourse.mybir import AluOpType, ActivationFunctionType
+A = AluOpType
+F = ActivationFunctionType
+W, L, NS, CP = 4096, 1024, 3, 96
+BF, F32, I32, U16, H16 = "bfloat16", "float32", "int32", "uint16", "float16"
+
+_S = {
+    "x": (4096, BF), "M": (4112, F32), "GF": (256, F32), "NI": (1024, I32), "NM": (1040, F32), "DI": (768, I32),
+    "WI": (8, I32), "TI": (8, I32), "PI": (8, I32), "C": (32, F32), "IC": (144, F32), "GC": (128, F32),
+    "RC": (256, F32), "OH": (16, F32), "OHn": (16, F32), "EQ": (64, F32), "Z1": (128, F32), "Z2": (128, F32), "Z": (128, F32),
+    "Wp": (144, BF), "Wn": (144, BF), "Wk": (144, BF), "Wm": (144, BF), "Wa": (144, BF), "Wl": (144, BF),
+    "LX": (128, H16), "cX": (16, U16), "OHh": (16, H16), "Ws": (144, BF), "WyA": (64, BF), "WyL": (64, BF), "Ib": (128, BF), "Ih": (128, H16),
+    "BLK": (128, BF), "BLKh": (128, H16), "TRb": (128, BF), "DLO": (128, BF), "O16": (128, BF), "DW": (2048, H16),
+    "TRa": (256, BF), "TRl": (256, BF), "RSx": (256, BF), "RSn": (256, BF), "RSd": (256, BF), "KC": (256, BF),
+    "CLn": (32, BF), "CLp": (32, BF), "SI": (16, F32), "cT": (16, U16), "TH": (16, H16), "Ab": (8, F32),
+    "L0": (32, I32), "GA": (1536, BF), "GAr": (96, BF), "YA": (256, F32),
+    "ny0": (256, BF), "ny1": (256, BF), "NO": (256, F32), "DF": (256, F32), "TT": (256, F32),
+    "SN": (256, F32), "kn1": (16, I32), "kn2": (16, I32), "kn": (16, U16),
+    "RD": (16, BF), "PRE": (32, BF), "NRC": (16, BF), "SL": (16, U16), "ON": (16, BF), "a1": (8, I32), "a2": (8, I32), "NF": (16, BF),
+}
+for _k in ("0", "1", "r"):
+    _n = 1536 if _k == "r" else 4096
+    _S.update({"mn" + _k: (_n, BF), "G" + _k: (_n, BF), "co" + _k: (256, U16), "SX" + _k: (256, F32),
+               "p1" + _k: (16, I32), "p2" + _k: (16, I32), "po" + _k: (16, U16),
+               "u1" + _k: (32, I32), "u2" + _k: (32, I32), "u3" + _k: (32, F32), "u4" + _k: (32, F32), "lo" + _k: (32, U16)})
+for _k in ("a", "l"):
+    _S.update({"v" + _k: (16, H16), "AB" + _k: (256, F32), "SD" + _k: (256, F32), "OF" + _k: (32, U16)})
+for _t in range(NS):
+    _S.update({"yr%d" % _t: (4096, BF), "yT%d" % _t: (256, BF), "box%d" % _t: (784, BF), "LB%d" % _t: (112, BF), "LV%d" % _t: (256, BF)})
+_S.update({"yr1h": (4096, BF), "yT1h": (256, BF), "yrr": (1536, BF)})
+_S.update({"LC0": (2, BF), "LC1": (2, BF)})
+_OWN = ("WI", "TI", "YA", "LB0", "LB1", "LB2", "LC0", "LC1")
+_AT, SCRATCH = {}, {}
+for _k, (_n, _d) in _S.items():
+    if _n > 256 or _k in _OWN:
+        SCRATCH[_k] = ("sbuf", [128, _n], _d)
+        _AT[_k] = (_k, 0)
+    else:
+        _o = SCRATCH.get("pool_" + _d, (0, [0, 0]))[1][1]
+        SCRATCH["pool_" + _d] = ("sbuf", [128, _o + (_n + 31) // 32 * 32], _d)
+        _AT[_k] = ("pool_" + _d, _o)
+_PS = ("pK0", "pK1", "pU", "pA", "pD", "pX", "pS", "pY")
+SCRATCH.update({k: ("psum", [128, 512], F32) for k in _PS})
+SEMAPHORES = ["V", "S", "P", "G", "sent", "arr0", "arr1", "arr2", "cnt0", "cnt1"] + ["d%d" % i for i in range(12)]
+
+K = {"cyc": 1.0, "g": 1.3, "sc": 3.2, "pe": 0.5, "lat": 100.0, "fix": 30.0, "look": 250.0, "look2": 1.0, "vpen": 20000.0,
+     "ch0": [2] * 7 + [1, 1], "ch1": [2] * 7 + [1, 1], "chr": [4, 4, 4, 2, 2], "spr": "VS", "early": 0,
+     "sp0": [(128, "VS"), (128, "VSG")], "sp1": [(128, "VS"), (128, "VSG")]}
+K.update({"wt": (120e3, 95e3, 160e3, 150e3), "rounds": 40, "seed": 1, "noise": 1000.0})
+MODS = [dict(cyc=1.0, g=1.3, sc=3.2, pe=.5, lat=100., rem=2800.), dict(cyc=.83, g=.92, sc=1.7, pe=.42, lat=60., rem=2000.),
+        dict(cyc=1.2, g=1.66, sc=4.6, pe=.6, lat=180., rem=4000.), dict(cyc=1.0, g=1.3, sc=3.2, pe=.9, lat=150., rem=2800.)]
+SILU1 = 1.2784645427610738
+BOOST = {'pK1<mn1': -1000, 'C<OH': -2000, 'OHh<OH': 5000, 'SN<RSn': 5000, 'M<M': -2000, 'NF<SI': -500, 'u41<u31': -2000, 'GF<GA': 500, 'Wl<IC': -1500, 'box2<ny1': -2000, 'yrr<LB1': 200, 'VGr<M': -18500, 'yrr<LB0': 2000, 'yT1<x': 2000, 'Vyr0<yT0': -21000, 'ny0<mn0': -500, 'NM<NO': -5000, 'u10<pU': 5000, 'SX1<RSx': 2000, 'Gr<M': 700, 'TT<OH': -4000, 'LX<u21': -5000, 'OFl<SDl': -1000, 'lo1<pX': 5500, 'u2r<u1r': 500, 'pS<RD': 1000, 'vl<pX': -2000, 'yrr<LB2': 1000, 'pS<PRE': -5000, 'pS<CLp': -5000, 'kn<kn2': -2000, 'SDl<RSd': -5000, 'PRE<ON': -500, 'yT1h<ny0': 5000, 'GA<G0': 500, 'pK1<G1': -2000, 'pK1<KC': 5000}
+_CACHE = {}
+
+
+def _clash(a, b):
+    if a[1] != b[1] or a[2] >= b[3] or b[2] >= a[3]:
+        return False
+    if a[4] > 1 and a[4] == b[4] and (a[2] - b[2]) % a[4]:
+        return False
+    return True
+
+
+def build(g, core, T, topo, rank):
+    ops = []
+    cyc = K["cyc"]
+
+    def R(name, a=0, b=None, s=1, parts=None):
+        real, o = _AT.get(name, (name, 0))
+        b = _S[name][0] if b is None else b
+        ps = slice(None) if parts is None else parts
+        return (T[real][ps, o + a:o + b:s] if s > 1 else T[real][ps, o + a:o + b], name, a, b, s)
+
+    def cnt(r):
+        return (r[3] - r[2] + r[4] - 1) // r[4]
+
+    def two(*rs):
+        return all(r[1] in _S and _S[r[1]][1] in (BF, H16, U16) for r in rs)
+
+    def add(alts, reads, writes, **kw):
+        o = {"alts": alts, "r": [r for r in reads if isinstance(r, tuple)], "w": list(writes), "grp": None, "sem": None, "lat": 0.0}
+        o.update(kw)
+        ops.append(o)
+
+    def ap(s):
+        return s[0] if isinstance(s, tuple) else s
+
+    def vcost(n, half):
+        return K["fix"] + max(64, n * (0.5 if half else 1.0)) * cyc
+
+    def gcost(n, e):
+        return (50 if e == "V" else 65) + n * K["g"]
+
+    def ts(out, in0, s1, s2, op0, op1=None, off=None):
+        def f(q):
+            i = in0[0].indirect(off[0]) if off else in0[0]
+            if op1 is None:
+                return q.tensor_scalar(out[0], i, ap(s1), None, op0)
+            return q.tensor_scalar(out[0], i, ap(s1), ap(s2), op0, op1)
+        add({"V": (f, gcost(cnt(out), "V") if off else vcost(cnt(out), two(out, in0)))}, [in0, s1, s2, off], [out])
+
+    def tt(out, in0, in1, op, off=None, scat=None):
+        def f(q):
+            return q.tensor_tensor(out[0].indirect(scat[0]) if scat else out[0], in0[0].indirect(off[0]) if off else in0[0], in1[0], op)
+        if scat:
+            c = 50 + cnt(in0) * K["sc"]
+        elif off:
+            c = gcost(cnt(out), "V")
+        else:
+            c = vcost(cnt(out) * (1 if in0[1] in _PS or in1[1] in _PS else 2), False)
+        add({"V": (f, c)}, [in0, in1, off, scat], [out])
+
+    def cp(out, in_, scat=None):
+        def f(q):
+            return q.tensor_copy(out[0].indirect(scat[0]) if scat else out[0], in_[0])
+        add({"V": (f, 50 + cnt(in_) * K["sc"] if scat else vcost(cnt(out), two(out, in_)))}, [in_, scat], [out])
+
+    def ms(out, v):
+        add({"V": (lambda q: q.memset(out[0], v), vcost(cnt(out), two(out)))}, [], [out])
+
+    def scan(out, d0, d1, op0, op1):
+        add({"V": (lambda q: q.tensor_tensor_scan(out[0], d0[0], d1[0], 0.0, op0, op1), vcost(cnt(out), two(out, d0, d1)))}, [d0, d1], [out])
+
+    def act(out, in_, func=F.Identity, scale=1.0, bias=0.0, off=None, scat=None):
+        if scat:
+            add({"S": (lambda q: q.activation(out[0].indirect(scat[0]), in_[0], func), 65 + cnt(in_) * K["sc"])}, [in_, scat], [out])
+            return
+
+        def f(q):
+            return q.activation(out[0], in_[0].indirect(off[0]) if off else in_[0], func, bias=ap(bias), scale=ap(scale))
+        add({"S": (f, gcost(cnt(out), "S") if off else vcost(cnt(out), False))}, [in_, scale, bias, off], [out])
+
+    def flex(out, in_, engs, scale=1.0, bias=None, off=None):
+        n = cnt(out)
+        alts = {}
+
+        def src():
+            return in_[0].indirect(off[0]) if off else in_[0]
+        if "V" in engs:
+            def fv(q):
+                if bias is not None:
+                    return q.tensor_scalar(out[0], src(), bias[0], None, A.add)
+                if scale != 1.0:
+                    return q.tensor_scalar(out[0], src(), scale, None, A.mult)
+                return q.tensor_copy(out[0], src())
+            alts["V"] = (fv, gcost(n, "V") if off else vcost(n, two(out, in_)))
+        if "S" in engs:
+            alts["S"] = (lambda q: q.activation(out[0], src(), F.Identity, bias=0.0 if bias is None else bias[0], scale=scale),
+                         gcost(n, "S") if off else vcost(n, False))
+        if "G" in engs:
+            alts["G"] = (lambda q: q.affine_select(out[0], in_[0], [[0, n]], A.is_ge, 0.0, 0, 0), 170 + 2 * n * cyc)
+        add(alts, [in_, bias, off], [out])
+
+    def iota(out, pat, base, cm):
+        fl = _S[out[1]][1] != I32
+        add({"G": (lambda q: q.iota(out[0], pat, base, cm, allow_small_or_imprecise_dtypes=True) if fl else q.iota(out[0], pat, base, cm),
+                   130 + 2 * cnt(out) * cyc)}, [], [out])
+
+    gid = [0]
+
+    def group():
+        gid[0] += 1
+        return [gid[0], True]
+
+    def mm(gr, out, lhsT, rhs):
+        first = gr[1]
+        gr[1] = False
+        add({"P": (lambda q, stop: q.matmul(out[0], lhsT[0], rhs[0], first, stop), max(64, cnt(out)) * K["pe"])},
+            [lhsT, rhs], [out], grp=gr[0], first=first)
+
+    nd = [0]
+
+    def dma(e, pairs, reads, writes, ns):
+        s = "d%d" % nd[0]
+        nd[0] += 1
+
+        def f(q):
+            for o, i in pairs:
+                q.dma_start(o, i).then_inc(T.sem[s], 16)
+        add({e: (f, 60.0 * len(pairs))}, reads, writes, sem=(s, 16 * len(pairs)), lat=ns)
+
+    def sl(name, j):
+        return R(name, 15 - j, 143 - j)
+
+    def col(j):
+        return R("C", j, j + 1)
+
+    def oh(j):
+        return R("OH", j, j + 1)
+
+    B0 = W - 256
+    dma("Y", [(T.WI[:, 0:1], T.wt[:])], [], [R("WI")], 1900)
+    dma("Y", [(T.x[:, B0:W], T.xc[:, B0:W])], [], [R("x", B0, W)], 2200)
+    dma("Y", [(T.NI[:], T.oc[:])], [], [R("NI")], 4200)
+    dma("Y", [(T.x[:, 0:B0], T.xc[:, 0:B0])], [], [R("x", 0, B0)], 6500)
+    for j in range(4):
+        ops[j]["boost"] = 1e6 * (4 - j)
+    iota(R("PI", 0, 1), [[0, 1]], 0, 1)
+    iota(R("IC"), [[1, 144]], 0, 0)
+    ts(R("PI", 1, 2), R("PI", 0, 1), 15, None, A.bitwise_and)
+    ts(R("PI", 2, 3), R("PI", 0, 1), 112, None, A.bitwise_and)
+    cp(R("C", 0, 3), R("PI", 0, 3))
+    ts(col(3), R("PI", 2, 3), 15.0, None, A.add)
+    cp(col(4), R("WI", 0, 1))
+    ts(col(5), R("WI", 0, 1), -1.0, None, A.mult)
+
+    def slide(name, c, n=144, at=3):
+        ts(R(name, 0, n), R("IC", 0, n), col(at), c, A.is_equal, A.mult)
+    slide("Wp", col(4))
+    slide("Wn", col(5))
+    ts(R("OH"), R("IC", 0, 16), col(1), None, A.is_equal)
+    ts(col(6), col(1), 16.0, None, A.mult)
+    ts(R("cT"), R("IC", 0, 16), col(6), None, A.add)
+    ts(R("EQ"), R("IC", 0, 64), oh(2), None, A.mult)
+    ts(col(22), oh(2), oh(1), 64.0, A.add, A.mult)
+    tt(col(23), col(22), oh(3), A.add)
+    ts(R("M", 16, 80), R("IC", 0, 64), oh(1), col(23), A.mult, A.add)
+    for w in (64, 256, 1024):
+        for j in (1, 2, 3):
+            flex(R("M", 16 + j * w, 16 + (j + 1) * w), R("M", 16, 16 + w), "VS", bias=R("EQ", j * w // 64, j * w // 64 + 1))
+    dma("G", [(T.M[0:128:16, 16:16 + W], T.mk[:])], [], [R("M", 16, 16 + W)], 3000)
+    ms(R("TI", 0, 1), 0)
+    dma("Y", [(T.TI[0:128:16, 0:1], T.th[:])], [], [R("TI")], 1900)
+    dma("Y", [(T.DI[r:128:16, :], T.dl[:]) for r in range(16)], [R("x")], [R("DI")], 3500)
+    slide("Wk", 4096.0)
+    ts(col(7), oh(0), 1048576.0, None, A.mult)
+    slide("Wm", col(7))
+    ts(R("Ib"), R("IC", 0, 128), col(0), None, A.is_equal)
+    iota(R("KC"), [[-16, 16], [0, 16]], 240, 0)
+    for nm, a, b in (("RSx", 1.0, -1e8), ("RSn", -1.0, 1e8), ("RSd", 0.0, 1e9)):
+        ms(R(nm), a)
+        ms(R(nm, 0, 256, 16), b)
+    ts(col(8), col(1), 256.0, 255.0, A.mult, A.add)
+    ts(col(9), col(1), 96.0, 255.0, A.mult, A.add)
+    ts(col(24), oh(0), oh(3), None, A.add)
+    ts(col(10), col(24), -1.0, 1.0, A.mult, A.add)
+    ts(col(25), col(24), SILU1, None, A.mult)
+    ts(col(11), oh(2), 64.0, oh(1), A.mult, A.add)
+    ts(col(26), oh(3), -4160.0, col(11), A.mult, A.add)
+    ts(col(12), oh(3), -6208.0, col(11), A.mult, A.add)
+    slide("Wa", col(12))
+    ts(col(13), oh(3), -8192.0, None, A.mult)
+    ts(col(14), oh(0), 8192.0, col(13), A.mult, A.add)
+    slide("Wl", col(14))
+    ts(R("cX", 0, 8), R("IC", 0, 8), 0.0, col(1), A.mult, A.add)
+    cp(R("OHh"), R("OH"))
+    slide("Ws", -1.0)
+    ts(col(17), col(2), 0.375, 5.0, A.mult, A.add)
+    slide("WyA", col(26), 64, 17)
+    slide("WyL", col(14), 64, 17)
+    iota(R("GC"), [[16, 8], [0, 16]], 0, 0)
+    iota(R("RC"), [[0, 16], [1, 16]], 0, 0)
+    ts(R("Ih"), R("IC", 0, 128), col(0), None, A.is_equal)
+    ts(R("BLK"), R("GC"), col(2), None, A.is_equal)
+    ts(R("BLKh"), R("GC"), col(2), None, A.is_equal)
+    ts(R("Z1"), R("GC"), col(2), -8192.0, A.is_equal, A.mult)
+    ts(R("Z2"), R("IC", 0, 128), col(0), 16384.0, A.is_equal, A.mult)
+    tt(R("Z"), R("Z1"), R("Z2"), A.add)
+    ts(R("OHn"), R("OH"), -8192.0, None, A.mult)
+    for s in range(15):
+        ts(R("DW", 128 * s, 128 * s + 128), R("Z"), R("OHn", s, s + 1), None, A.max)
+    for nm, v in (("TRa", 2064.0), ("TRl", 16.0)):
+        ts(R(nm), R("RC"), col(1), 67108864.0, A.is_ge, A.mult)
+        ms(R(nm, 15, 256, 16), v)
+    ts(R("Z1"), R("RC", 0, 128), col(1), None, A.is_ge)
+    tt(R("TRb"), R("Z1"), R("BLK"), A.mult)
+    ts(col(18), col(1), -1.0, None, A.mult)
+    ts(R("DLO"), R("IC", 0, 128), col(0), col(18), A.is_equal, A.mult)
+    ts(col(19), col(1), -1.0, None, A.add)
+    ms(R("O16"), 1.0 / 16)
+    ms(R("ON"), 1.0)
+    ms(R("PRE", 0, 1), 0.0)
+    iota(R("CLn", 0, 16), [[-16, 16]], -256, 0)
+    iota(R("CLp", 0, 16), [[16, 16]], 256, 0)
+    ms(R("CLp", 16, 17), 0.0)
+    ts(col(20), col(1), 6.0, None, A.mult)
+    ts(R("SI", 0, 6), R("IC", 0, 6), col(20), None, A.add)
+    ts(col(21), R("TI", 0, 1), -1.0, None, A.mult)
+    ts(R("TH"), R("ON"), col(21), None, A.mult)
+    for t in range(NS):
+        ms(R("box%d" % t, 0, 112), 0.0)
+    cp(R("NM", 16, 1040), R("NI"))
+    AB0 = 312 - 0.40625
+
+    def place(k, n, ab, out=None):
+        cp(R("u1" + k, 0, n), R("pU", 0, n))
+        ts(R("u2" + k, 0, n), R("u1" + k, 0, n), 4095, None, A.bitwise_and)
+        ts(R("u3" + k, 0, n), R("u2" + k, 0, n), 592.0, None, A.add)
+        tt(R("u4" + k, 0, n), R("u3" + k, 0, n), R("u3" + k, 0, n), A.mult)
+        if out:
+            ts(out, R("u4" + k, 0, n), 1.0 / 32, ab, A.mult, A.add)
+            return
+        ts(R("u1" + k, 0, n), R("u4" + k, 0, n), 1.0 / 32, ab, A.mult, A.add)
+        place2(k, n)
+
+    def place2(k, n):
+        ts(R("u2" + k, 0, n), R("u1" + k, 0, n), 1023, None, A.bitwise_and)
+        cp(R("lo" + k, 0, n), R("u2" + k, 0, n))
+
+    def umm(o, wn, rhs):
+        gr = group()
+        for j in range(16):
+            mm(gr, o, sl(wn, j), rhs(j))
+
+    def columns(k, n, t, names):
+        ts(R("co" + k, 0, 16 * n), names, (15 - t) / 16.0, -15.0 / 32, A.mult, A.add, off=R("lo" + k, 0, n))
+
+    def spread(yr, src, parts, scale=1.0):
+        b = 0
+        for n, e in parts:
+            a, b = b, b + n
+            for k in range(16):
+                flex(R(yr, 16 * a + k, 16 * b, 16), R(src[0], src[1] + a, src[1] + b), e, scale=scale)
+
+    def scores(k, n, B, yr, pk):
+        gr = group()
+        w = 16 * n
+        mm(gr, R(pk, 0, w), R("Ib"), R("KC", 0, w))
+        for nm, wn in (("mn", "Wk"), ("G", "Wm")):
+            a = 0
+            for ch in K["ch" + k]:
+                o = R("co" + k, n * a, n * (a + ch))
+                if nm == "mn":
+                    tt(R(nm + k, w * a, w * (a + ch)), R("x", 0, B), R(yr, w * a, w * (a + ch)), A.min, off=o)
+                else:
+                    flex(R(nm + k, w * a, w * (a + ch)), R("M", 16, 16 + B), "VS", off=o)
+                ops[-1]["rest"] = (16 - a - ch) * w * K["g"]
+                for j in range(a, a + ch):
+                    mm(gr, R(pk, 0, w), sl(wn, j), R(nm + k, w * j, w * j + w))
+                a += ch
+
+    def best(k, n, pk, pc):
+        w = 16 * n
+        scan(R("SX" + k, 0, w), R("RSx", 0, w), R(pk, 0, w), A.add, A.max)
+        cp(R("p1" + k, 0, n), R("SX" + k, 15, w, 16))
+        ts(R("p2" + k, 0, n), R("p1" + k, 0, n), 4095, None, A.bitwise_and)
+        ts(R("po" + k, 0, n), R("p2" + k, 0, n), -1.0, pc, A.mult, A.add)
+
+    def first_of(k, n, tri, pd):
+        w = 16 * n
+        gr = group()
+        mm(gr, R(pd, 0, w), R("Ib"), R(tri, 0, w))
+        for s in range(16):
+            mm(gr, R(pd, s, w, 16), R("DW", 128 * s, 128 * s + 128) if s < 15 else R("Ih"), R("v" + k, 0, n))
+        act(R("AB" + k, 0, w), R(pd, 0, w), F.Abs)
+        scan(R("SD" + k, 0, w), R("RSd", 0, w), R("AB" + k, 0, w), A.add, A.min)
+        ts(R("OF" + k, 0, 2 * n, 2), R("SD" + k, 15, w, 16), col(1), None, A.max)
+
+    def mark(k, n, B, ga, dead):
+        a0 = ga[2]
+        act(ga, R("G" + k, 0, 256 * n), off=R("po" + k, 0, n))
+        act(R("GF", 0, 16 * n), ga, scale=col(10), bias=col(25))
+        gr = group()
+        dead(gr, R("pA", 0, n))
+        for j in range(16):
+            mm(gr, R("pA", 0, n), sl("Wa", j), R(ga[1], a0 + j, a0 + 16 * n, 16))
+        ts(R("va", 0, n), R("pA", 0, n), -2064.0, None, A.max)
+        first_of("a", n, "TRa", "pD")
+        for j in range(n):
+            act(R("M", 0, 16 + B), R("GF", 16 * j, 16 * j + 16), F.Silu, scat=R("OFa", 2 * j, 2 * j + 1))
+
+    def not_live(t, wn="Wl"):
+        def f(gr, o):
+            for j in range(16):
+                mm(gr, o, sl(wn, j), R("LV%d" % t, j, 256, 16))
+        return f
+
+    umm(R("pU", 0, 16), "Wp", lambda j: R("x", B0 + 16 * j, B0 + 16 * j + 16))
+    place("0", 16, AB0)
+    for t in range(NS):
+        B = W - 256 * (t + 1)
+        flex(R("yT%d" % t), R("x", B, B + 256), "S", off=R("cT"))
+    spread("yr0", ("yT0", 0), K["sp0"])
+    for t in (1, 2):
+        B = W - 256 * (t + 1)
+        umm(R("pU", 16 * t - 16, 16 * t), "Wp", lambda j: R("x", B + 16 * j, B + 16 * j + 16))
+    place("1", 32, AB0, out=R("L0"))
+    for t in (1, 2):
+        spread("yr%d" % t, ("yT%d" % t, 0), [(256, "G")])
+    gy = group()
+    py = R("pY", 0, 256, parts=slice(0, 48))
+    N = len(T.cores)
+    for t in range(NS):
+        B = W - 256 * (t + 1)
+        ab = AB0 if t == 0 else R("Ab", t, t + 1)
+        flex(R("LV%d" % t), R("M", 16 + B, 16 + B + 256), "VS")
+        if t:
+            mm(group(), R("pS", 64, 65), R("O16"), R("LC%d" % (t - 1), 1, 2) if K["early"] else R("LB%d" % (t - 1), 15, 16))
+            cp(R("a1", 0, 1), R("pS", 64, 65))
+            ts(R("a2", 0, 1), R("a1", 0, 1), 63, None, A.bitwise_and)
+            ts(ab, R("a2", 0, 1), AB0, None, A.add)
+            ts(R("u10", 0, 16), R("L0", 16 * t - 16, 16 * t), ab, -AB0, A.add, A.add)
+            place2("0", 16)
+        columns("0", 16, t, R("NM", 16, 1040) if t else R("NI"))
+        scores("0", 16, B, "yr%d" % t, "pK0")
+        best("0", 16, "pK0", col(8))
+        tt(R("ny0"), R("mn0"), R("x", B, B + 256), A.subtract, off=R("po0"))
+        ga0 = R("GA", 512 * t, 512 * t + 256)
+        umm(R("pU", 0, 16), "Wn", lambda j: R("ny0", 16 * j, 16 * j + 16))
+        place("1", 16, ab)
+        columns("1", 16, t, R("NM", 16, 1040))
+        flex(R("yT1h"), R("ny0"), "S", scale=-1.0, off=R("cT"))
+        mark("0", 16, B, ga0, not_live(t))
+        spread("yr1h", ("yT1h", 0), K["sp1"])
+        scores("1", 16, B, "yr1h", "pK1")
+        tt(R("LX"), R("u21", 0, 16), R("BLK"), A.mult, off=R("cX", 0, 8))
+        gr = group()
+        not_live(t)(gr, R("pX", 0, 16))
+        mm(gr, R("pX", 0, 16), R("LX"), R("OHh"))
+        ts(R("vl"), R("pX", 0, 16), -16.0, None, A.max)
+        ts(R("lo1", 16, 32), R("pX", 0, 16), 0.0, None, A.max)
+        act(R("NO"), R("NM", 16, 1040), off=R("lo1", 16, 32))
+        tt(R("DF"), R("NM", 16, 1040), R("DI", 256 * t, 256 * t + 256), A.subtract, off=R("lo1", 16, 32))
+        first_of("l", 16, "TRl", "pX")
+        best("1", 16, "pK1", col(8))
+        tt(R("ny1"), R("mn1"), R("ny0"), A.add, off=R("po1"))
+        box, lb = "box%d" % t, "LB%d" % t
+        gr = group()
+        mm(gr, R("pS", 0, 16), R("BLKh"), R("TH"))
+        not_live(t)(gr, R("pS", 0, 16))
+        for j in range(16):
+            mm(gr, R("pS", 0, 16), sl("Ws", j), R("ny1", j, 256, 16))
+        ts(R("RD"), R("pS", 0, 16), 0.0, None, A.is_ge)
+        scan(R("PRE", 1, 17), R("ON"), R("RD"), A.mult, A.add)
+        tt(R("NRC"), R("RD"), R("CLn", 0, 16), A.mult)
+        gr = group()
+        mm(gr, R("pS", 32, 49), R("Ib"), R("CLp", 0, 17))
+        mm(gr, R("pS", 32, 48), R("TRb"), R("RD"))
+        mm(gr, R("pS", 32, 48), R("DLO"), R("RD"))
+        mm(gr, R("pS", 32, 48), R("Ib"), R("NRC"))
+        mm(gr, R("pS", 32, 49), R("BLK"), R("PRE", 0, 17))
+        ts(R("SL"), R("pS", 32, 48), col(19), None, A.add)
+        ts(R(box, 15, 16), R("pS", 48, 49), float(CP), None, A.min)
+        cp(R(box, 16, 784), R("ny1"), scat=R("SL"))
+        dst = T.cores[(rank + 1 + t % (N - 1)) % N]
+        rid, pid, _se = topo.addr(dst)
+
+        def put(q, box=box, lb=lb, t=t, dst=dst, rid=rid, pid=pid):
+            q.remote_dma(T[lb][:], T[box][:, 0:112], T.sem["arr%d" % t], T.sem.sent, pid, rid, topo.mask(core, dst))
+        ne = len(topo.engines(core, dst))
+        if t < NS - 1 and K["early"]:
+            def putc(q, box=box, t=t, dst=dst, rid=rid, pid=pid):
+                q.remote_dma(T["LC%d" % t][:], T[box][:, 14:16], T.sem["cnt%d" % t], T.sem.sent, pid, rid, topo.mask(core, dst))
+            add({"G": (putc, 300.0)}, [R(box, 14, 16)], [R("LC%d" % t)], sem=("cnt%d" % t, ne), lat=2800.0, sent=ne)
+        add({"G": (put, 300.0)}, [R(box, 0, 112)], [R(lb)], sem=("arr%d" % t, ne), lat=2800.0, sent=ne)
+        scan(R("SN"), R("RSn"), R("pK1", 0, 256), A.add, A.min)
+        ts(R("kn1"), R("SN", 15, 256, 16), 15.0, None, A.add)
+        ts(R("kn2"), R("kn1"), 15, None, A.bitwise_and)
+        cp(R("kn"), R("kn2"))
+        tt(R("TT"), R("OH"), R("DF"), A.mult, off=R("kn"))
+        for j in range(15, -1, -1):
+            tt(R("NM"), R("NO", 16 * j, 16 * j + 16), R("TT", 16 * j, 16 * j + 16), A.subtract, scat=R("OFl", 2 * j, 2 * j + 1))
+        ga1 = R("GA", 512 * t + 256, 512 * t + 512)
+        mark("1", 16, B, ga1, not_live(t))
+        for h, ga in ((0, ga0), (1, ga1)):
+            j = 2 * t + h
+            mm(gy, py, R("WyA", 5 - j, 53 - j), ga)
+            mm(gy, py, R("WyL", 5 - j, 53 - j), R("LV%d" % t))
+        umm(R("pU", 0, 6), "Wn", lambda j: R(lb, 16 + j, 112, 16))
+        place("r", 6, ab)
+        columns("r", 6, t, R("NM", 16, 1040))
+        spread("yrr", (lb, 16), [(96, K["spr"])], scale=-1.0)
+        scores("r", 6, B, "yrr", "pK1")
+        best("r", 6, "pK1", col(9))
+        ts(R("NF", 0, 6), R("SI", 0, 6), R(lb, 15, 16), -8192.0, A.is_ge, A.mult)
+        mark("r", 6, B, R("GAr"), lambda gr, o: mm(gr, o, R("Ib"), R("NF", 0, 6)))
+    ya = R("YA", parts=slice(0, 48))
+    ts(ya, py, -1.0, None, A.max)
+    dma("Y", [(T.ya[:], ya[0])], [ya], [], 2000)
+    dma("Y", [(T.yo[:], T.NM[:, 16:1040])], [R("NM")], [], 4000)
+    dma("G", [(T.ym[:], T.M[0:128:16, 16:16 + W])], [R("M")], [], 2300)
+    return ops
+
+
+def depend(ops):
+    hist = {}
+    for i, o in enumerate(ops):
+        d = set()
+        for r, wr in [(r, False) for r in o["r"]] + [(r, True) for r in o["w"]]:
+            ps = r[1] in _PS
+            h = hist.setdefault(r[1], [])
+            for j, r2, wr2 in h:
+                if j == i:
+                    continue
+                if ps:
+                    if o["grp"] is not None and o["grp"] == ops[j]["grp"]:
+                        if ops[j]["first"]:
+                            d.add(j)
+                    elif wr or wr2 or set(o["alts"]) != set(ops[j]["alts"]):
+                        d.add(j)
+                elif (wr or wr2) and _clash(r, r2):
+                    d.add(j)
+            if wr and r[4] == 1 and not ps:
+                h[:] = [e for e in h if not (r[2] <= e[1][2] and e[1][3] <= r[3])]
+            if ps and o["grp"] is not None and o["first"]:
+                h[:] = []
+            h.append((i, r, wr))
+        o["dep"] = sorted(d)
+
+
+def label(o):
+    return (o["w"][0][1] + "<" + (o["r"][-1 if o["grp"] else 0][1] if o["r"] else "")) if o["w"] else "out"
+
+
+def schedule(ops):
+    n = len(ops)
+    succ = [[] for _ in range(n)]
+    for i, o in enumerate(ops):
+        for j in o["dep"]:
+            succ[j].append(i)
+    lat = K["lat"]
+    pr = [0.0] * n
+    for i in range(n - 1, -1, -1):
+        c = min(a[1] for a in ops[i]["alts"].values()) + ops[i]["lat"] + ops[i].get("rest", 0.0)
+        pr[i] = c + max([pr[j] + (0 if ops[i]["grp"] and ops[j]["grp"] else lat) for j in succ[i]], default=0.0)
+    for i, o in enumerate(ops):
+        pr[i] += o.get("boost", 0.0) + BOOST.get(label(o), 0.0)
+    prv = [pr[i] + (BOOST.get("V" + label(o), -K["vpen"]) if len(o["alts"]) > 1 else 0.0) for i, o in enumerate(ops)]
+    left = [len(o["dep"]) for o in ops]
+    ready = [0.0] * n
+    now = {e: 0.0 for e in "VSPGY"}
+    pool = {e: set(i for i in range(n) if not left[i] and e in ops[i]["alts"]) for e in now}
+    order = {e: [] for e in now}
+    done = 0
+    while done < n:
+        pick = None
+        for e in now:
+            if pool[e]:
+                s = max(now[e], min(ready[i] for i in pool[e]))
+                if pick is None or s < pick[0]:
+                    pick = (s, e)
+        s, e = pick
+        c = pool[e]
+        pe = prv if e == "V" else pr
+        best = max((i for i in c if ready[i] <= s), key=lambda i: (pe[i], -i))
+        dur = ops[best]["alts"][e][1]
+        soon = [i for i in c if s < ready[i] < s + min(dur, K["look"]) and pe[i] > pe[best] + K["look2"] * dur]
+        if soon:
+            best = max(soon, key=lambda i: (pe[i], -i))
+            s = ready[best]
+            dur = ops[best]["alts"][e][1]
+        for e2 in ops[best]["alts"]:
+            pool[e2].discard(best)
+        order[e].append(best)
+        now[e] = s + dur
+        end = s + dur + ops[best]["lat"]
+        for j in succ[best]:
+            ready[j] = max(ready[j], end + (0 if ops[best]["grp"] and ops[j]["grp"] else lat))
+            left[j] -= 1
+            if not left[j]:
+                for e2 in ops[j]["alts"]:
+                    pool[e2].add(j)
+        done += 1
+    return order
+
+
+def times(ops, order, c):
+    cost, lt, lat = c
+    st, end = {}, {}
+    head = {e: 0 for e in order}
+    now = {e: 0.0 for e in order}
+    moved = True
+    while moved:
+        moved = False
+        for e, l in order.items():
+            while head[e] < len(l) and all(j in end for j in ops[l[head[e]]]["dep"]):
+                i = l[head[e]]
+                s = max([now[e]] + [end[j] + lt[j] + (0 if ops[i]["grp"] and ops[j]["grp"] else lat) for j in ops[i]["dep"]])
+                st[i] = s
+                end[i] = now[e] = s + cost[i][e]
+                head[e] += 1
+                moved = True
+    return st, end
+
+
+def fill(ops, seq, pre, c, rev):
+    cost, lt, lat = c
+    busy = {e: ([], []) for e in "VSPGY"}
+    st, en, eg = {}, {}, {}
+    for i in seq:
+        o = ops[i]
+        est = lt[i] if rev else 0.0
+        for j in pre[i]:
+            x = en[j] + (0 if o["grp"] and ops[j]["grp"] else lat) + (lt[i] if rev else lt[j])
+            if x > est:
+                est = x
+        best = None
+        for e, d in cost[i].items():
+            S, E = busy[e]
+            a, k = 0, len(E)
+            while a < k:
+                m = (a + k) // 2
+                if E[m] <= est:
+                    a = m + 1
+                else:
+                    k = m
+            s = est
+            while k < len(S) and S[k] < s + d - 1e-6:
+                s = max(s, E[k])
+                k += 1
+            if best is None or s + d < best[0]:
+                best = (s + d, s, e, k)
+        f, s, e, k = best
+        busy[e][0].insert(k, s)
+        busy[e][1].insert(k, f)
+        st[i], en[i], eg[i] = s, f, e
+    return st, en, eg
+
+
+def polish(ops, order, cs, rounds, seed, noise):
+    n = len(ops)
+    pre = [o["dep"] for o in ops]
+    suc = [[] for _ in ops]
+    for i, o in enumerate(ops):
+        for j in o["dep"]:
+            suc[j].append(i)
+
+    def worth(od):
+        return sum(max(e + c[1][i] for i, e in times(ops, od, c)[1].items()) / w for c, w in zip(cs, K["wt"]))
+    best = (worth(order), order, times(ops, order, cs[0])[1])
+    x = seed
+    for it in range(rounds):
+        key = {}
+        for i in range(n - 1, -1, -1):
+            x = (x * 1103515245 + 12345) % 2147483648
+            v = best[2][i] + (noise * (x / 2147483648.0) if it and x % 16 == 0 else 0.0)
+            key[i] = min([v] + [key[j] - 1e-3 for j in suc[i]])
+        e2 = fill(ops, sorted(range(n), key=lambda i: (-key[i], -i)), suc, cs[0], True)[1]
+        st, en, eg = fill(ops, sorted(range(n), key=lambda i: (-e2[i] - ops[i].get("boost", 0.0), i)), pre, cs[0], False)
+        od = {e: sorted((i for i in range(n) if eg[i] == e), key=lambda i: (st[i], i)) for e in "VSPGY"}
+        w = worth(od)
+        if w < best[0]:
+            best = (w, od, en)
+    return best[1]
+
+
+def emit(g, T, ops, order):
+    queue = {"V": g.vector, "S": g.scalar, "P": g.tensor, "G": g, "Y": g.sync}
+    eng, pos, last = {}, {}, {}
+    for e in order:
+        for p, i in enumerate(order[e]):
+            eng[i], pos[i] = e, p
+            if ops[i]["grp"]:
+                last[ops[i]["grp"]] = i
+    seen = {e: {} for e in order}
+    know, waits, need = {}, {}, set()
+    head = {e: 0 for e in order}
+    moved = True
+    while moved:
+        moved = False
+        for e in order:
+            while head[e] < len(order[e]) and all(j in know for j in ops[order[e][head[e]]]["dep"]):
+                i = order[e][head[e]]
+                s = seen[e]
+                ws = []
+                for j in sorted(ops[i]["dep"], key=lambda j: -pos[j]):
+                    if e == "P" and eng[j] == "P":
+                        continue
+                    key = ops[j]["sem"][0] if ops[j]["sem"] else eng[j]
+                    if s.get(key, -1) >= pos[j]:
+                        continue
+                    ws.append(j)
+                    need.add(j)
+                    s[key] = pos[j]
+                    for k2, v in know[j].items():
+                        if s.get(k2, -1) < v and "sent" not in ops[j]:
+                            s[k2] = v
+                waits[i] = ws
+                know[i] = dict(s)
+                head[e] += 1
+                moved = True
+    count, total = {}, {}
+    for e in order:
+        c = 0
+        for i in order[e]:
+            if not ops[i]["sem"] and i in need:
+                c += 1
+                count[i] = c
+        total[e] = c
+    sent = 0
+    for e in order:
+        q = queue[e]
+        for i in order[e]:
+            o = ops[i]
+            for j in waits[i]:
+                if ops[j]["sem"]:
+                    q.wait_ge(T.sem[ops[j]["sem"][0]], ops[j]["sem"][1])
+                else:
+                    q.wait_ge(T.sem[eng[j]], count[j])
+            f = o["alts"][e][0]
+            ins = f(q, last[o["grp"]] == i) if o["grp"] else f(q)
+            if i in count:
+                ins.then_inc(T.sem[e], 1)
+            sent += o.get("sent", 0)
+    for e in "VSPG":
+        if total[e]:
+            g.sync.wait_ge(T.sem[e], total[e])
+    for o in ops:
+        if o["sem"]:
+            g.sync.wait_ge(T.sem[o["sem"][0]], o["sem"][1])
+    g.sync.wait_ge(T.sem.sent, sent)
+
+
+def rank_program(g, core, T, topo):
+    rank = T.rank_of(core)
+    if rank is None:
+        return
+    if "o" not in _CACHE:
+        cs = []
+        for m in MODS[::-1]:
+            K.update(m)
+            ops = build(g, core, T, topo, rank)
+            cs.insert(0, ([{e: a[1] for e, a in o["alts"].items()} for o in ops], [m["rem"] if "sent" in o else o["lat"] for o in ops], m["lat"]))
+        depend(ops)
+        _CACHE["o"] = (polish(ops, schedule(ops), cs, K["rounds"], K["seed"], K["noise"]), [o["dep"] for o in ops])
+    ops = build(g, core, T, topo, rank)
+    order, deps = _CACHE["o"]
+    for o, d in zip(ops, deps):
+        o["dep"] = d
+    emit(g, T, ops, order)

@@ -10,8 +10,9 @@ _S = {
     "RC": (256, F32), "OH": (16, F32), "OHn": (16, F32), "EQ": (64, F32), "Z1": (128, F32), "Z2": (128, F32), "Z": (128, F32),
     "Wp": (144, BF), "Wn": (144, BF), "Wk": (144, BF), "Wm": (144, BF), "Wa": (144, BF), "Wl": (144, BF),
     "LX": (128, H16), "cX": (16, U16), "OHh": (16, H16), "Ws": (144, BF), "WyA": (64, BF), "WyL": (64, BF), "Ib": (128, BF), "Ih": (128, H16),
-    "BLK": (128, BF), "BLKh": (128, H16), "TRb": (128, BF), "DLO": (128, BF), "O16": (128, BF), "DW": (2048, H16),
-    "TRa": (256, BF), "TRl": (256, BF), "RSx": (256, BF), "RSn": (256, BF), "RSd": (256, BF), "KC": (256, BF),
+    "BLK": (128, BF), "BLKh": (128, H16), "TRb": (128, BF), "DLO": (128, BF), "O16": (128, BF), "DW": (2048, BF),
+    "SE": (2048, BF), "I16": (128, BF), "I8": (128, H16), "R2": (64, F32), "q1": (16, I32), "q2": (16, I32), "q3": (16, F32), "q4": (16, F32),
+    "TRr": (192, BF), "TRa": (512, BF), "TRl": (512, BF), "RSx": (256, BF), "RSn": (256, BF), "RSd": (512, BF), "KC": (256, BF),
     "CLn": (32, BF), "CLp": (32, BF), "SI": (16, F32), "cT": (16, U16), "TH": (16, H16), "Ab": (8, F32),
     "L0": (32, I32), "GA": (1536, BF), "GAr": (96, BF), "YA": (256, F32),
     "ny0": (256, BF), "ny1": (256, BF), "NO": (256, F32), "DF": (256, F32), "TT": (256, F32),
@@ -24,7 +25,7 @@ for _k in ("0", "1", "r"):
                "p1" + _k: (16, I32), "p2" + _k: (16, I32), "po" + _k: (16, U16),
                "u1" + _k: (32, I32), "u2" + _k: (32, I32), "u3" + _k: (32, F32), "u4" + _k: (32, F32), "lo" + _k: (32, U16)})
 for _k in ("a", "l"):
-    _S.update({"v" + _k: (16, H16), "AB" + _k: (256, F32), "SD" + _k: (256, F32), "OF" + _k: (32, U16)})
+    _S.update({"v" + _k: (16, H16), "AB" + _k: (512, F32), "SD" + _k: (512, F32), "OF" + _k: (32, U16)})
 for _t in range(NS):
     _S.update({"yr%d" % _t: (4096, BF), "yT%d" % _t: (256, BF), "box%d" % _t: (784, BF), "LB%d" % _t: (112, BF), "LV%d" % _t: (256, BF)})
 _S.update({"yr1h": (4096, BF), "yT1h": (256, BF), "yrr": (1536, BF)})
@@ -39,18 +40,22 @@ for _k, (_n, _d) in _S.items():
         _o = SCRATCH.get("pool_" + _d, (0, [0, 0]))[1][1]
         SCRATCH["pool_" + _d] = ("sbuf", [128, _o + (_n + 31) // 32 * 32], _d)
         _AT[_k] = ("pool_" + _d, _o)
+for _k in ("M", "NM"):
+    SCRATCH[_k] = ("sbuf", [128, _S[_k][0] + 16], F32)
+    _AT[_k] = (_k, 16)
 _PS = ("pK0", "pK1", "pU", "pA", "pD", "pX", "pS", "pY")
 SCRATCH.update({k: ("psum", [128, 512], F32) for k in _PS})
 SEMAPHORES = ["V", "S", "P", "G", "sent", "arr0", "arr1", "arr2", "cnt0", "cnt1"] + ["d%d" % i for i in range(12)]
 
 K = {"cyc": 1.0, "g": 1.3, "sc": 3.2, "pe": 0.5, "lat": 100.0, "fix": 30.0, "look": 250.0, "look2": 1.0, "vpen": 20000.0,
-     "ch0": [2] * 7 + [1, 1], "ch1": [2] * 7 + [1, 1], "chr": [4, 4, 4, 2, 2], "spr": "VS", "early": 0,
+     "ch0": [2] * 7 + [1, 1], "ch1": [4, 4, 2, 2, 2, 1, 1], "chr": [8, 4, 4], "spr": "VS", "early": 0,
      "sp0": [(128, "VS"), (128, "VSG")], "sp1": [(128, "VS"), (128, "VSG")]}
 K.update({"wt": (120e3, 95e3, 160e3, 150e3), "rounds": 40, "seed": 1, "noise": 1000.0})
-MODS = [dict(cyc=1.0, g=1.3, sc=3.2, pe=.5, lat=100., rem=2800.), dict(cyc=.83, g=.92, sc=1.7, pe=.42, lat=60., rem=2000.),
-        dict(cyc=1.2, g=1.66, sc=4.6, pe=.6, lat=180., rem=4000.), dict(cyc=1.0, g=1.3, sc=3.2, pe=.9, lat=150., rem=2800.)]
+MODS = [dict(cyc=.9, g=1.3, sc=3.2, pe=.45, lat=200., rem=3200.), dict(cyc=.83, g=1.0, sc=2.0, pe=.42, lat=170., rem=2800.),
+        dict(cyc=1.2, g=1.66, sc=4.6, pe=.6, lat=260., rem=4000.), dict(cyc=.9, g=1.3, sc=3.2, pe=.7, lat=170., rem=3200.)]
 SILU1 = 1.2784645427610738
 BOOST = {'pK1<mn1': -1000, 'C<OH': -2000, 'OHh<OH': 5000, 'SN<RSn': 5000, 'M<M': -2000, 'NF<SI': -500, 'u41<u31': -2000, 'GF<GA': 500, 'Wl<IC': -1500, 'box2<ny1': -2000, 'yrr<LB1': 200, 'VGr<M': -18500, 'yrr<LB0': 2000, 'yT1<x': 2000, 'Vyr0<yT0': -21000, 'ny0<mn0': -500, 'NM<NO': -5000, 'u10<pU': 5000, 'SX1<RSx': 2000, 'Gr<M': 700, 'TT<OH': -4000, 'LX<u21': -5000, 'OFl<SDl': -1000, 'lo1<pX': 5500, 'u2r<u1r': 500, 'pS<RD': 1000, 'vl<pX': -2000, 'yrr<LB2': 1000, 'pS<PRE': -5000, 'pS<CLp': -5000, 'kn<kn2': -2000, 'SDl<RSd': -5000, 'PRE<ON': -500, 'yT1h<ny0': 5000, 'GA<G0': 500, 'pK1<G1': -2000, 'pK1<KC': 5000}
+BOOST.update({'yrr<LB0': -5000, 'Vyr0<yT0': -19000, 'NM<NO': -10000, 'TT<OH': 1000, 'LX<u21': -10000, 'SDl<RSd': -7000, 'yT1h<ny0': 3000, 'GA<G0': -500, 'pK1<G1': 0, 'pK1<KC': 3500, 'pX<vl': -2000, 'pD<va': 2000, 'pX<LV0': -5000, 'ny1<mn1': -5000, 'NO<NM': -2000, 'p20<p10': 2000, 'q3<q2': 2000, 'pS<NRC': 5000, 'u11<pU': 2000, 'YA<pY': -1500, 'por<p2r': 1000, 'u40<u30': 1000, 'G0<M': -1000, 'yr1h<yT1h': 2000, 'L0<u41': -2000, 'box0<ny1': -2000, 'yr1<yT1': -1000, 'pD<TRr': 2500, 'u11<u41': 2000, 'a1<pS': 2000, 'lo1<u21': 3000, 'GF<GAr': -500, 'p10<SX0': 5000, 'box2<pS': -2000, 'yT0<x': 1500, 'u3r<pU': 1000, 'q4<pS': -2000, 'NRC<RD': -500, 'pY<GA': 1000, 'GAr<Gr': 500, 'u1r<pU': -5000, 'pK1<mnr': -1000, 'u4r<u3r': 500, 'kn1<SN': 1000, 'VM<M': -21000, 'mn0<x': -5000, 'pU<LB0': -1000, 'pK0<G0': 5000, 'box1<pS': -500})
 _CACHE = {}
 
 
@@ -202,8 +207,9 @@ def build(g, core, T, topo, rank):
     ts(R("PI", 2, 3), R("PI", 0, 1), 112, None, A.bitwise_and)
     cp(R("C", 0, 3), R("PI", 0, 3))
     ts(col(3), R("PI", 2, 3), 15.0, None, A.add)
-    cp(col(4), R("WI", 0, 1))
-    ts(col(5), R("WI", 0, 1), -1.0, None, A.mult)
+    ts(col(4), R("WI", 0, 1), 1.0 / 4096, None, A.mult)
+    ts(col(5), R("WI", 0, 1), -1.0 / 4096, None, A.mult)
+    ms(col(16), 592.0)
 
     def slide(name, c, n=144, at=3):
         ts(R(name, 0, n), R("IC", 0, n), col(at), c, A.is_equal, A.mult)
@@ -219,21 +225,21 @@ def build(g, core, T, topo, rank):
     for w in (64, 256, 1024):
         for j in (1, 2, 3):
             flex(R("M", 16 + j * w, 16 + (j + 1) * w), R("M", 16, 16 + w), "VS", bias=R("EQ", j * w // 64, j * w // 64 + 1))
-    dma("G", [(T.M[0:128:16, 16:16 + W], T.mk[:])], [], [R("M", 16, 16 + W)], 3000)
+    dma("G", [(T.M[r:128:16, 32:32 + W], T.mk[:]) for r in (0, 4)], [], [R("M", 16, 16 + W)], 3000)
     ms(R("TI", 0, 1), 0)
     dma("Y", [(T.TI[0:128:16, 0:1], T.th[:])], [], [R("TI")], 1900)
     dma("Y", [(T.DI[r:128:16, :], T.dl[:]) for r in range(16)], [R("x")], [R("DI")], 3500)
-    slide("Wk", 4096.0)
-    ts(col(7), oh(0), 1048576.0, None, A.mult)
+    slide("Wk", 512.0)
+    ts(col(7), oh(0), 131072.0, oh(4), A.mult, A.add)
     slide("Wm", col(7))
     ts(R("Ib"), R("IC", 0, 128), col(0), None, A.is_equal)
-    iota(R("KC"), [[-16, 16], [0, 16]], 240, 0)
-    for nm, a, b in (("RSx", 1.0, -1e8), ("RSn", -1.0, 1e8), ("RSd", 0.0, 1e9)):
+    iota(R("KC"), [[-32, 16], [0, 16]], 480, 0)
+    for nm, a, b, w in (("RSx", 2.0, -1e8, 16), ("RSn", -2.0, 1e8, 16), ("RSd", 0.0, 1e9, 32)):
         ms(R(nm), a)
-        ms(R(nm, 0, 256, 16), b)
+        ms(R(nm, 0, 16 * w, w), b)
     ts(col(8), col(1), 256.0, 255.0, A.mult, A.add)
     ts(col(9), col(1), 96.0, 255.0, A.mult, A.add)
-    ts(col(24), oh(0), oh(3), None, A.add)
+    ts(col(24), oh(0), oh(3), oh(4), A.add, A.add)
     ts(col(10), col(24), -1.0, 1.0, A.mult, A.add)
     ts(col(25), col(24), SILU1, None, A.mult)
     ts(col(11), oh(2), 64.0, oh(1), A.mult, A.add)
@@ -253,16 +259,29 @@ def build(g, core, T, topo, rank):
     iota(R("RC"), [[0, 16], [1, 16]], 0, 0)
     ts(R("Ih"), R("IC", 0, 128), col(0), None, A.is_equal)
     ts(R("BLK"), R("GC"), col(2), None, A.is_equal)
+    ts(R("I16"), R("IC", 0, 128), col(0), 8192.0, A.is_equal, A.mult)
     ts(R("BLKh"), R("GC"), col(2), None, A.is_equal)
-    ts(R("Z1"), R("GC"), col(2), -8192.0, A.is_equal, A.mult)
-    ts(R("Z2"), R("IC", 0, 128), col(0), 16384.0, A.is_equal, A.mult)
-    tt(R("Z"), R("Z1"), R("Z2"), A.add)
     ts(R("OHn"), R("OH"), -8192.0, None, A.mult)
-    for s in range(15):
-        ts(R("DW", 128 * s, 128 * s + 128), R("Z"), R("OHn", s, s + 1), None, A.max)
-    for nm, v in (("TRa", 2064.0), ("TRl", 16.0)):
-        ts(R(nm), R("RC"), col(1), 67108864.0, A.is_ge, A.mult)
-        ms(R(nm, 15, 256, 16), v)
+    for s in range(16):
+        se, dw = R("SE", 128 * s, 128 * s + 128), R("DW", 128 * s, 128 * s + 128)
+        act(se, R("BLK"), scale=R("OHn", s, s + 1))
+        if s < 15:
+            add({"G": (lambda q, se=se, dw=dw: q.affine_select(dw[0], se[0], [[-1, 128]], A.not_equal, 8192.0, 0, 1), 170 + 256 * cyc),
+                 "V": (lambda q, se=se, dw=dw: q.tensor_tensor(dw[0], se[0], R("I16")[0], A.add), vcost(256, False))},
+                [se, R("I16")], [dw])
+    ts(R("I8"), R("Ih"), 8192.0, None, A.mult)
+    ts(col(15), col(1), 16.0, None, A.add)
+    iota(R("R2", 0, 32), [[0, 16], [0, 2]], 99, 0)
+    iota(R("R2", 32, 48), [[0, 16]], -1, 0)
+    for j in (16, 48):
+        iota(R("R2", j, j + 16), [[1, 16]], 0, 0)
+    for nm, v in (("TRa", 2080.0), ("TRl", 32.0)):
+        ts(R(nm, 0, 64), R("R2"), col(1), 67108864.0, A.is_ge, A.mult)
+        ms(R(nm, 31, 64, 32), v)
+        for w in (64, 128, 256):
+            cp(R(nm, w, 2 * w), R(nm, 0, w))
+    for j in range(6):
+        cp(R("TRr", 32 * j, 32 * j + 32), R("TRa", 0, 32))
     ts(R("Z1"), R("RC", 0, 128), col(1), None, A.is_ge)
     tt(R("TRb"), R("Z1"), R("BLK"), A.mult)
     ts(col(18), col(1), -1.0, None, A.mult)
@@ -284,10 +303,9 @@ def build(g, core, T, topo, rank):
     AB0 = 312 - 0.40625
 
     def place(k, n, ab, out=None):
-        cp(R("u1" + k, 0, n), R("pU", 0, n))
-        ts(R("u2" + k, 0, n), R("u1" + k, 0, n), 4095, None, A.bitwise_and)
-        ts(R("u3" + k, 0, n), R("u2" + k, 0, n), 592.0, None, A.add)
-        tt(R("u4" + k, 0, n), R("u3" + k, 0, n), R("u3" + k, 0, n), A.mult)
+        ts(R("u1" + k, 0, n), R("pU", 0, n), -0.5 + 2.0 ** -13, None, A.add)
+        tt(R("u3" + k, 0, n), R("pU", 0, n), R("u1" + k, 0, n), A.subtract)
+        act(R("u4" + k, 0, n), R("u3" + k, 0, n), F.Square, scale=4096.0, bias=col(16))
         if out:
             ts(out, R("u4" + k, 0, n), 1.0 / 32, ab, A.mult, A.add)
             return
@@ -334,18 +352,25 @@ def build(g, core, T, topo, rank):
         w = 16 * n
         scan(R("SX" + k, 0, w), R("RSx", 0, w), R(pk, 0, w), A.add, A.max)
         cp(R("p1" + k, 0, n), R("SX" + k, 15, w, 16))
-        ts(R("p2" + k, 0, n), R("p1" + k, 0, n), 4095, None, A.bitwise_and)
+        ts(R("p2" + k, 0, n), R("p1" + k, 0, n), 1, 255, A.arith_shift_right, A.bitwise_and)
         ts(R("po" + k, 0, n), R("p2" + k, 0, n), -1.0, pc, A.mult, A.add)
 
     def first_of(k, n, tri, pd):
-        w = 16 * n
+        w = 32 * n
         gr = group()
         mm(gr, R(pd, 0, w), R("Ib"), R(tri, 0, w))
         for s in range(16):
-            mm(gr, R(pd, s, w, 16), R("DW", 128 * s, 128 * s + 128) if s < 15 else R("Ih"), R("v" + k, 0, n))
+            mm(gr, R(pd, 16 + s, w, 32), R("DW", 128 * s, 128 * s + 128) if s < 15 else R("Ih"), R("v" + k, 0, n))
+            if tri != "TRr":
+                mm(gr, R(pd, 32 + s, w, 64), R("SE", 128 * s, 128 * s + 128), R("v" + k, 0, n, 2))
+                mm(gr, R(pd, 32 + s, w, 64), R("I8"), R("v" + k, 1, n, 2))
         act(R("AB" + k, 0, w), R(pd, 0, w), F.Abs)
         scan(R("SD" + k, 0, w), R("RSd", 0, w), R("AB" + k, 0, w), A.add, A.min)
-        ts(R("OF" + k, 0, 2 * n, 2), R("SD" + k, 15, w, 16), col(1), None, A.max)
+        if tri == "TRr":
+            ts(R("OF" + k, 0, 2 * n, 2), R("SD" + k, 31, w, 32), col(1), None, A.max)
+            return
+        ts(R("OF" + k, 0, n, 2), R("SD" + k, 31, w, 64), col(1), None, A.max)
+        ts(R("OF" + k, 1, n, 2), R("SD" + k, 63, w, 64), col(15), None, A.max)
 
     def mark(k, n, B, ga, dead):
         a0 = ga[2]
@@ -355,10 +380,15 @@ def build(g, core, T, topo, rank):
         dead(gr, R("pA", 0, n))
         for j in range(16):
             mm(gr, R("pA", 0, n), sl("Wa", j), R(ga[1], a0 + j, a0 + 16 * n, 16))
-        ts(R("va", 0, n), R("pA", 0, n), -2064.0, None, A.max)
+        ts(R("va", 0, n), R("pA", 0, n), -2080.0, None, A.max)
+        if k == "r":
+            first_of("a", n, "TRr", "pD")
+            for j in range(n):
+                act(R("M", -16, 16 + B), R("GF", 16 * j, 16 * j + 16), F.Silu, scat=R("OFa", 2 * j, 2 * j + 1))
+            return
         first_of("a", n, "TRa", "pD")
-        for j in range(n):
-            act(R("M", 0, 16 + B), R("GF", 16 * j, 16 * j + 16), F.Silu, scat=R("OFa", 2 * j, 2 * j + 1))
+        for j in range(0, n, 2):
+            act(R("M", -16, 16 + B), R("GF", 16 * j, 16 * j + 32), F.Silu, scat=R("OFa", j, j + 2))
 
     def not_live(t, wn="Wl"):
         def f(gr, o):
@@ -408,7 +438,7 @@ def build(g, core, T, topo, rank):
         gr = group()
         not_live(t)(gr, R("pX", 0, 16))
         mm(gr, R("pX", 0, 16), R("LX"), R("OHh"))
-        ts(R("vl"), R("pX", 0, 16), -16.0, None, A.max)
+        ts(R("vl"), R("pX", 0, 16), -32.0, None, A.max)
         ts(R("lo1", 16, 32), R("pX", 0, 16), 0.0, None, A.max)
         act(R("NO"), R("NM", 16, 1040), off=R("lo1", 16, 32))
         tt(R("DF"), R("NM", 16, 1040), R("DI", 256 * t, 256 * t + 256), A.subtract, off=R("lo1", 16, 32))
@@ -420,8 +450,12 @@ def build(g, core, T, topo, rank):
         mm(gr, R("pS", 0, 16), R("BLKh"), R("TH"))
         not_live(t)(gr, R("pS", 0, 16))
         for j in range(16):
-            mm(gr, R("pS", 0, 16), sl("Ws", j), R("ny1", j, 256, 16))
-        ts(R("RD"), R("pS", 0, 16), 0.0, None, A.is_ge)
+            mm(gr, R("pS", 0, 16), sl("Ws", j), R("ny0", j, 256, 16))
+        ts(R("q1"), R("p11"), 9, None, A.arith_shift_right)
+        ts(R("q2"), R("p11"), 1, None, A.bitwise_and)
+        ts(R("q3"), R("q2"), -256.0, None, A.mult)
+        tt(R("q4"), R("pS", 0, 16), R("q1"), A.subtract)
+        tt(R("RD"), R("q4"), R("q3"), A.is_ge)
         scan(R("PRE", 1, 17), R("ON"), R("RD"), A.mult, A.add)
         tt(R("NRC"), R("RD"), R("CLn", 0, 16), A.mult)
         gr = group()
@@ -445,12 +479,12 @@ def build(g, core, T, topo, rank):
             add({"G": (putc, 300.0)}, [R(box, 14, 16)], [R("LC%d" % t)], sem=("cnt%d" % t, ne), lat=2800.0, sent=ne)
         add({"G": (put, 300.0)}, [R(box, 0, 112)], [R(lb)], sem=("arr%d" % t, ne), lat=2800.0, sent=ne)
         scan(R("SN"), R("RSn"), R("pK1", 0, 256), A.add, A.min)
-        ts(R("kn1"), R("SN", 15, 256, 16), 15.0, None, A.add)
-        ts(R("kn2"), R("kn1"), 15, None, A.bitwise_and)
+        ts(R("kn1"), R("SN", 15, 256, 16), 30.0, None, A.add)
+        ts(R("kn2"), R("kn1"), 1, 15, A.arith_shift_right, A.bitwise_and)
         cp(R("kn"), R("kn2"))
         tt(R("TT"), R("OH"), R("DF"), A.mult, off=R("kn"))
-        for j in range(15, -1, -1):
-            tt(R("NM"), R("NO", 16 * j, 16 * j + 16), R("TT", 16 * j, 16 * j + 16), A.subtract, scat=R("OFl", 2 * j, 2 * j + 1))
+        for j in range(14, -1, -2):
+            tt(R("NM", -16, 1040), R("NO", 16 * j, 16 * j + 32), R("TT", 16 * j, 16 * j + 32), A.subtract, scat=R("OFl", j, j + 2))
         ga1 = R("GA", 512 * t + 256, 512 * t + 512)
         mark("1", 16, B, ga1, not_live(t))
         for h, ga in ((0, ga0), (1, ga1)):
@@ -468,8 +502,8 @@ def build(g, core, T, topo, rank):
     ya = R("YA", parts=slice(0, 48))
     ts(ya, py, -1.0, None, A.max)
     dma("Y", [(T.ya[:], ya[0])], [ya], [], 2000)
-    dma("Y", [(T.yo[:], T.NM[:, 16:1040])], [R("NM")], [], 4000)
-    dma("G", [(T.ym[:], T.M[0:128:16, 16:16 + W])], [R("M")], [], 2300)
+    dma("Y", [(T.yo[:], T.NM[:, 32:1056])], [R("NM")], [], 4000)
+    dma("G", [(T.ym[:], T.M[0:128:16, 32:32 + W])], [R("M")], [], 2300)
     return ops
 
 

@@ -3,59 +3,57 @@ A = AluOpType
 F = ActivationFunctionType
 W, L, NS, CP = 4096, 1024, 3, 96
 BF, F32, I32, U16, H16 = "bfloat16", "float32", "int32", "uint16", "float16"
+SP = 32
+KS = 2.0 ** -17
 
 _S = {
-    "x": (4096, BF), "M": (4112, F32), "GF": (256, F32), "NI": (1024, I32), "NM": (1040, F32), "DI": (768, I32),
-    "WI": (8, I32), "TI": (8, I32), "PI": (8, I32), "C": (32, F32), "IC": (144, F32), "GC": (128, F32),
-    "RC": (256, F32), "OH": (16, F32), "OHn": (16, F32), "EQ": (64, F32), "Z1": (128, F32), "Z2": (128, F32), "Z": (128, F32),
-    "Wp": (144, BF), "Wn": (144, BF), "Wk": (144, BF), "Wm": (144, BF), "Wa": (144, BF), "Wl": (144, BF),
-    "LX": (128, H16), "cX": (16, U16), "OHh": (16, H16), "Ws": (144, BF), "WyA": (64, BF), "WyL": (64, BF), "Ib": (128, BF), "Ih": (128, H16),
-    "BLK": (128, BF), "BLKh": (128, H16), "TRb": (128, BF), "DLO": (128, BF), "O16": (128, BF), "DW": (2048, BF),
-    "SE": (2048, BF), "I16": (128, BF), "I8": (128, H16), "R2": (64, F32), "q1": (16, I32), "q2": (16, I32), "q3": (16, F32), "q4": (16, F32),
-    "TRr": (192, BF), "TRa": (512, BF), "TRl": (512, BF), "RSx": (256, BF), "RSn": (256, BF), "RSd": (512, BF), "KC": (256, BF),
-    "CLn": (32, BF), "CLp": (32, BF), "SI": (16, F32), "cT": (16, U16), "TH": (16, H16), "Ab": (8, F32),
-    "L0": (32, I32), "GA": (1536, BF), "GAr": (96, BF), "YA": (256, F32),
+    "x": (W, BF), "M": (W + 2 * SP, F32), "MK": (W, BF), "CT": (512, BF), "M1": (L, F32), "GF": (256, F32), "NI": (L, I32),
+    "NM": (L + 2 * SP, F32), "DI": (768, I32), "DW": (768, F32),
+    "WI": (8, I32), "TI": (8, I32), "PI": (8, I32), "C": (64, F32), "IC": (144, F32), "GC": (128, F32),
+    "RC": (128, F32), "OH": (16, F32), "NOH": (16, F32), "EQ": (8, F32), "E8": (8, F32), "Z1": (128, F32), "Z2": (128, F32), "Z3": (128, F32),
+    "Wp": (144, BF), "Wn": (144, BF), "Wk": (144, BF), "Wm": (144, BF), "Wl": (144, BF), "Ws": (144, BF),
+    "WyA": (64, BF), "WyL": (64, BF), "Ib": (128, BF), "Is": (128, BF), "BLK": (128, BF), "TRb": (128, BF), "DLO": (128, BF), "O16": (128, BF),
+    "SEL": (128, BF), "SE2": (128, BF), "K5": (32, BF), "KC": (256, BF), "RSx": (256, BF), "RSn": (256, BF),
+    "Dp": (128, BF), "Dn": (128, BF), "Dv": (128, BF), "Lp": (128, BF), "Ln": (128, BF), "Lv": (128, BF),
+    "J": (288, BF), "RBa": (288, BF), "RBl": (288, BF), "RAa0": (256, BF), "RAa1": (256, BF), "RAl0": (256, BF), "RAl1": (256, BF),
+    "SLT": (96, BF), "Ob": (8, BF), "LVr": (96, BF), "LVv": (256, BF), "PT": (256, BF), "PV": (256, BF),
+    "q2": (16, I32), "q4": (16, F32), "CLn": (32, BF), "CLp": (32, BF), "cT": (16, U16), "cV": (16, U16), "cW": (16, U16),
+    "TH": (16, H16), "Ab": (8, F32), "L0": (32, I32), "GA": (1536, BF), "GAr": (96, BF), "YA": (256, F32),
     "ny0": (256, BF), "ny1": (256, BF), "NO": (256, F32), "DF": (256, F32), "TT": (256, F32),
     "SN": (256, F32), "kn1": (16, I32), "kn2": (16, I32), "kn": (16, U16),
-    "RD": (16, BF), "PRE": (32, BF), "NRC": (16, BF), "SL": (16, U16), "ON": (16, BF), "a1": (8, I32), "a2": (8, I32), "NF": (16, BF),
+    "RD": (16, BF), "PRE": (32, BF), "NRC": (16, BF), "SL": (16, U16), "ON": (16, BF), "a1": (8, I32), "a2": (8, I32),
 }
 for _k in ("0", "1", "r"):
     _n = 1536 if _k == "r" else 4096
     _S.update({"mn" + _k: (_n, BF), "G" + _k: (_n, BF), "co" + _k: (256, U16), "SX" + _k: (256, F32),
                "p1" + _k: (16, I32), "p2" + _k: (16, I32), "po" + _k: (16, U16),
                "u1" + _k: (32, I32), "u2" + _k: (32, I32), "u3" + _k: (32, F32), "u4" + _k: (32, F32), "lo" + _k: (32, U16)})
-for _k in ("a", "l"):
-    _S.update({"v" + _k: (16, H16), "AB" + _k: (512, F32), "SD" + _k: (512, F32), "OF" + _k: (32, U16)})
+for _k in ("a", "b", "l"):
+    _S.update({"DS0" + _k: (256, F32), "DS1" + _k: (256, F32), "SD0" + _k: (256, F32), "SD1" + _k: (256, F32), "OF" + _k: (16, U16)})
 for _t in range(NS):
     _S.update({"yr%d" % _t: (4096, BF), "yT%d" % _t: (256, BF), "box%d" % _t: (784, BF), "LB%d" % _t: (112, BF), "LV%d" % _t: (256, BF)})
-_S.update({"yr1h": (4096, BF), "yT1h": (256, BF), "yrr": (1536, BF)})
-_S.update({"LC0": (2, BF), "LC1": (2, BF)})
-_OWN = ("WI", "TI", "YA", "LB0", "LB1", "LB2", "LC0", "LC1")
+_S.update({"yr1h": (4096, BF), "yT1h": (256, BF), "yrr": (1536, BF), "GFb": (256, F32)})
+_OWN = ("WI", "TI", "YA", "LB0", "LB1", "LB2")
 _AT, SCRATCH = {}, {}
 for _k, (_n, _d) in _S.items():
-    if _n > 256 or _k in _OWN:
+    if _n > 288 or _k in _OWN:
         SCRATCH[_k] = ("sbuf", [128, _n], _d)
         _AT[_k] = (_k, 0)
     else:
         _o = SCRATCH.get("pool_" + _d, (0, [0, 0]))[1][1]
         SCRATCH["pool_" + _d] = ("sbuf", [128, _o + (_n + 31) // 32 * 32], _d)
         _AT[_k] = ("pool_" + _d, _o)
-for _k in ("M", "NM"):
-    SCRATCH[_k] = ("sbuf", [128, _S[_k][0] + 16], F32)
-    _AT[_k] = (_k, 16)
 _PS = ("pK0", "pK1", "pU", "pA", "pD", "pX", "pS", "pY")
 SCRATCH.update({k: ("psum", [128, 512], F32) for k in _PS})
-SEMAPHORES = ["V", "S", "P", "G", "sent", "arr0", "arr1", "arr2", "cnt0", "cnt1"] + ["d%d" % i for i in range(12)]
+SEMAPHORES = ["V", "S", "P", "G", "sent", "arr0", "arr1", "arr2"] + ["d%d" % i for i in range(12)]
 
 K = {"cyc": 1.0, "g": 1.3, "sc": 3.2, "pe": 0.5, "lat": 100.0, "fix": 30.0, "look": 250.0, "look2": 1.0, "vpen": 20000.0,
-     "ch0": [2] * 7 + [1, 1], "ch1": [4, 4, 2, 2, 2, 1, 1], "chr": [8, 4, 4], "spr": "VS", "early": 0,
-     "sp0": [(128, "VS"), (128, "VSG")], "sp1": [(128, "VS"), (128, "VSG")]}
-K.update({"wt": (120e3, 95e3, 160e3, 150e3), "rounds": 40, "seed": 1, "noise": 1000.0})
+     "ch0": [2] * 7 + [1, 1], "ch1": [4, 4, 2, 2, 2, 1, 1], "chr": [8, 4, 4], "spr": "VS",
+     "sp0": [(128, "VSG"), (128, "VSG")], "sp1": [(128, "VS"), (128, "VSG")]}
+K.update({"wt": (120e3, 95e3, 160e3, 150e3), "rounds": 200, "seed": 1, "noise": 1000.0})
 MODS = [dict(cyc=.9, g=1.3, sc=3.2, pe=.45, lat=200., rem=3200.), dict(cyc=.83, g=1.0, sc=2.0, pe=.42, lat=170., rem=2800.),
-        dict(cyc=1.2, g=1.66, sc=4.6, pe=.6, lat=260., rem=4000.), dict(cyc=.9, g=1.3, sc=3.2, pe=.7, lat=170., rem=3200.)]
+        dict(cyc=1.2, g=1.9, sc=4.6, pe=.6, lat=260., rem=4000.), dict(cyc=.9, g=1.3, sc=3.2, pe=.7, lat=170., rem=3200.)]
 SILU1 = 1.2784645427610738
-BOOST = {'pK1<mn1': -1000, 'C<OH': -2000, 'OHh<OH': 5000, 'SN<RSn': 5000, 'M<M': -2000, 'NF<SI': -500, 'u41<u31': -2000, 'GF<GA': 500, 'Wl<IC': -1500, 'box2<ny1': -2000, 'yrr<LB1': 200, 'VGr<M': -18500, 'yrr<LB0': 2000, 'yT1<x': 2000, 'Vyr0<yT0': -21000, 'ny0<mn0': -500, 'NM<NO': -5000, 'u10<pU': 5000, 'SX1<RSx': 2000, 'Gr<M': 700, 'TT<OH': -4000, 'LX<u21': -5000, 'OFl<SDl': -1000, 'lo1<pX': 5500, 'u2r<u1r': 500, 'pS<RD': 1000, 'vl<pX': -2000, 'yrr<LB2': 1000, 'pS<PRE': -5000, 'pS<CLp': -5000, 'kn<kn2': -2000, 'SDl<RSd': -5000, 'PRE<ON': -500, 'yT1h<ny0': 5000, 'GA<G0': 500, 'pK1<G1': -2000, 'pK1<KC': 5000}
-BOOST.update({'yrr<LB0': -5000, 'Vyr0<yT0': -19000, 'NM<NO': -10000, 'TT<OH': 1000, 'LX<u21': -10000, 'SDl<RSd': -7000, 'yT1h<ny0': 3000, 'GA<G0': -500, 'pK1<G1': 0, 'pK1<KC': 3500, 'pX<vl': -2000, 'pD<va': 2000, 'pX<LV0': -5000, 'ny1<mn1': -5000, 'NO<NM': -2000, 'p20<p10': 2000, 'q3<q2': 2000, 'pS<NRC': 5000, 'u11<pU': 2000, 'YA<pY': -1500, 'por<p2r': 1000, 'u40<u30': 1000, 'G0<M': -1000, 'yr1h<yT1h': 2000, 'L0<u41': -2000, 'box0<ny1': -2000, 'yr1<yT1': -1000, 'pD<TRr': 2500, 'u11<u41': 2000, 'a1<pS': 2000, 'lo1<u21': 3000, 'GF<GAr': -500, 'p10<SX0': 5000, 'box2<pS': -2000, 'yT0<x': 1500, 'u3r<pU': 1000, 'q4<pS': -2000, 'NRC<RD': -500, 'pY<GA': 1000, 'GAr<Gr': 500, 'u1r<pU': -5000, 'pK1<mnr': -1000, 'u4r<u3r': 500, 'kn1<SN': 1000, 'VM<M': -21000, 'mn0<x': -5000, 'pU<LB0': -1000, 'pK0<G0': 5000, 'box1<pS': -500})
 _CACHE = {}
 
 
@@ -70,6 +68,7 @@ def _clash(a, b):
 def build(g, core, T, topo, rank):
     ops = []
     cyc = K["cyc"]
+    top = slice(0, 8)
 
     def R(name, a=0, b=None, s=1, parts=None):
         real, o = _AT.get(name, (name, 0))
@@ -145,17 +144,22 @@ def build(g, core, T, topo, rank):
         if "V" in engs:
             def fv(q):
                 if bias is not None:
-                    return q.tensor_scalar(out[0], src(), bias[0], None, A.add)
+                    return q.tensor_scalar(out[0], src(), ap(scale), ap(bias), A.mult, A.add)
                 if scale != 1.0:
-                    return q.tensor_scalar(out[0], src(), scale, None, A.mult)
+                    return q.tensor_scalar(out[0], src(), ap(scale), None, A.mult)
                 return q.tensor_copy(out[0], src())
             alts["V"] = (fv, gcost(n, "V") if off else vcost(n, two(out, in_)))
         if "S" in engs:
-            alts["S"] = (lambda q: q.activation(out[0], src(), F.Identity, bias=0.0 if bias is None else bias[0], scale=scale),
+            alts["S"] = (lambda q: q.activation(out[0], src(), F.Identity, bias=0.0 if bias is None else ap(bias), scale=ap(scale)),
                          gcost(n, "S") if off else vcost(n, False))
         if "G" in engs:
             alts["G"] = (lambda q: q.affine_select(out[0], in_[0], [[0, n]], A.is_ge, 0.0, 0, 0), 170 + 2 * n * cyc)
-        add(alts, [in_, bias, off], [out])
+        add(alts, [in_, scale, bias, off], [out])
+
+    def square(out, in_):
+        n = cnt(out)
+        add({"V": (lambda q: q.tensor_tensor(out[0], in_[0], in_[0], A.mult), vcost(2 * n, False)),
+             "S": (lambda q: q.activation(out[0], in_[0], F.Square), vcost(n, False))}, [in_], [out])
 
     def iota(out, pat, base, cm):
         fl = _S[out[1]][1] != I32
@@ -176,140 +180,146 @@ def build(g, core, T, topo, rank):
 
     nd = [0]
 
-    def dma(e, pairs, reads, writes, ns):
+    def dma(e, pairs, reads, writes, ns, boost=0.0):
         s = "d%d" % nd[0]
         nd[0] += 1
 
         def f(q):
             for o, i in pairs:
                 q.dma_start(o, i).then_inc(T.sem[s], 16)
-        add({e: (f, 60.0 * len(pairs))}, reads, writes, sem=(s, 16 * len(pairs)), lat=ns)
+        add({e: (f, (300.0 if e == "G" else 60.0) * len(pairs))}, reads, writes, sem=(s, 16 * len(pairs)), lat=ns, boost=boost)
 
     def sl(name, j):
         return R(name, 15 - j, 143 - j)
 
-    def col(j):
-        return R("C", j, j + 1)
+    cols = {}
+
+    def col(name, parts=None):
+        j = cols.setdefault(name, len(cols))
+        return R("C", j, j + 1, parts=parts)
 
     def oh(j):
         return R("OH", j, j + 1)
 
     B0 = W - 256
-    dma("Y", [(T.WI[:, 0:1], T.wt[:])], [], [R("WI")], 1900)
-    dma("Y", [(T.x[:, B0:W], T.xc[:, B0:W])], [], [R("x", B0, W)], 2200)
-    dma("Y", [(T.NI[:], T.oc[:])], [], [R("NI")], 4200)
-    dma("Y", [(T.x[:, 0:B0], T.xc[:, 0:B0])], [], [R("x", 0, B0)], 6500)
-    for j in range(4):
-        ops[j]["boost"] = 1e6 * (4 - j)
+    dma("Y", [(T.WI[:, 0:1], T.wt[:])], [], [R("WI")], 1900, 6e6)
+    dma("Y", [(T.x[:, B0:W], T.xc[:, B0:W])], [], [R("x", B0, W)], 2200, 5e6)
+    dma("Y", [(T.MK[0:8, :], T.mk[:])], [], [R("MK")], 2400, 4e6)
+    dma("Y", [(T.NI[:], T.oc[:])], [], [R("NI")], 4200, 3e6)
+    dma("Y", [(T.x[:, 0:B0], T.xc[:, 0:B0])], [], [R("x", 0, B0)], 6500, 2e6)
     iota(R("PI", 0, 1), [[0, 1]], 0, 1)
     iota(R("IC"), [[1, 144]], 0, 0)
     ts(R("PI", 1, 2), R("PI", 0, 1), 15, None, A.bitwise_and)
     ts(R("PI", 2, 3), R("PI", 0, 1), 112, None, A.bitwise_and)
+    p, r, g16 = col("p"), col("r"), col("g16")
     cp(R("C", 0, 3), R("PI", 0, 3))
-    ts(col(3), R("PI", 2, 3), 15.0, None, A.add)
-    ts(col(4), R("WI", 0, 1), 1.0 / 4096, None, A.mult)
-    ts(col(5), R("WI", 0, 1), -1.0 / 4096, None, A.mult)
-    ms(col(16), 592.0)
+    ts(col("last"), R("PI", 2, 3), 15.0, None, A.add)
+    ts(col("w"), R("WI", 0, 1), 1.0 / W, None, A.mult)
+    ts(col("-w"), R("WI", 0, 1), -1.0 / W, None, A.mult)
 
-    def slide(name, c, n=144, at=3):
+    def slide(name, c, n=144, at="last"):
         ts(R(name, 0, n), R("IC", 0, n), col(at), c, A.is_equal, A.mult)
-    slide("Wp", col(4))
-    slide("Wn", col(5))
-    ts(R("OH"), R("IC", 0, 16), col(1), None, A.is_equal)
-    ts(col(6), col(1), 16.0, None, A.mult)
-    ts(R("cT"), R("IC", 0, 16), col(6), None, A.add)
-    ts(R("EQ"), R("IC", 0, 64), oh(2), None, A.mult)
-    ts(col(22), oh(2), oh(1), 64.0, A.add, A.mult)
-    tt(col(23), col(22), oh(3), A.add)
-    ts(R("M", 16, 80), R("IC", 0, 64), oh(1), col(23), A.mult, A.add)
-    for w in (64, 256, 1024):
-        for j in (1, 2, 3):
-            flex(R("M", 16 + j * w, 16 + (j + 1) * w), R("M", 16, 16 + w), "VS", bias=R("EQ", j * w // 64, j * w // 64 + 1))
-    dma("G", [(T.M[r:128:16, 32:32 + W], T.mk[:]) for r in (0, 4)], [], [R("M", 16, 16 + W)], 3000)
-    ms(R("TI", 0, 1), 0)
-    dma("Y", [(T.TI[0:128:16, 0:1], T.th[:])], [], [R("TI")], 1900)
-    dma("Y", [(T.DI[r:128:16, :], T.dl[:]) for r in range(16)], [R("x")], [R("DI")], 3500)
-    slide("Wk", 512.0)
-    ts(col(7), oh(0), 131072.0, oh(4), A.mult, A.add)
-    slide("Wm", col(7))
-    ts(R("Ib"), R("IC", 0, 128), col(0), None, A.is_equal)
+
+    def mix(name, *terms):
+        (j, v), rest = terms[0], terms[1:]
+        flex(col(name), oh(j), "VS", scale=v)
+        for j, v in rest:
+            flex(col(name), oh(j), "VS", scale=v, bias=col(name))
+        return col(name)
+    slide("Wp", col("w"))
+    slide("Wn", col("-w"))
+    ts(R("OH"), R("IC", 0, 16), r, None, A.is_equal)
+    ts(R("Ib"), R("IC", 0, 128), p, None, A.is_equal)
+    ms(R("K5"), 592.0 / W)
+    flex(col("16r"), r, "VS", scale=16.0)
+    ts(R("cT"), R("IC", 0, 16), col("16r"), None, A.add)
+    flex(R("E8"), R("IC", 0, 8), "VS", scale=oh(2), bias=mix("dig", (1, 64.0), (2, 64.0), (3, 1.0)))
+    for j in range(8):
+        flex(R("CT", 64 * j, 64 * j + 64), R("IC", 0, 64), "VS", scale=oh(1), bias=R("E8", j, j + 1))
+    ts(R("EQ"), R("IC", 0, 8), oh(2), 8.0, A.mult, A.mult)
+    iota(R("Z2", parts=top), [[100, 8], [0, 2], [1, 8]], 0, -100)
+    ts(R("SEL", parts=top), R("Z2", parts=top), 0.0, None, A.is_equal)
+    for j, bank in enumerate(("pK1", "pA", "pD", "pX", "pS", "pY", "pK0", "pK1")):
+        gr = group()
+        mm(gr, R(bank, 0, 512), R("Ib"), R("CT"))
+        mm(gr, R(bank, 0, 512), R("SEL", parts=top), R("MK", 512 * j, 512 * j + 512, parts=top))
+        flex(R("M", SP + 512 * j, SP + 512 * j + 512), R(bank, 0, 512), "VS", bias=R("EQ", j, j + 1))
+    dma("G", [(T.TI[0:8, 0:1], T.th[:])], [], [R("TI")], 2500)
+    dma("Y", [(T.DI[j:128:16, :], T.dl[:]) for j in range(16)], [R("x")], [R("DI")], 3500)
+    slide("Wk", 512.0 * KS)
+    slide("Wm", mix("m", (0, 1.0), (8, KS)))
+    ts(R("Is"), R("IC", 0, 128), p, KS, A.is_equal, A.mult)
     iota(R("KC"), [[-32, 16], [0, 16]], 480, 0)
-    for nm, a, b, w in (("RSx", 2.0, -1e8, 16), ("RSn", -2.0, 1e8, 16), ("RSd", 0.0, 1e9, 32)):
+    for nm, a, b in (("RSx", 2.0 * KS, -1e4), ("RSn", -2.0 * KS, 1e4)):
         ms(R(nm), a)
-        ms(R(nm, 0, 16 * w, w), b)
-    ts(col(8), col(1), 256.0, 255.0, A.mult, A.add)
-    ts(col(9), col(1), 96.0, 255.0, A.mult, A.add)
-    ts(col(24), oh(0), oh(3), oh(4), A.add, A.add)
-    ts(col(10), col(24), -1.0, 1.0, A.mult, A.add)
-    ts(col(25), col(24), SILU1, None, A.mult)
-    ts(col(11), oh(2), 64.0, oh(1), A.mult, A.add)
-    ts(col(26), oh(3), -4160.0, col(11), A.mult, A.add)
-    ts(col(12), oh(3), -6208.0, col(11), A.mult, A.add)
-    slide("Wa", col(12))
-    ts(col(13), oh(3), -8192.0, None, A.mult)
-    ts(col(14), oh(0), 8192.0, col(13), A.mult, A.add)
-    slide("Wl", col(14))
-    ts(R("cX", 0, 8), R("IC", 0, 8), 0.0, col(1), A.mult, A.add)
-    cp(R("OHh"), R("OH"))
-    slide("Ws", -1.0)
-    ts(col(17), col(2), 0.375, 5.0, A.mult, A.add)
-    slide("WyA", col(26), 64, 17)
-    slide("WyL", col(14), 64, 17)
+        ms(R(nm, 0, 256, 16), b)
+    flex(col("pc"), r, "VS", scale=256.0, bias=255.0)
+    flex(col("pcr"), r, "VS", scale=96.0, bias=255.0)
+    mix("one", (0, 1.0), (3, 1.0), (8, 1.0))
+    flex(col("keep"), col("one"), "VS", scale=-1.0, bias=1.0)
+    flex(col("silu"), col("one"), "VS", scale=SILU1)
+    slide("Wl", mix("live", (0, 8192.0), (3, -8192.0)))
+    slide("Ws", -512.0 * KS)
+    flex(col("ya"), g16, "VS", scale=0.375, bias=5.0)
+    slide("WyA", mix("col", (1, 1.0), (2, 64.0), (3, -4160.0)), 64, "ya")
+    slide("WyL", col("live"), 64, "ya")
     iota(R("GC"), [[16, 8], [0, 16]], 0, 0)
-    iota(R("RC"), [[0, 16], [1, 16]], 0, 0)
-    ts(R("Ih"), R("IC", 0, 128), col(0), None, A.is_equal)
-    ts(R("BLK"), R("GC"), col(2), None, A.is_equal)
-    ts(R("I16"), R("IC", 0, 128), col(0), 8192.0, A.is_equal, A.mult)
-    ts(R("BLKh"), R("GC"), col(2), None, A.is_equal)
-    ts(R("OHn"), R("OH"), -8192.0, None, A.mult)
-    for s in range(16):
-        se, dw = R("SE", 128 * s, 128 * s + 128), R("DW", 128 * s, 128 * s + 128)
-        act(se, R("BLK"), scale=R("OHn", s, s + 1))
-        if s < 15:
-            add({"G": (lambda q, se=se, dw=dw: q.affine_select(dw[0], se[0], [[-1, 128]], A.not_equal, 8192.0, 0, 1), 170 + 256 * cyc),
-                 "V": (lambda q, se=se, dw=dw: q.tensor_tensor(dw[0], se[0], R("I16")[0], A.add), vcost(256, False))},
-                [se, R("I16")], [dw])
-    ts(R("I8"), R("Ih"), 8192.0, None, A.mult)
-    ts(col(15), col(1), 16.0, None, A.add)
-    iota(R("R2", 0, 32), [[0, 16], [0, 2]], 99, 0)
-    iota(R("R2", 32, 48), [[0, 16]], -1, 0)
-    for j in (16, 48):
-        iota(R("R2", j, j + 16), [[1, 16]], 0, 0)
-    for nm, v in (("TRa", 2080.0), ("TRl", 32.0)):
-        ts(R(nm, 0, 64), R("R2"), col(1), 67108864.0, A.is_ge, A.mult)
-        ms(R(nm, 31, 64, 32), v)
-        for w in (64, 128, 256):
-            cp(R(nm, w, 2 * w), R(nm, 0, w))
-    for j in range(6):
-        cp(R("TRr", 32 * j, 32 * j + 32), R("TRa", 0, 32))
-    ts(R("Z1"), R("RC", 0, 128), col(1), None, A.is_ge)
+    iota(R("RC"), [[0, 8], [1, 16]], 0, 0)
+    ts(R("BLK"), R("GC"), g16, None, A.is_equal)
+    for nm, c, s in (("Dp", mix("dp", (1, 2.0 ** 14), (2, 2.0 ** 20)), 1.0), ("Dn", mix("dn", (1, -2.0 ** 14), (2, -2.0 ** 20)), 1.0),
+                     ("Dv", mix("dv", (1, 1.0), (2, 64.0), (3, SP - 4160.0)), 1.0), ("Lp", mix("lp", (0, -2.0 ** 27)), 1.0),
+                     ("Ln", mix("ln", (0, 2.0 ** 27)), 1.0), ("Lv", mix("lv", (0, -8192.0), (3, 8192.0)), 1.0)):
+        flex(R(nm), R("BLK"), "VS", scale=c)
+    iota(R("J"), [[0, 9], [1, 32]], 0, 0)
+    flex(col("15-r"), r, "VS", scale=-1.0, bias=15.0)
+    for k, c in (("a", r), ("l", col("15-r"))):
+        ts(R("RB" + k), R("J"), c, 1e9, A.is_equal, A.mult)
+        for h in (0, 1):
+            o = 16 * (h if k == "a" else 1 - h)
+            ra = "RA%s%d" % (k, h)
+            ts(R(ra), R("J", o, o + 256), c, None, A.not_equal)
+            flex(R(ra, 31, 256, 32), R(ra, 31, 256, 32), "VS", scale=2.0 ** -14)
+    flex(col("r16"), r, "VS", bias=16.0)
+    for nm, v in (("a0", W + SP), ("a1", W + SP + 16), ("l0", L + SP), ("l1", L + SP + 16)):
+        flex(col(nm), r, "VS", bias=float(v))
+    ts(R("cV"), R("cT"), -1.0, 255.0, A.mult, A.add)
+    iota(R("Z3", 0, 16), [[-16, 16]], 255, 0)
+    ts(R("cW"), R("Z3", 0, 16), r, None, A.subtract)
+    iota(R("SLT"), [[1, 6], [6, 16]], 0, 0)
+    flex(R("Ob", 0, 1), oh(3), "VS")
+    flex(R("NOH"), R("OH"), "VS", scale=-1.0, bias=1.0)
+    ts(R("Z1"), R("RC"), r, None, A.is_ge)
     tt(R("TRb"), R("Z1"), R("BLK"), A.mult)
-    ts(col(18), col(1), -1.0, None, A.mult)
-    ts(R("DLO"), R("IC", 0, 128), col(0), col(18), A.is_equal, A.mult)
-    ts(col(19), col(1), -1.0, None, A.add)
+    flex(col("-r"), r, "VS", scale=-1.0)
+    flex(R("DLO"), R("Ib"), "VS", scale=col("-r"))
+    flex(col("r-1"), r, "VS", bias=-1.0)
     ms(R("O16"), 1.0 / 16)
     ms(R("ON"), 1.0)
     ms(R("PRE", 0, 1), 0.0)
     iota(R("CLn", 0, 16), [[-16, 16]], -256, 0)
-    iota(R("CLp", 0, 16), [[16, 16]], 256, 0)
+    iota(R("CLp", 0, 17), [[16, 17]], 256, 0)
     ms(R("CLp", 16, 17), 0.0)
-    ts(col(20), col(1), 6.0, None, A.mult)
-    ts(R("SI", 0, 6), R("IC", 0, 6), col(20), None, A.add)
-    ts(col(21), R("TI", 0, 1), -1.0, None, A.mult)
-    ts(R("TH"), R("ON"), col(21), None, A.mult)
+    iota(R("Z3", 0, 128, parts=top), [[1, 8], [0, 16]], 0, -1)
+    ts(R("SE2", parts=top), R("Z3", 0, 128, parts=top), 0.0, 512.0 * KS, A.is_equal, A.mult)
+    ts(col("th", top), R("TI", 0, 1, parts=top), -1.0, 1.0, A.mult, A.add)
+    ts(R("TH", parts=top), R("ON", parts=top), col("th", top), None, A.mult)
     for t in range(NS):
         ms(R("box%d" % t, 0, 112), 0.0)
-    cp(R("NM", 16, 1040), R("NI"))
+        cp(R("DW", 256 * t, 256 * t + 256), R("DI", 256 * t, 256 * t + 256))
+    for j in range(4):
+        cp(R("NM", SP + 256 * j, SP + 256 * j + 256), R("NI", 256 * j, 256 * j + 256))
+    flex(R("M1"), R("M", SP, SP + L), "G")
+    names = R("NM", SP, SP + L)
     AB0 = 312 - 0.40625
 
     def place(k, n, ab, out=None):
-        ts(R("u1" + k, 0, n), R("pU", 0, n), -0.5 + 2.0 ** -13, None, A.add)
+        ts(R("u1" + k, 0, n), R("pU", 0, n), -0.5 + 2.0 ** -13 - 592.0 / W, None, A.add)
         tt(R("u3" + k, 0, n), R("pU", 0, n), R("u1" + k, 0, n), A.subtract)
-        act(R("u4" + k, 0, n), R("u3" + k, 0, n), F.Square, scale=4096.0, bias=col(16))
+        square(R("u4" + k, 0, n), R("u3" + k, 0, n))
         if out:
-            ts(out, R("u4" + k, 0, n), 1.0 / 32, ab, A.mult, A.add)
+            ts(out, R("u4" + k, 0, n), 2.0 ** 19, ab, A.mult, A.add)
             return
-        ts(R("u1" + k, 0, n), R("u4" + k, 0, n), 1.0 / 32, ab, A.mult, A.add)
+        ts(R("u1" + k, 0, n), R("u4" + k, 0, n), 2.0 ** 19, ab, A.mult, A.add)
         place2(k, n)
 
     def place2(k, n):
@@ -318,11 +328,12 @@ def build(g, core, T, topo, rank):
 
     def umm(o, wn, rhs):
         gr = group()
+        mm(gr, o, R("Ib"), R("K5", 0, cnt(o)))
         for j in range(16):
             mm(gr, o, sl(wn, j), rhs(j))
 
-    def columns(k, n, t, names):
-        ts(R("co" + k, 0, 16 * n), names, (15 - t) / 16.0, -15.0 / 32, A.mult, A.add, off=R("lo" + k, 0, n))
+    def columns(k, n, t, nm):
+        ts(R("co" + k, 0, 16 * n), nm, (15 - t) / 16.0, -15.0 / 32, A.mult, A.add, off=R("lo" + k, 0, n))
 
     def spread(yr, src, parts, scale=1.0):
         b = 0
@@ -334,7 +345,7 @@ def build(g, core, T, topo, rank):
     def scores(k, n, B, yr, pk):
         gr = group()
         w = 16 * n
-        mm(gr, R(pk, 0, w), R("Ib"), R("KC", 0, w))
+        mm(gr, R(pk, 0, w), R("Is"), R("KC", 0, w))
         for nm, wn in (("mn", "Wk"), ("G", "Wm")):
             a = 0
             for ch in K["ch" + k]:
@@ -342,7 +353,7 @@ def build(g, core, T, topo, rank):
                 if nm == "mn":
                     tt(R(nm + k, w * a, w * (a + ch)), R("x", 0, B), R(yr, w * a, w * (a + ch)), A.min, off=o)
                 else:
-                    flex(R(nm + k, w * a, w * (a + ch)), R("M", 16, 16 + B), "VS", off=o)
+                    flex(R(nm + k, w * a, w * (a + ch)), R("M", SP, SP + B), "VS", off=o)
                 ops[-1]["rest"] = (16 - a - ch) * w * K["g"]
                 for j in range(a, a + ch):
                     mm(gr, R(pk, 0, w), sl(wn, j), R(nm + k, w * j, w * j + w))
@@ -351,50 +362,36 @@ def build(g, core, T, topo, rank):
     def best(k, n, pk, pc):
         w = 16 * n
         scan(R("SX" + k, 0, w), R("RSx", 0, w), R(pk, 0, w), A.add, A.max)
-        cp(R("p1" + k, 0, n), R("SX" + k, 15, w, 16))
+        ts(R("p1" + k, 0, n), R("SX" + k, 15, w, 16), 1 / KS, None, A.mult)
         ts(R("p2" + k, 0, n), R("p1" + k, 0, n), 1, 255, A.arith_shift_right, A.bitwise_and)
         ts(R("po" + k, 0, n), R("p2" + k, 0, n), -1.0, pc, A.mult, A.add)
 
-    def first_of(k, n, tri, pd):
-        w = 32 * n
+    def single(k, tab, w, dig, lv, pd):
+        (dn, d0), (ln, l0) = dig, lv
         gr = group()
-        mm(gr, R(pd, 0, w), R("Ib"), R(tri, 0, w))
-        for s in range(16):
-            mm(gr, R(pd, 16 + s, w, 32), R("DW", 128 * s, 128 * s + 128) if s < 15 else R("Ih"), R("v" + k, 0, n))
-            if tri != "TRr":
-                mm(gr, R(pd, 32 + s, w, 64), R("SE", 128 * s, 128 * s + 128), R("v" + k, 0, n, 2))
-                mm(gr, R(pd, 32 + s, w, 64), R("I8"), R("v" + k, 1, n, 2))
-        act(R("AB" + k, 0, w), R(pd, 0, w), F.Abs)
-        scan(R("SD" + k, 0, w), R("RSd", 0, w), R("AB" + k, 0, w), A.add, A.min)
-        if tri == "TRr":
-            ts(R("OF" + k, 0, 2 * n, 2), R("SD" + k, 31, w, 32), col(1), None, A.max)
-            return
-        ts(R("OF" + k, 0, n, 2), R("SD" + k, 31, w, 64), col(1), None, A.max)
-        ts(R("OF" + k, 1, n, 2), R("SD" + k, 63, w, 64), col(15), None, A.max)
+        mm(gr, R(pd, 0, w - 1), R("Lp"), R(ln, l0, l0 + w - 1))
+        mm(gr, R(pd, 0, w - 1), R("Ln"), R(ln, l0 + 1, l0 + w))
+        mm(gr, R(pd, 0, w - 1), R("Dp"), R(dn, d0, d0 + w - 1))
+        mm(gr, R(pd, 0, w - 1), R("Dn"), R(dn, d0 + 1, d0 + w))
+        gr = group()
+        mm(gr, R(pd, 31, w, 32), R("Lv"), R(ln, l0 + 31, l0 + w, 32))
+        mm(gr, R(pd, 31, w, 32), R("Dv"), R(dn, d0 + 31, d0 + w, 32))
+        for h in (0, 1):
+            ds, sd = R("DS%d%s" % (h, k), 0, w), "SD%d%s" % (h, k)
+            o = 16 * (h if tab == "a" else 1 - h)
+            scan(ds, R("RA%s%d" % (tab, h), 0, w), R(pd, 0, w), A.mult, A.add)
+            act(ds, ds, F.Abs)
+            scan(R(sd, 0, w), R("RB" + tab, o, o + w), ds, A.add, A.min)
+            ts(R("OF" + k, h, w // 16, 2), R(sd, 31, w, 32), col("r16") if h else r, col(tab + str(h)), A.max, A.min)
 
-    def mark(k, n, B, ga, dead):
-        a0 = ga[2]
+    def mark(k, n, ga, lv, s, pd):
+        w = 16 * n
+        gf = "GF" if s == "a" else "GFb"
         act(ga, R("G" + k, 0, 256 * n), off=R("po" + k, 0, n))
-        act(R("GF", 0, 16 * n), ga, scale=col(10), bias=col(25))
-        gr = group()
-        dead(gr, R("pA", 0, n))
-        for j in range(16):
-            mm(gr, R("pA", 0, n), sl("Wa", j), R(ga[1], a0 + j, a0 + 16 * n, 16))
-        ts(R("va", 0, n), R("pA", 0, n), -2080.0, None, A.max)
-        if k == "r":
-            first_of("a", n, "TRr", "pD")
-            for j in range(n):
-                act(R("M", -16, 16 + B), R("GF", 16 * j, 16 * j + 16), F.Silu, scat=R("OFa", 2 * j, 2 * j + 1))
-            return
-        first_of("a", n, "TRa", "pD")
+        flex(R(gf, 0, w), ga, "SV", scale=col("keep"), bias=col("silu"))
+        single(s, "a", w, (ga[1], ga[2]), (lv, 0), pd)
         for j in range(0, n, 2):
-            act(R("M", -16, 16 + B), R("GF", 16 * j, 16 * j + 32), F.Silu, scat=R("OFa", j, j + 2))
-
-    def not_live(t, wn="Wl"):
-        def f(gr, o):
-            for j in range(16):
-                mm(gr, o, sl(wn, j), R("LV%d" % t, j, 256, 16))
-        return f
+            act(R("M"), R(gf, 16 * j, 16 * j + 32), F.Silu, scat=R("OF" + s, j, j + 2))
 
     umm(R("pU", 0, 16), "Wp", lambda j: R("x", B0 + 16 * j, B0 + 16 * j + 16))
     place("0", 16, AB0)
@@ -414,48 +411,45 @@ def build(g, core, T, topo, rank):
     for t in range(NS):
         B = W - 256 * (t + 1)
         ab = AB0 if t == 0 else R("Ab", t, t + 1)
-        flex(R("LV%d" % t), R("M", 16 + B, 16 + B + 256), "VS")
+        lv = "LV%d" % t
+        flex(R(lv), R("M", SP + B, SP + B + 256), "VS")
         if t:
-            mm(group(), R("pS", 64, 65), R("O16"), R("LC%d" % (t - 1), 1, 2) if K["early"] else R("LB%d" % (t - 1), 15, 16))
+            mm(group(), R("pS", 64, 65), R("O16"), R("LB%d" % (t - 1), 15, 16))
             cp(R("a1", 0, 1), R("pS", 64, 65))
             ts(R("a2", 0, 1), R("a1", 0, 1), 63, None, A.bitwise_and)
             ts(ab, R("a2", 0, 1), AB0, None, A.add)
             ts(R("u10", 0, 16), R("L0", 16 * t - 16, 16 * t), ab, -AB0, A.add, A.add)
             place2("0", 16)
-        columns("0", 16, t, R("NM", 16, 1040) if t else R("NI"))
+        columns("0", 16, t, names if t else R("NI"))
         scores("0", 16, B, "yr%d" % t, "pK0")
-        best("0", 16, "pK0", col(8))
+        best("0", 16, "pK0", col("pc"))
         tt(R("ny0"), R("mn0"), R("x", B, B + 256), A.subtract, off=R("po0"))
         ga0 = R("GA", 512 * t, 512 * t + 256)
         umm(R("pU", 0, 16), "Wn", lambda j: R("ny0", 16 * j, 16 * j + 16))
         place("1", 16, ab)
-        columns("1", 16, t, R("NM", 16, 1040))
+        columns("1", 16, t, names if t else R("NI"))
         flex(R("yT1h"), R("ny0"), "S", scale=-1.0, off=R("cT"))
-        mark("0", 16, B, ga0, not_live(t))
+        mark("0", 16, ga0, lv, "a", "pD")
         spread("yr1h", ("yT1h", 0), K["sp1"])
         scores("1", 16, B, "yr1h", "pK1")
-        tt(R("LX"), R("u21", 0, 16), R("BLK"), A.mult, off=R("cX", 0, 8))
-        gr = group()
-        not_live(t)(gr, R("pX", 0, 16))
-        mm(gr, R("pX", 0, 16), R("LX"), R("OHh"))
-        ts(R("vl"), R("pX", 0, 16), -32.0, None, A.max)
-        ts(R("lo1", 16, 32), R("pX", 0, 16), 0.0, None, A.max)
-        act(R("NO"), R("NM", 16, 1040), off=R("lo1", 16, 32))
-        tt(R("DF"), R("NM", 16, 1040), R("DI", 256 * t, 256 * t + 256), A.subtract, off=R("lo1", 16, 32))
-        first_of("l", 16, "TRl", "pX")
-        best("1", 16, "pK1", col(8))
+        act(R("NO"), names, off=R("lo1", 0, 16))
+        act(R("PT"), R("M1"), off=R("lo1", 0, 16))
+        act(R("PV"), R("PT"), off=R("cV"))
+        act(R("LVv"), R(lv), off=R("cW"))
+        tt(R("DF"), R("NO"), R("DW", 256 * t, 256 * t + 256), A.subtract, off=R("cT"))
+        single("l", "l", 256, ("PV", 0), ("LVv", 0), "pX")
+        best("1", 16, "pK1", col("pc"))
         tt(R("ny1"), R("mn1"), R("ny0"), A.add, off=R("po1"))
         box, lb = "box%d" % t, "LB%d" % t
         gr = group()
-        mm(gr, R("pS", 0, 16), R("BLKh"), R("TH"))
-        not_live(t)(gr, R("pS", 0, 16))
+        mm(gr, R("pS", 0, 16), R("SE2", parts=top), R("TH", parts=top))
+        for j in range(16):
+            mm(gr, R("pS", 0, 16), sl("Wl", j), R(lv, j, 256, 16))
         for j in range(16):
             mm(gr, R("pS", 0, 16), sl("Ws", j), R("ny0", j, 256, 16))
-        ts(R("q1"), R("p11"), 9, None, A.arith_shift_right)
-        ts(R("q2"), R("p11"), 1, None, A.bitwise_and)
-        ts(R("q3"), R("q2"), -256.0, None, A.mult)
-        tt(R("q4"), R("pS", 0, 16), R("q1"), A.subtract)
-        tt(R("RD"), R("q4"), R("q3"), A.is_ge)
+        ts(R("q2"), R("p11", 0, 16), 1, None, A.bitwise_and)
+        tt(R("q4"), R("SX1", 15, 256, 16), R("pS", 0, 16), A.subtract)
+        tt(R("RD"), R("q2"), R("q4"), A.is_gt)
         scan(R("PRE", 1, 17), R("ON"), R("RD"), A.mult, A.add)
         tt(R("NRC"), R("RD"), R("CLn", 0, 16), A.mult)
         gr = group()
@@ -464,7 +458,7 @@ def build(g, core, T, topo, rank):
         mm(gr, R("pS", 32, 48), R("DLO"), R("RD"))
         mm(gr, R("pS", 32, 48), R("Ib"), R("NRC"))
         mm(gr, R("pS", 32, 49), R("BLK"), R("PRE", 0, 17))
-        ts(R("SL"), R("pS", 32, 48), col(19), None, A.add)
+        ts(R("SL"), R("pS", 32, 48), col("r-1"), None, A.add)
         ts(R(box, 15, 16), R("pS", 48, 49), float(CP), None, A.min)
         cp(R(box, 16, 784), R("ny1"), scat=R("SL"))
         dst = T.cores[(rank + 1 + t % (N - 1)) % N]
@@ -473,37 +467,34 @@ def build(g, core, T, topo, rank):
         def put(q, box=box, lb=lb, t=t, dst=dst, rid=rid, pid=pid):
             q.remote_dma(T[lb][:], T[box][:, 0:112], T.sem["arr%d" % t], T.sem.sent, pid, rid, topo.mask(core, dst))
         ne = len(topo.engines(core, dst))
-        if t < NS - 1 and K["early"]:
-            def putc(q, box=box, t=t, dst=dst, rid=rid, pid=pid):
-                q.remote_dma(T["LC%d" % t][:], T[box][:, 14:16], T.sem["cnt%d" % t], T.sem.sent, pid, rid, topo.mask(core, dst))
-            add({"G": (putc, 300.0)}, [R(box, 14, 16)], [R("LC%d" % t)], sem=("cnt%d" % t, ne), lat=2800.0, sent=ne)
         add({"G": (put, 300.0)}, [R(box, 0, 112)], [R(lb)], sem=("arr%d" % t, ne), lat=2800.0, sent=ne)
         scan(R("SN"), R("RSn"), R("pK1", 0, 256), A.add, A.min)
-        ts(R("kn1"), R("SN", 15, 256, 16), 30.0, None, A.add)
+        ts(R("kn1"), R("SN", 15, 256, 16), 1 / KS, 30.0, A.mult, A.add)
         ts(R("kn2"), R("kn1"), 1, 15, A.arith_shift_right, A.bitwise_and)
         cp(R("kn"), R("kn2"))
-        tt(R("TT"), R("OH"), R("DF"), A.mult, off=R("kn"))
-        for j in range(14, -1, -2):
-            tt(R("NM", -16, 1040), R("NO", 16 * j, 16 * j + 32), R("TT", 16 * j, 16 * j + 32), A.subtract, scat=R("OFl", j, j + 2))
+        tt(R("TT"), R("NOH"), R("DF"), A.mult, off=R("kn"))
+        for j in range(8):
+            a = 224 - 32 * j
+            tt(R("NM"), R("TT", a, a + 32), R("DW", 256 * t + a, 256 * t + a + 32), A.add, scat=R("OFl", 2 * j, 2 * j + 2))
         ga1 = R("GA", 512 * t + 256, 512 * t + 512)
-        mark("1", 16, B, ga1, not_live(t))
+        mark("1", 16, ga1, lv, "b", "pA")
         for h, ga in ((0, ga0), (1, ga1)):
             j = 2 * t + h
             mm(gy, py, R("WyA", 5 - j, 53 - j), ga)
-            mm(gy, py, R("WyL", 5 - j, 53 - j), R("LV%d" % t))
+            mm(gy, py, R("WyL", 5 - j, 53 - j), R(lv))
         umm(R("pU", 0, 6), "Wn", lambda j: R(lb, 16 + j, 112, 16))
         place("r", 6, ab)
-        columns("r", 6, t, R("NM", 16, 1040))
+        columns("r", 6, t, names)
         spread("yrr", (lb, 16), [(96, K["spr"])], scale=-1.0)
         scores("r", 6, B, "yrr", "pK1")
-        best("r", 6, "pK1", col(9))
-        ts(R("NF", 0, 6), R("SI", 0, 6), R(lb, 15, 16), -8192.0, A.is_ge, A.mult)
-        mark("r", 6, B, R("GAr"), lambda gr, o: mm(gr, o, R("Ib"), R("NF", 0, 6)))
+        best("r", 6, "pK1", col("pcr"))
+        ts(R("LVr"), R("SLT"), R(lb, 15, 16), R("Ob", 0, 1), A.is_lt, A.max)
+        mark("r", 6, R("GAr"), "LVr", "a", "pD")
     ya = R("YA", parts=slice(0, 48))
     ts(ya, py, -1.0, None, A.max)
     dma("Y", [(T.ya[:], ya[0])], [ya], [], 2000)
-    dma("Y", [(T.yo[:], T.NM[:, 32:1056])], [R("NM")], [], 4000)
-    dma("G", [(T.ym[:], T.M[0:128:16, 32:32 + W])], [R("M")], [], 2300)
+    dma("Y", [(T.yo[:], T.NM[:, SP:SP + L])], [R("NM")], [], 4000)
+    dma("G", [(T.ym[:], T.M[0:128:16, SP:SP + W])], [R("M")], [], 2300)
     return ops
 
 
@@ -521,7 +512,7 @@ def depend(ops):
                     if o["grp"] is not None and o["grp"] == ops[j]["grp"]:
                         if ops[j]["first"]:
                             d.add(j)
-                    elif wr or wr2 or set(o["alts"]) != set(ops[j]["alts"]):
+                    elif wr or wr2 or len(o["alts"]) > 1 or set(o["alts"]) != set(ops[j]["alts"]):
                         d.add(j)
                 elif (wr or wr2) and _clash(r, r2):
                     d.add(j)
@@ -549,8 +540,8 @@ def schedule(ops):
         c = min(a[1] for a in ops[i]["alts"].values()) + ops[i]["lat"] + ops[i].get("rest", 0.0)
         pr[i] = c + max([pr[j] + (0 if ops[i]["grp"] and ops[j]["grp"] else lat) for j in succ[i]], default=0.0)
     for i, o in enumerate(ops):
-        pr[i] += o.get("boost", 0.0) + BOOST.get(label(o), 0.0)
-    prv = [pr[i] + (BOOST.get("V" + label(o), -K["vpen"]) if len(o["alts"]) > 1 else 0.0) for i, o in enumerate(ops)]
+        pr[i] += o.get("boost", 0.0)
+    prv = [pr[i] - (K["vpen"] if len(o["alts"]) > 1 else 0.0) for i, o in enumerate(ops)]
     left = [len(o["dep"]) for o in ops]
     ready = [0.0] * n
     now = {e: 0.0 for e in "VSPGY"}
@@ -736,18 +727,23 @@ def emit(g, T, ops, order):
     g.sync.wait_ge(T.sem.sent, sent)
 
 
+def plan(g, core, T, topo, rank):
+    cs = []
+    for m in MODS[::-1]:
+        K.update(m)
+        ops = build(g, core, T, topo, rank)
+        cs.insert(0, ([{e: a[1] for e, a in o["alts"].items()} for o in ops], [m["rem"] if "sent" in o else o["lat"] for o in ops], m["lat"]))
+    depend(ops)
+    return ops, cs, polish(ops, schedule(ops), cs, K["rounds"], K["seed"], K["noise"])
+
+
 def rank_program(g, core, T, topo):
     rank = T.rank_of(core)
     if rank is None:
         return
     if "o" not in _CACHE:
-        cs = []
-        for m in MODS[::-1]:
-            K.update(m)
-            ops = build(g, core, T, topo, rank)
-            cs.insert(0, ([{e: a[1] for e, a in o["alts"].items()} for o in ops], [m["rem"] if "sent" in o else o["lat"] for o in ops], m["lat"]))
-        depend(ops)
-        _CACHE["o"] = (polish(ops, schedule(ops), cs, K["rounds"], K["seed"], K["noise"]), [o["dep"] for o in ops])
+        ops, cs, order = plan(g, core, T, topo, rank)
+        _CACHE["o"] = (order, [o["dep"] for o in ops])
     ops = build(g, core, T, topo, rank)
     order, deps = _CACHE["o"]
     for o, d in zip(ops, deps):

@@ -7,21 +7,25 @@ SP = 32
 KS = 2.0 ** -17
 
 _S = {
-    "x": (W, BF), "M": (W + 2 * SP, F32), "MK": (W, BF), "CT": (512, BF), "M1": (L, F32), "GF": (256, F32), "NI": (L, I32),
-    "NM": (L + 2 * SP, F32), "DI": (768, I32), "DW": (768, F32),
+    "x": (W, BF), "M": (W + 2 * SP, F32), "MK": (W, BF), "CT": (512, BF), "NI": (L, I32),
+    "NM": (L + 64 + 2 * SP, F32), "DI": (768, I32), "DW": (768, F32),
     "WI": (8, I32), "TI": (8, I32), "PI": (8, I32), "C": (64, F32), "IC": (144, F32), "GC": (128, F32),
     "RC": (128, F32), "OH": (16, F32), "NOH": (16, F32), "EQ": (8, F32), "E8": (8, F32), "Z1": (128, F32), "Z2": (128, F32), "Z3": (128, F32),
-    "Wp": (144, BF), "Wn": (144, BF), "Wk": (144, BF), "Wm": (144, BF), "Wl": (144, BF), "Ws": (144, BF),
+    "Wp": (144, BF), "Wn": (144, BF), "Wk0": (144, BF), "Wk1": (144, BF), "Wk2": (144, BF), "Wk3": (144, BF),
+    "RZ": (512, BF), "ZR": (1536, BF), "XR": (2560, BF), "MR": (2560, BF), "Y31": (2560, BF), "Y32": (2560, BF), "SC": (128, BF), "PC": (17, F32), "Z5": (4, F32), "HI": (4, F32), "pq": (8, U16), "sel": (128, BF),
+    "yU1": (128, BF), "yU2": (128, BF), "Wm": (144, BF), "Wl": (144, BF),
     "WyA": (64, BF), "WyL": (64, BF), "Ib": (128, BF), "Is": (128, BF), "BLK": (128, BF), "TRb": (128, BF), "DLO": (128, BF), "O16": (128, BF),
     "SEL": (128, BF), "SE2": (128, BF), "K5": (32, BF), "KC": (256, BF), "RSx": (256, BF), "RSn": (256, BF),
     "Dp": (128, BF), "Dn": (128, BF), "Dv": (128, BF), "Lp": (128, BF), "Ln": (128, BF), "Lv": (128, BF),
-    "J": (288, BF), "RBa": (288, BF), "RBl": (288, BF), "RAa0": (256, BF), "RAa1": (256, BF), "RAl0": (256, BF), "RAl1": (256, BF),
-    "SLT": (96, BF), "Ob": (8, BF), "LVr": (96, BF), "LVv": (256, BF), "PT": (256, BF), "PV": (256, BF),
-    "q2": (16, I32), "q4": (16, F32), "CLn": (32, BF), "CLp": (32, BF), "cT": (16, U16), "cV": (16, U16), "cW": (16, U16),
-    "TH": (16, H16), "Ab": (8, F32), "L0": (32, I32), "GA": (1536, BF), "GAr": (96, BF), "YA": (256, F32),
-    "ny0": (256, BF), "ny1": (256, BF), "NO": (256, F32), "DF": (256, F32), "TT": (256, F32),
+    "J": (288, BF), "RAa0": (256, BF), "RAa1": (256, BF), "RAl0": (256, BF), "RAl1": (256, BF),
+    "RBa": (288, BF), "RBl": (288, BF), "aq": (8, BF), "KX": (8, BF),
+    "SLT": (96, BF), "Ob": (8, BF), "PT": (256, BF),
+    "q2": (16, I32), "q4": (16, F32), "CLn": (32, BF), "CLp": (32, BF), "cT": (16, U16),
+    "GAr": (96, BF), "LVr": (96, BF), "LV0": (256, BF), "LV1": (256, BF), "LV2": (256, BF), "ZZ": (128, BF),
+    "TH": (16, H16), "Ab": (8, F32), "L0": (32, I32), "GA": (6 * 272, BF), "YA": (256, F32),
+    "ny0": (256, BF), "ny1": (256, BF), "NO": (256, F32), "DF": (256, I32), "TT": (256, F32), "NW": (256, F32), "YO": (L, F32),
     "SN": (256, F32), "kn1": (16, I32), "kn2": (16, I32), "kn": (16, U16),
-    "RD": (16, BF), "PRE": (32, BF), "NRC": (16, BF), "SL": (16, U16), "ON": (16, BF), "a1": (8, I32), "a2": (8, I32),
+    "RD": (16, BF), "PRE": (32, BF), "NRC": (16, BF), "SL": (16, U16), "ON": (32, BF), "MB": (W + 2 * SP, BF),
 }
 for _k in ("0", "1", "r"):
     _n = 1536 if _k == "r" else 4096
@@ -31,8 +35,9 @@ for _k in ("0", "1", "r"):
 for _k in ("a", "b", "l"):
     _S.update({"DS0" + _k: (256, F32), "DS1" + _k: (256, F32), "SD0" + _k: (256, F32), "SD1" + _k: (256, F32), "OF" + _k: (16, U16)})
 for _t in range(NS):
-    _S.update({"yr%d" % _t: (4096, BF), "yT%d" % _t: (256, BF), "box%d" % _t: (784, BF), "LB%d" % _t: (112, BF), "LV%d" % _t: (256, BF)})
-_S.update({"yr1h": (4096, BF), "yT1h": (256, BF), "yrr": (1536, BF), "GFb": (256, F32)})
+    _S.update({"yr%d" % _t: (4096, BF), "yT%d" % _t: (256, BF), "box%d" % _t: (784, BF), "LB%d" % _t: (112, BF)})
+_S.update({"yr1h": (4096, BF), "yP": (256, BF), "nyN": (256, BF), "yrr": (1536, BF), "GFb": (256, F32),
+           "GFa": (256, F32), "cN": (16, U16), "Z4": (16, F32), "yQ1": (128, BF), "yQ2": (128, BF)})
 _OWN = ("WI", "TI", "YA", "LB0", "LB1", "LB2")
 _AT, SCRATCH = {}, {}
 for _k, (_n, _d) in _S.items():
@@ -47,13 +52,20 @@ _PS = ("pK0", "pK1", "pU", "pA", "pD", "pX", "pS", "pY")
 SCRATCH.update({k: ("psum", [128, 512], F32) for k in _PS})
 SEMAPHORES = ["V", "S", "P", "G", "sent", "arr0", "arr1", "arr2"] + ["d%d" % i for i in range(12)]
 
-K = {"cyc": 1.0, "g": 1.3, "sc": 3.2, "pe": 0.5, "lat": 100.0, "fix": 30.0, "look": 250.0, "look2": 1.0, "vpen": 20000.0,
-     "ch0": [2] * 7 + [1, 1], "ch1": [4, 4, 2, 2, 2, 1, 1], "chr": [8, 4, 4], "spr": "VS",
-     "sp0": [(128, "VSG"), (128, "VSG")], "sp1": [(128, "VS"), (128, "VSG")]}
-K.update({"wt": (120e3, 95e3, 160e3, 150e3), "rounds": 200, "seed": 1, "noise": 1000.0})
+K = {"cyc": 1.0, "g": 1.3, "sc": 3.2, "pe": 0.5, "lat": 100.0, "fix": 30.0, "look": 250.0, "look2": 1.0, "tau": 0.0, "rest": 0.7, "ramp": 0, "vpen": 20000.0,
+     "ch0": ([4, 4, 4, 4], [4, 4, 4, 2, 2]), "ch1": ([4, 4, 2, 2, 2, 1, 1],) * 2, "chr": ([8, 4, 4],) * 2, "spr": "VS",
+     "ng": 11, "far": 30, "back": 2, "cutl": [96], "parts": [(160, 256), (0, 160)], "soon": 20000.0}
+K.update({"wt": (120e3, 110e3, 150e3), "rounds": 30, "seed": 1, "noise": 1000.0, "anneal": (16, 1350, 120, 0.0015, 0.05, 4),
+          "ramp": 1, "cutl": [128], "parts": [(128, 256), (0, 128)],
+          "soon": 10000.0, "chr": ([4, 4, 4, 2, 2],) * 2,
+          "tau": 100.0, "look": 450.0, "vpen": 2000.0, "rest": 1.0,
+          "ch0": ([2] * 8, [4, 4, 2, 2, 2, 2]), "ch1": ([2] * 7 + [1, 1], [4, 4, 2, 2, 2, 1, 1])})
 MODS = [dict(cyc=.9, g=1.3, sc=3.2, pe=.45, lat=200., rem=3200.), dict(cyc=.83, g=1.0, sc=2.0, pe=.42, lat=170., rem=2800.),
-        dict(cyc=1.2, g=1.9, sc=4.6, pe=.6, lat=260., rem=4000.), dict(cyc=.9, g=1.3, sc=3.2, pe=.7, lat=170., rem=3200.)]
+        dict(cyc=1.25, g=2.3, sc=6., pe=.65, lat=260., rem=4000.)]
 SILU1 = 1.2784645427610738
+EXTRA = {}
+PULL = ("NM<NW", "co0<NM", "XR<x", "MR<XR", "mn0<x")
+K["pull"] = 10.0
 _CACHE = {}
 
 
@@ -121,7 +133,10 @@ def build(g, core, T, topo, rank):
         add({"V": (f, 50 + cnt(in_) * K["sc"] if scat else vcost(cnt(out), two(out, in_)))}, [in_, scat], [out])
 
     def ms(out, v):
-        add({"V": (lambda q: q.memset(out[0], v), vcost(cnt(out), two(out)))}, [], [out])
+        alts = {"V": (lambda q: q.memset(out[0], v), vcost(cnt(out), two(out)))}
+        if v == int(v):
+            alts["G"] = (lambda q: q.iota(out[0], [[0, cnt(out)]], int(v), 0, allow_small_or_imprecise_dtypes=True), 130 + 2 * cnt(out) * cyc)
+        add(alts, [], [out])
 
     def scan(out, d0, d1, op0, op1):
         add({"V": (lambda q: q.tensor_tensor_scan(out[0], d0[0], d1[0], 0.0, op0, op1), vcost(cnt(out), two(out, d0, d1)))}, [d0, d1], [out])
@@ -166,6 +181,13 @@ def build(g, core, T, topo, rank):
         add({"G": (lambda q: q.iota(out[0], pat, base, cm, allow_small_or_imprecise_dtypes=True) if fl else q.iota(out[0], pat, base, cm),
                    130 + 2 * cnt(out) * cyc)}, [], [out])
 
+    turns = {}
+
+    def turn(k):
+        if k in turns:
+            ops[-1]["turn"] = [turns[k]]
+        turns[k] = len(ops) - 1
+
     gid = [0]
 
     def group():
@@ -173,10 +195,18 @@ def build(g, core, T, topo, rank):
         return [gid[0], True]
 
     def mm(gr, out, lhsT, rhs):
+        mms(gr, [(out, lhsT, rhs)])
+
+    def mms(gr, calls):
         first = gr[1]
         gr[1] = False
-        add({"P": (lambda q, stop: q.matmul(out[0], lhsT[0], rhs[0], first, stop), max(64, cnt(out)) * K["pe"])},
-            [lhsT, rhs], [out], grp=gr[0], first=first)
+
+        def f(q, stop):
+            for j, (out, lhsT, rhs) in enumerate(calls):
+                ins = q.matmul(out[0], lhsT[0], rhs[0], first and not j, stop and j == len(calls) - 1)
+            return ins
+        add({"P": (f, sum(max(64, cnt(c[0])) for c in calls) * K["pe"])},
+            [c[j] for j in (1, 2) for c in calls], [c[0] for c in calls], grp=gr[0], first=first)
 
     nd = [0]
 
@@ -220,11 +250,8 @@ def build(g, core, T, topo, rank):
     def slide(name, c, n=144, at="last"):
         ts(R(name, 0, n), R("IC", 0, n), col(at), c, A.is_equal, A.mult)
 
-    def mix(name, *terms):
-        (j, v), rest = terms[0], terms[1:]
-        flex(col(name), oh(j), "VS", scale=v)
-        for j, v in rest:
-            flex(col(name), oh(j), "VS", scale=v, bias=col(name))
+    def mix(name, a, v, b):
+        flex(col(name), a, "VS", scale=v, bias=b)
         return col(name)
     slide("Wp", col("w"))
     slide("Wn", col("-w"))
@@ -232,11 +259,20 @@ def build(g, core, T, topo, rank):
     ts(R("Ib"), R("IC", 0, 128), p, None, A.is_equal)
     ms(R("K5"), 592.0 / W)
     flex(col("16r"), r, "VS", scale=16.0)
-    ts(R("cT"), R("IC", 0, 16), col("16r"), None, A.add)
-    flex(R("E8"), R("IC", 0, 8), "VS", scale=oh(2), bias=mix("dig", (1, 64.0), (2, 64.0), (3, 1.0)))
-    for j in range(8):
+    iota(R("Z4"), [[1, 2], [2, 8]], 0, 0)
+    ts(R("cT"), R("Z4"), col("16r"), None, A.add)
+    ts(R("PI", 5, 6), R("PI", 1, 2), 1, None, A.bitwise_and)
+    ts(R("PI", 6, 7), R("PI", 1, 2), 14, None, A.bitwise_and)
+    ts(col("8b"), R("PI", 6, 7), 8.0, None, A.mult)
+    ts(col("at"), R("PI", 5, 6), 128.0, col("8b"), A.mult, A.add)
+    ts(R("cN"), R("IC", 0, 16), col("at"), None, A.add)
+    mix("pc1", col("at"), 16.0, 255.0)
+    keep = mix("keep", oh(1), 1.0, oh(2))
+    flex(R("E8"), R("IC", 0, 8), "VS", scale=oh(2), bias=mix("dig", keep, 64.0, oh(3)))
+    for j in range(4):
         flex(R("CT", 64 * j, 64 * j + 64), R("IC", 0, 64), "VS", scale=oh(1), bias=R("E8", j, j + 1))
-    ts(R("EQ"), R("IC", 0, 8), oh(2), 8.0, A.mult, A.mult)
+    flex(R("EQ"), R("IC", 0, 8, ), "VS", scale=mix("8hi", oh(2), 8.0, 0.0))
+    flex(R("CT", 256, 512), R("CT", 0, 256), "VS", bias=mix("4hi", oh(2), 4.0, 0.0))
     iota(R("Z2", parts=top), [[100, 8], [0, 2], [1, 8]], 0, -100)
     ts(R("SEL", parts=top), R("Z2", parts=top), 0.0, None, A.is_equal)
     for j, bank in enumerate(("pK1", "pA", "pD", "pX", "pS", "pY", "pK0", "pK1")):
@@ -244,32 +280,29 @@ def build(g, core, T, topo, rank):
         mm(gr, R(bank, 0, 512), R("Ib"), R("CT"))
         mm(gr, R(bank, 0, 512), R("SEL", parts=top), R("MK", 512 * j, 512 * j + 512, parts=top))
         flex(R("M", SP + 512 * j, SP + 512 * j + 512), R(bank, 0, 512), "VS", bias=R("EQ", j, j + 1))
-    dma("G", [(T.TI[0:8, 0:1], T.th[:])], [], [R("TI")], 2500)
+    dma("Y", [(T.TI[0:8, 0:1], T.th[:])], [], [R("TI")], 2500)
     dma("Y", [(T.DI[j:128:16, :], T.dl[:]) for j in range(16)], [R("x")], [R("DI")], 3500)
-    slide("Wk", 512.0 * KS)
-    slide("Wm", mix("m", (0, 1.0), (8, KS)))
+    slide("Wk0", 512.0 * KS)
+    slide("Wm", mix("m", oh(8), KS, oh(0)))
     ts(R("Is"), R("IC", 0, 128), p, KS, A.is_equal, A.mult)
     iota(R("KC"), [[-32, 16], [0, 16]], 480, 0)
     for nm, a, b in (("RSx", 2.0 * KS, -1e4), ("RSn", -2.0 * KS, 1e4)):
         ms(R(nm), a)
         ms(R(nm, 0, 256, 16), b)
-    flex(col("pc"), r, "VS", scale=256.0, bias=255.0)
-    flex(col("pcr"), r, "VS", scale=96.0, bias=255.0)
-    mix("one", (0, 1.0), (3, 1.0), (8, 1.0))
-    flex(col("keep"), col("one"), "VS", scale=-1.0, bias=1.0)
-    flex(col("silu"), col("one"), "VS", scale=SILU1)
-    slide("Wl", mix("live", (0, 8192.0), (3, -8192.0)))
-    slide("Ws", -512.0 * KS)
-    flex(col("ya"), g16, "VS", scale=0.375, bias=5.0)
-    slide("WyA", mix("col", (1, 1.0), (2, 64.0), (3, -4160.0)), 64, "ya")
-    slide("WyL", col("live"), 64, "ya")
+    flex(R("PC"), R("IC", 0, 17), "VS", scale=col("16r"), bias=255.0)
+    mix("silu", keep, -SILU1, SILU1)
+    ts(col("dead"), oh(3), oh(0), 8192.0, A.subtract, A.mult)
+    slide("Wl", col("dead"))
+    mix("ya", g16, 0.375, 5.0)
+    slide("WyA", mix("slot", oh(3), SP - 4160.0, mix("num", oh(2), 64.0, oh(1))), 64, "ya")
+    slide("WyL", mix("live", col("dead"), -1.0, 0.0), 64, "ya")
     iota(R("GC"), [[16, 8], [0, 16]], 0, 0)
     iota(R("RC"), [[0, 8], [1, 16]], 0, 0)
     ts(R("BLK"), R("GC"), g16, None, A.is_equal)
-    for nm, c, s in (("Dp", mix("dp", (1, 2.0 ** 14), (2, 2.0 ** 20)), 1.0), ("Dn", mix("dn", (1, -2.0 ** 14), (2, -2.0 ** 20)), 1.0),
-                     ("Dv", mix("dv", (1, 1.0), (2, 64.0), (3, SP - 4160.0)), 1.0), ("Lp", mix("lp", (0, -2.0 ** 27)), 1.0),
-                     ("Ln", mix("ln", (0, 2.0 ** 27)), 1.0), ("Lv", mix("lv", (0, -8192.0), (3, 8192.0)), 1.0)):
-        flex(R(nm), R("BLK"), "VS", scale=c)
+    for k, c in (("D", "slot"), ("L", "dead")):
+        flex(R(k + "v"), R("BLK"), "VS", scale=col(c))
+        flex(R(k + "p"), R(k + "v"), "VS", scale=2.0 ** 14)
+        flex(R(k + "n"), R(k + "v"), "VS", scale=-2.0 ** 14)
     iota(R("J"), [[0, 9], [1, 32]], 0, 0)
     flex(col("15-r"), r, "VS", scale=-1.0, bias=15.0)
     for k, c in (("a", r), ("l", col("15-r"))):
@@ -279,13 +312,14 @@ def build(g, core, T, topo, rank):
             ra = "RA%s%d" % (k, h)
             ts(R(ra), R("J", o, o + 256), c, None, A.not_equal)
             flex(R(ra, 31, 256, 32), R(ra, 31, 256, 32), "VS", scale=2.0 ** -14)
-    flex(col("r16"), r, "VS", bias=16.0)
-    for nm, v in (("a0", W + SP), ("a1", W + SP + 16), ("l0", L + SP), ("l1", L + SP + 16)):
-        flex(col(nm), r, "VS", bias=float(v))
-    ts(R("cV"), R("cT"), -1.0, 255.0, A.mult, A.add)
-    iota(R("Z3", 0, 16), [[-16, 16]], 255, 0)
-    ts(R("cW"), R("Z3", 0, 16), r, None, A.subtract)
-    iota(R("SLT"), [[1, 6], [6, 16]], 0, 0)
+    ms(R("ZZ"), 0.0)
+    iota(R("Z5"), [[W - L - 64, 2], [16, 2]], L + 64 + SP, 0)
+    flex(R("HI"), R("Z5"), "VS", bias=r)
+    mix("r16", r, 1.0, 16.0)
+    iota(R("SLT"), [[-1, 6], [-6, 16]], CP, 0)
+    iota(R("RZ"), [[0, 32], [128, 16]], 0, 0)
+    for a in range(0, 1536, 512):
+        ms(R("ZR", a, a + 512), 0.0)
     flex(R("Ob", 0, 1), oh(3), "VS")
     flex(R("NOH"), R("OH"), "VS", scale=-1.0, bias=1.0)
     ts(R("Z1"), R("RC"), r, None, A.is_ge)
@@ -293,118 +327,167 @@ def build(g, core, T, topo, rank):
     flex(col("-r"), r, "VS", scale=-1.0)
     flex(R("DLO"), R("Ib"), "VS", scale=col("-r"))
     flex(col("r-1"), r, "VS", bias=-1.0)
-    ms(R("O16"), 1.0 / 16)
+    ms(R("O16"), -1.0 / 16)
+    ms(R("KX", 0, 1), 8.0 * CP - 12288.0)
     ms(R("ON"), 1.0)
     ms(R("PRE", 0, 1), 0.0)
     iota(R("CLn", 0, 16), [[-16, 16]], -256, 0)
-    iota(R("CLp", 0, 17), [[16, 17]], 256, 0)
-    ms(R("CLp", 16, 17), 0.0)
+    iota(R("CLp", 0, 16), [[16, 16]], 256, 0)
     iota(R("Z3", 0, 128, parts=top), [[1, 8], [0, 16]], 0, -1)
     ts(R("SE2", parts=top), R("Z3", 0, 128, parts=top), 0.0, 512.0 * KS, A.is_equal, A.mult)
-    ts(col("th", top), R("TI", 0, 1, parts=top), -1.0, 1.0, A.mult, A.add)
-    ts(R("TH", parts=top), R("ON", parts=top), col("th", top), None, A.mult)
+    ts(col("th", top), R("TI", 0, 1, parts=top), -1.0, None, A.add)
+    ts(R("TH", parts=top), R("ON", 0, 16, parts=top), col("th", top), None, A.mult)
     for t in range(NS):
         ms(R("box%d" % t, 0, 112), 0.0)
-        cp(R("DW", 256 * t, 256 * t + 256), R("DI", 256 * t, 256 * t + 256))
+        ts(R("DW", 256 * t, 256 * t + 256), R("DI", 256 * t, 256 * t + 256), 64.0, None, A.add)
     for j in range(4):
-        cp(R("NM", SP + 256 * j, SP + 256 * j + 256), R("NI", 256 * j, 256 * j + 256))
-    flex(R("M1"), R("M", SP, SP + L), "G")
+        ts(R("NM", SP + 256 * j, SP + 256 * j + 256), R("NI", 256 * j, 256 * j + 256), 64.0, None, A.add)
     names = R("NM", SP, SP + L)
     AB0 = 312 - 0.40625
 
-    def place(k, n, ab, out=None):
-        ts(R("u1" + k, 0, n), R("pU", 0, n), -0.5 + 2.0 ** -13 - 592.0 / W, None, A.add)
-        tt(R("u3" + k, 0, n), R("pU", 0, n), R("u1" + k, 0, n), A.subtract)
-        square(R("u4" + k, 0, n), R("u3" + k, 0, n))
-        if out:
-            ts(out, R("u4" + k, 0, n), 2.0 ** 19, ab, A.mult, A.add)
-            return
-        ts(R("u1" + k, 0, n), R("u4" + k, 0, n), 2.0 ** 19, ab, A.mult, A.add)
-        place2(k, n)
+    def place(k, pu, ab, a=0, out=None):
+        u1, u2, u3, u4 = (R("u%d%s" % (j, k), a, a + cnt(pu)) for j in (1, 2, 3, 4))
+        ts(u1, pu, -0.5 + 2.0 ** -13 - 592.0 / W, None, A.add)
+        tt(u3, pu, u1, A.subtract)
+        square(u4, u3)
+        ts(u1, u4, 2.0 ** 19, ab, A.mult, A.add)
+        ts(out or u2, u1, 1023, None, A.bitwise_and)
+        if not out:
+            cp(R("lo" + k, a, a + cnt(pu)), u2)
 
-    def place2(k, n):
-        ts(R("u2" + k, 0, n), R("u1" + k, 0, n), 1023, None, A.bitwise_and)
-        cp(R("lo" + k, 0, n), R("u2" + k, 0, n))
-
-    def umm(o, wn, rhs):
+    def umm(o, rhs, wn="Wn"):
         gr = group()
         mm(gr, o, R("Ib"), R("K5", 0, cnt(o)))
-        for j in range(16):
-            mm(gr, o, sl(wn, j), rhs(j))
+        mms(gr, [(o, sl(wn, j), rhs(j)) for j in range(16)])
+        return o
 
-    def columns(k, n, t, nm):
-        ts(R("co" + k, 0, 16 * n), nm, (15 - t) / 16.0, -15.0 / 32, A.mult, A.add, off=R("lo" + k, 0, n))
+    def columns(k, n, t, nm, a=0):
+        up = 0 if nm[1] == "NI" else 4 * (15 - t)
+        ts(R("co" + k, 16 * a, 16 * (a + n)), nm, (15 - t) / 16.0, -15.0 / 32 - up, A.mult, A.add, off=R("lo" + k, a, a + n))
 
-    def spread(yr, src, parts, scale=1.0):
-        b = 0
-        for n, e in parts:
-            a, b = b, b + n
-            for k in range(16):
-                flex(R(yr, 16 * a + k, 16 * b, 16), R(src[0], src[1] + a, src[1] + b), e, scale=scale)
+    def spread(yr, h, src, e, scale=1.0, plus=None, ng=0):
+        for k in range(16):
+            out = R(yr, 2048 * h + k, 2048 * h + 2048, 16)
+            if k < ng:
+                flex(out, plus, "G")
+            else:
+                flex(out, src, e, scale=scale)
 
-    def scores(k, n, B, yr, pk):
+    def scores(k, n, B, yr, pk, chunks, c0=0, ramp=None):
         gr = group()
-        w = 16 * n
+        w, e0 = 16 * n, 256 * c0
         mm(gr, R(pk, 0, w), R("Is"), R("KC", 0, w))
-        for nm, wn in (("mn", "Wk"), ("G", "Wm")):
+        if ramp:
+            for a in range(0, 16, 2):
+                j, e = a // 4, 5 * w * (a % 4)
+                act(R("XR", e + j, e + 10 * w, 5), R("x", 0, B), scale=2.0 ** j, bias=128.0 * 2 ** j,
+                    off=R("co" + k, 16 * c0 + n * a, 16 * c0 + n * (a + 2)))
+            for e in (0, 1280):
+                scan(R("MR", e, e + 1280), R("XR", e, e + 1280), R(ramp, e, e + 1280), A.max, A.min)
+                mms(gr, [(R(pk, 0, w), sl("Wk%d" % (a // 4), a), R("MR", 5 * w * (a % 4) + a // 4, 5 * w * (a % 4 + 1), 5))
+                         for a in range(16) if a % 4 // 2 == e // 1280])
+        for nm, wn, chs in (("mn", "Wk0", [] if ramp else chunks[0]), ("G", "Wm", chunks[1])):
             a = 0
-            for ch in K["ch" + k]:
-                o = R("co" + k, n * a, n * (a + ch))
+            for ch in chs:
+                o = R("co" + k, 16 * c0 + n * a, 16 * c0 + n * (a + ch))
+                out = R(nm + k, e0 + w * a, e0 + w * (a + ch))
                 if nm == "mn":
-                    tt(R(nm + k, w * a, w * (a + ch)), R("x", 0, B), R(yr, w * a, w * (a + ch)), A.min, off=o)
+                    tt(out, R("x", 0, B), R(yr, out[2], out[3]), A.min, off=o)
+                    turn(k == "r")
                 else:
-                    flex(R(nm + k, w * a, w * (a + ch)), R("M", SP, SP + B), "VS", off=o)
-                ops[-1]["rest"] = (16 - a - ch) * w * K["g"]
-                for j in range(a, a + ch):
-                    mm(gr, R(pk, 0, w), sl(wn, j), R(nm + k, w * j, w * j + w))
+                    flex(out, R("M", SP, SP + B), "VS", off=o)
+                    ops[-1]["rest"] = (16 - a - ch) * w * K["g"] * K["rest"]
+                mms(gr, [(R(pk, 0, w), sl(wn, 2 * (j % 8) + j // 8 if k == "1" else j), R(nm + k, e0 + w * j, e0 + w * j + w))
+                         for j in range(a, a + ch)])
                 a += ch
 
-    def best(k, n, pk, pc):
-        w = 16 * n
-        scan(R("SX" + k, 0, w), R("RSx", 0, w), R(pk, 0, w), A.add, A.max)
-        ts(R("p1" + k, 0, n), R("SX" + k, 15, w, 16), 1 / KS, None, A.mult)
-        ts(R("p2" + k, 0, n), R("p1" + k, 0, n), 1, 255, A.arith_shift_right, A.bitwise_and)
-        ts(R("po" + k, 0, n), R("p2" + k, 0, n), -1.0, pc, A.mult, A.add)
+    def best(k, n, pk, pc, c0=0):
+        w, e0 = 16 * n, 16 * c0
+        scan(R("SX" + k, e0, e0 + w), R("RSx", 0, w), R(pk, 0, w), A.add, A.max)
+        p1, p2 = R("p1" + k, c0, c0 + n), R("p2" + k, c0, c0 + n)
+        ts(p1, R("SX" + k, e0 + 15, e0 + w, 16), 1 / KS, None, A.mult)
+        ts(p2, p1, 1, 255, A.arith_shift_right, A.bitwise_and)
+        ts(R("po" + k, c0, c0 + n), p2, -1.0, pc, A.mult, A.add)
 
-    def single(k, tab, w, dig, lv, pd):
-        (dn, d0), (ln, l0) = dig, lv
+    def run(name, f, d, n):
+        if d > 0:
+            return R(name, f, f + d * (n - 1) + 1, d)
+        real, o = _AT[name]
+        e = o + f + d * n
+        return (T[real][:, o + f:e if e >= 0 else None:d], name, f + d * (n - 1), f + 1, -d)
+
+    def plain(name, f, w):
+        return [(0, 1, w, name, f, 1)], (name, f + 31, 32)
+
+    def single(k, tab, w, dig, lv, pd, a=0, cut=[]):
         gr = group()
-        mm(gr, R(pd, 0, w - 1), R("Lp"), R(ln, l0, l0 + w - 1))
-        mm(gr, R(pd, 0, w - 1), R("Ln"), R(ln, l0 + 1, l0 + w))
-        mm(gr, R(pd, 0, w - 1), R("Dp"), R(dn, d0, d0 + w - 1))
-        mm(gr, R(pd, 0, w - 1), R("Dn"), R(dn, d0 + 1, d0 + w))
-        gr = group()
-        mm(gr, R(pd, 31, w, 32), R("Lv"), R(ln, l0 + 31, l0 + w, 32))
-        mm(gr, R(pd, 31, w, 32), R("Dv"), R(dn, d0 + 31, d0 + w, 32))
-        for h in (0, 1):
-            ds, sd = R("DS%d%s" % (h, k), 0, w), "SD%d%s" % (h, k)
-            o = 16 * (h if tab == "a" else 1 - h)
-            scan(ds, R("RA%s%d" % (tab, h), 0, w), R(pd, 0, w), A.mult, A.add)
+        for c, (runs, ends) in (("L", lv), ("D", dig)):
+            calls = [(R(pd, 0, w), R("Lp"), R("ZZ", 0, w))] if c == "L" and len(runs) > 1 else []
+            for o, s, n, nm, f, d in runs:
+                calls.append((R(pd, o, o + s * (n - 1) + 1, s), R(c + "p"), run(nm, f, d, n)))
+            for o, s, n, nm, f, d in runs:
+                if o == 0:
+                    o, n, f = s, n - 1, f + d
+                calls.append((R(pd, o - 1, o + s * (n - 1), s), R(c + "n"), run(nm, f, d, n)))
+            mms(gr, calls)
+        mms(group(), [(R(pd, 31, w, 32), R(c + "v"), run(*ends, w // 32)) for c, (runs, ends) in (("L", lv), ("D", dig))])
+        for h, u, v in [(h, u, v) for u, v in zip([0] + cut, cut + [w]) for h in (0, 1)]:
+            o = u + 16 * (h if tab == "a" else 1 - h)
+            ds, sd = R("DS%d%s" % (h, k), a + o, a + v), "SD%d%s" % (h, k)
+            scan(ds, R("RA%s%d" % (tab, h), o, v), R(pd, o, v), A.mult, A.add)
             act(ds, ds, F.Abs)
-            scan(R(sd, 0, w), R("RB" + tab, o, o + w), ds, A.add, A.min)
-            ts(R("OF" + k, h, w // 16, 2), R(sd, 31, w, 32), col("r16") if h else r, col(tab + str(h)), A.max, A.min)
+            scan(R(sd, a + o, a + v), R("RB" + tab, 2 * o - u, o + v - u), ds, A.add, A.min)
+            ts(R("OF" + k, (a + u) // 16 + h, (a + v) // 16, 2), R(sd, a + u + 31, a + v, 32), col("r16") if h else r,
+               R("HI", h + 2 * (tab == "a"), h + 2 * (tab == "a") + 1),
+               A.max, A.min)
 
-    def mark(k, n, ga, lv, s, pd):
-        w = 16 * n
-        gf = "GF" if s == "a" else "GFb"
-        act(ga, R("G" + k, 0, 256 * n), off=R("po" + k, 0, n))
-        flex(R(gf, 0, w), ga, "SV", scale=col("keep"), bias=col("silu"))
-        single(s, "a", w, (ga[1], ga[2]), (lv, 0), pd)
+    def winners(k, n, ga, lv, s, pd, c0=0, whole=True):
+        w, e0 = 16 * n, 16 * c0
+        act(ga, R("G" + k, 256 * c0, 256 * (c0 + n)), off=R("po" + k, c0, c0 + n))
+        if whole:
+            flex(R("GF" + s, e0, e0 + w), ga, "SV", scale=col("keep"), bias=col("silu"))
+        single(s, "a", w, plain(ga[1], ga[2], w), lv, pd, e0)
+
+    def mark(n, s):
         for j in range(0, n, 2):
-            act(R("M"), R(gf, 16 * j, 16 * j + 32), F.Silu, scat=R("OF" + s, j, j + 2))
+            act(R("M"), R("GF" + s, 16 * j, 16 * j + 32), F.Silu, scat=R("OF" + s, j, j + 2))
 
-    umm(R("pU", 0, 16), "Wp", lambda j: R("x", B0 + 16 * j, B0 + 16 * j + 16))
-    place("0", 16, AB0)
+    early = len(ops)
     for t in range(NS):
         B = W - 256 * (t + 1)
-        flex(R("yT%d" % t), R("x", B, B + 256), "S", off=R("cT"))
-    spread("yr0", ("yT0", 0), K["sp0"])
-    for t in (1, 2):
-        B = W - 256 * (t + 1)
-        umm(R("pU", 16 * t - 16, 16 * t), "Wp", lambda j: R("x", B + 16 * j, B + 16 * j + 16))
-    place("1", 32, AB0, out=R("L0"))
-    for t in (1, 2):
-        spread("yr%d" % t, ("yT%d" % t, 0), [(256, "G")])
+        act(R("yT%d" % t), R("x", B, B + 256), off=R("cT"))
+        for h in (0, 1):
+            o = 16 * max(t - 1, 0) + 8 * h
+            umm(R("pS" if t else "pU", o, o + 8), lambda j: R("x", B + 2 * j + h, B + 256, 32), "Wp")
+        if t == 0:
+            place("0", R("pU", 0, 16), AB0)
+        spread("yr%d" % t, 0, R("x", B, B + 256, 2), "G" if t else "VSG")
+        if not (t and K["ramp"]):
+            spread("yr%d" % t, 1, R("x", B + 1, B + 256, 2), "G" if t else "VSG")
+        else:
+            for j in range(4):
+                flex(R("yQ%d" % t, 32 * j, 32 * j + 32), R("x", B + 64 * j + 1, B + 64 * j + 64, 2), "VS", scale=2.0 ** j, bias=128.0 * 2 ** j)
+            flex(R("yU%d" % t), R("yT%d" % t, 128, 256), "VS", bias=128.0)
+            ms(R("Y3%d" % t, 4, 2560, 5), 0.0)
+            spread("yr%d" % t, 1, R("yQ%d" % t), "G")
+            for j in range(4):
+                flex(R("Y3%d" % t, j, 2560, 5), R("yr%d" % t, 2048 + 512 * j, 2560 + 512 * j), "G")
+    for o in ops[early:]:
+        if list(o["alts"]) == ["G"] or o["w"][0][1][:2] == "yQ":
+            o["boost"] = K["soon"]
+    if K["ramp"]:
+        ms(R("XR", 4, 2560, 5), 0.0)
+        for j in (1, 2, 3):
+            flex(R("Wk%d" % j), R("Wk0"), "VS", scale=0.5 ** j)
+        for j in range(4):
+            ms(R("SC", 4 * j, 4 * j + 4), 0.5 ** j)
+        for a in (16, 32, 64):
+            flex(R("SC", a, 2 * a), R("SC", 0, a), "VSG")
+        ts(R("PI", 3, 4), R("PI", 1, 2), 3, None, A.bitwise_and)
+        ts(R("PI", 4, 5), R("PI", 1, 2), 2, None, A.arith_shift_right)
+        ts(col("q3"), R("PI", 3, 4), 640.0, 1275.0, A.mult, A.add)
+        ts(col("pq"), R("PI", 4, 5), col("q3"), None, A.add)
+    place("r", R("pS", 0, 32), AB0, out=R("L0"))
     gy = group()
     py = R("pY", 0, 256, parts=slice(0, 48))
     N = len(T.cores)
@@ -412,55 +495,65 @@ def build(g, core, T, topo, rank):
         B = W - 256 * (t + 1)
         ab = AB0 if t == 0 else R("Ab", t, t + 1)
         lv = "LV%d" % t
-        flex(R(lv), R("M", SP + B, SP + B + 256), "VS")
+        flex(R(lv, 0, 256), R("M", SP + B, SP + B + 256), "VS")
         if t:
-            mm(group(), R("pS", 64, 65), R("O16"), R("LB%d" % (t - 1), 15, 16))
-            cp(R("a1", 0, 1), R("pS", 64, 65))
-            ts(R("a2", 0, 1), R("a1", 0, 1), 63, None, A.bitwise_and)
-            ts(ab, R("a2", 0, 1), AB0, None, A.add)
-            ts(R("u10", 0, 16), R("L0", 16 * t - 16, 16 * t), ab, -AB0, A.add, A.add)
-            place2("0", 16)
-        columns("0", 16, t, names if t else R("NI"))
-        scores("0", 16, B, "yr%d" % t, "pK0")
-        best("0", 16, "pK0", col("pc"))
-        tt(R("ny0"), R("mn0"), R("x", B, B + 256), A.subtract, off=R("po0"))
-        ga0 = R("GA", 512 * t, 512 * t + 256)
-        umm(R("pU", 0, 16), "Wn", lambda j: R("ny0", 16 * j, 16 * j + 16))
-        place("1", 16, ab)
-        columns("1", 16, t, names if t else R("NI"))
-        flex(R("yT1h"), R("ny0"), "S", scale=-1.0, off=R("cT"))
-        mark("0", 16, ga0, lv, "a", "pD")
-        spread("yr1h", ("yT1h", 0), K["sp1"])
-        scores("1", 16, B, "yr1h", "pK1")
+            flex(ab, R("LB%d" % (t - 1), 14, 15), "VS", bias=AB0)
+        else:
+            columns("0", 16, t, R("NI"))
+        for h, pk, pd in ((0, "pK0", "pD"), (1, "pX", "pA")):
+            e = 128 * h
+            ramp = K["ramp"] and t and h and "Y3%d" % t
+            scores("0", 8, B, "yr%d" % t, pk, K["ch0"], 8 * h, ramp)
+            best("0", 8, pk, R("PC", 8, 9), 8 * h)
+            if ramp:
+                ts(R("pq"), R("p20", 8, 16), -5.0, col("pq"), A.mult, A.add)
+                tt(R("sel"), R("MR"), R("SC"), A.mult, off=R("pq"))
+                tt(R("ny0", e, e + 128), R("sel"), R("yU%d" % t), A.subtract)
+            else:
+                tt(R("ny0", e, e + 128), R("mn0", 16 * e, 16 * e + 2048), R("yT%d" % t, e, e + 128), A.subtract, off=R("po0", 8 * h, 8 * h + 8))
+            place("1", umm(R("pU", 8 * h, 8 * h + 8), lambda j: R("ny0", e + j, e + 128, 16)), ab, 8 * h)
+            columns("1", 8, t, names if t else R("NI"), 8 * h)
+            winners("0", 8, R("GA", 544 * t + 136 * h, 544 * t + 136 * h + 128),
+                    ([(16 * b, 1, 16, lv, 2 * b + h, 16) for b in range(8)], (lv, 242 + h, 4)), "a", pd, 8 * h)
+        flex(R("yP", 128, 256), R("ny0", 128, 256), "VS", scale=-1.0)
+        act(R("nyN"), R("ny0"), off=R("cN"))
+        mark(16, "a")
+        spread("yr1h", 0, R("ny0", 0, 128), "VS", -1.0)
+        spread("yr1h", 1, R("ny0", 128, 256), "VS", -1.0, R("yP", 128, 256), K["ng"])
+        scores("1", 16, B, "yr1h", "pK1", K["ch1"])
         act(R("NO"), names, off=R("lo1", 0, 16))
-        act(R("PT"), R("M1"), off=R("lo1", 0, 16))
-        act(R("PV"), R("PT"), off=R("cV"))
-        act(R("LVv"), R(lv), off=R("cW"))
-        tt(R("DF"), R("NO"), R("DW", 256 * t, 256 * t + 256), A.subtract, off=R("cT"))
-        single("l", "l", 256, ("PV", 0), ("LVv", 0), "pX")
-        best("1", 16, "pK1", col("pc"))
-        tt(R("ny1"), R("mn1"), R("ny0"), A.add, off=R("po1"))
+        act(R("PT"), R("M", SP, SP + L), off=R("lo1", 0, 16))
+        for a, b in K["parts"]:
+            tt(R("DF", a, b), R("NO"), R("DW", 256 * t + a, 256 * t + b), A.subtract, off=R("cN", a // 16, b // 16))
+        single("l", "l", 256, ([(15 - 2 * (j % 8) - j // 8, 16, 16, "PT", 16 * j + 15, -1) for j in range(16)], ("PT", 14, -2)),
+               ([(0, 1, 256, lv, 255, -1)], (lv, 224, -32)), "pX", cut=K["cutl"])
+        best("1", 16, "pK1", col("pc1"))
+        act(R("ny1"), R("mn1"), off=R("po1"))
         box, lb = "box%d" % t, "LB%d" % t
         gr = group()
         mm(gr, R("pS", 0, 16), R("SE2", parts=top), R("TH", parts=top))
-        for j in range(16):
-            mm(gr, R("pS", 0, 16), sl("Wl", j), R(lv, j, 256, 16))
-        for j in range(16):
-            mm(gr, R("pS", 0, 16), sl("Ws", j), R("ny0", j, 256, 16))
+        mms(gr, [(R("pS", 0, 16), sl("Wl", j), R(lv, j, 256, 16)) for j in range(16)])
+        mms(gr, [(R("pS", 0, 16), sl("Wk0", 2 * (j % 8) + j // 8), R("ny0", 16 * j, 16 * j + 16)) for j in range(16)])
         ts(R("q2"), R("p11", 0, 16), 1, None, A.bitwise_and)
-        tt(R("q4"), R("SX1", 15, 256, 16), R("pS", 0, 16), A.subtract)
+        tt(R("q4"), R("SX1", 15, 256, 16), R("pS", 0, 16), A.add)
         tt(R("RD"), R("q2"), R("q4"), A.is_gt)
-        scan(R("PRE", 1, 17), R("ON"), R("RD"), A.mult, A.add)
+        scan(R("PRE", 1, 17), R("ON", 0, 16), R("RD"), A.mult, A.add)
         tt(R("NRC"), R("RD"), R("CLn", 0, 16), A.mult)
         gr = group()
-        mm(gr, R("pS", 32, 49), R("Ib"), R("CLp", 0, 17))
-        mm(gr, R("pS", 32, 48), R("TRb"), R("RD"))
-        mm(gr, R("pS", 32, 48), R("DLO"), R("RD"))
+        mm(gr, R("pS", 32, 48), R("Ib"), R("CLp", 0, 16))
+        mms(gr, [(R("pS", 32, 48), R("TRb"), R("RD")), (R("pS", 32, 48), R("DLO"), R("RD"))])
         mm(gr, R("pS", 32, 48), R("Ib"), R("NRC"))
-        mm(gr, R("pS", 32, 49), R("BLK"), R("PRE", 0, 17))
+        mm(gr, R("pS", 32, 48), R("BLK"), R("PRE", 0, 16))
         ts(R("SL"), R("pS", 32, 48), col("r-1"), None, A.add)
-        ts(R(box, 15, 16), R("pS", 48, 49), float(CP), None, A.min)
-        cp(R(box, 16, 784), R("ny1"), scat=R("SL"))
+        mm(group(), R("pK0", 0, 1), R("BLK"), R("PRE", 16, 17))
+        act(R(box, 15, 16), R("pK0", 0, 1), F.Relu, scale=-1.0, bias=float(CP))
+        if t < NS - 1:
+            gr = group()
+            mm(gr, R("pK0", 1, 2), R("Ib"), R("KX", 0, 1))
+            mm(gr, R("pK0", 1, 2), R("O16"), R(box, 15, 16))
+            act(R("aq", 0, 1), R("pK0", 1, 2), scale=-1.0, bias=31.5)
+            act(R(box, 14, 15), R("pK0", 1, 2), bias=R("aq", 0, 1))
+        tt(R(box, 16, 784), R("ny1"), R("nyN"), A.add, scat=R("SL"))
         dst = T.cores[(rank + 1 + t % (N - 1)) % N]
         rid, pid, _se = topo.addr(dst)
 
@@ -472,29 +565,52 @@ def build(g, core, T, topo, rank):
         ts(R("kn1"), R("SN", 15, 256, 16), 1 / KS, 30.0, A.mult, A.add)
         ts(R("kn2"), R("kn1"), 1, 15, A.arith_shift_right, A.bitwise_and)
         cp(R("kn"), R("kn2"))
-        tt(R("TT"), R("NOH"), R("DF"), A.mult, off=R("kn"))
+        for a, b in K["parts"]:
+            tt(R("TT", a, b), R("NOH"), R("DF", a, b), A.mult, off=R("kn", a // 16, b // 16))
+            tt(R("NW", a, b), R("TT", a, b), R("DW", 256 * t + a, 256 * t + b), A.add)
         for j in range(8):
             a = 224 - 32 * j
-            tt(R("NM"), R("TT", a, a + 32), R("DW", 256 * t + a, 256 * t + a + 32), A.add, scat=R("OFl", 2 * j, 2 * j + 2))
-        ga1 = R("GA", 512 * t + 256, 512 * t + 512)
-        mark("1", 16, ga1, lv, "b", "pA")
-        for h, ga in ((0, ga0), (1, ga1)):
-            j = 2 * t + h
-            mm(gy, py, R("WyA", 5 - j, 53 - j), ga)
-            mm(gy, py, R("WyL", 5 - j, 53 - j), R(lv))
-        umm(R("pU", 0, 6), "Wn", lambda j: R(lb, 16 + j, 112, 16))
-        place("r", 6, ab)
+            act(R("NM"), R("NW", a, a + 32), F.Silu, scat=R("OFl", 2 * j, 2 * j + 2))
+        ga1 = R("GA", 544 * t + 272, 544 * t + 528)
+        winners("1", 16, ga1, plain(lv, 0, 256), "b", "pA")
+        mark(16, "b")
+        for j in (2 * t, 2 * t + 1):
+            mm(gy, py, R("WyL", 5 - j, 53 - j), R(lv, 0, 256))
+        mm(gy, py, R("WyA", 4 - 2 * t, 52 - 2 * t), ga1)
+        for b in range(0, 32, 4):
+            mms(gy, [(R("pY", 16 * (a // 2) + a % 2, 16 * (a // 2) + 16, 2, parts=slice(0, 48)), R("WyA", 5 - 2 * t, 53 - 2 * t),
+                      R("GA", 544 * t + 136 * (a % 2) + a // 2, 544 * t + 136 * (a % 2) + 128, 16)) for a in range(b, b + 4)])
+        if t < NS - 1:
+            ts(R("lo0", 0, 16), R("L0", 16 * t, 16 * t + 16), R(lb, 14, 15), None, A.add)
+            flex(R("NM", SP + L, SP + L + 64), R("NM", SP, SP + 64), "VS")
+            columns("0", 16, t + 1, R("NM", SP, SP + L + 64))
+            first = len(ops) - 1
+        place("r", umm(R("pU", 64, 70), lambda j: R(lb, 16 + j, 112, 16)), ab)
         columns("r", 6, t, names)
-        spread("yrr", (lb, 16), [(96, K["spr"])], scale=-1.0)
-        scores("r", 6, B, "yrr", "pK1")
-        best("r", 6, "pK1", col("pcr"))
-        ts(R("LVr"), R("SLT"), R(lb, 15, 16), R("Ob", 0, 1), A.is_lt, A.max)
-        mark("r", 6, R("GAr"), "LVr", "a", "pD")
+        if t < NS - 1:
+            ops[-K["back"]]["turn"] = [first]
+        flex(R("ZR", 0, 1536, 16), R(lb, 16, 112), "VS", scale=-1.0)
+        for a in range(0, 1536, 512):
+            scan(R("yrr", a, a + 512), R("RZ"), R("ZR", a, a + 512), A.min, A.add)
+        scores("r", 6, B, "yrr", "pK1", K["chr"])
+        best("r", 6, "pK1", R("PC", 6, 7))
+        ts(R("LVr", 0, 96), R("SLT"), R(lb, 15, 16), R("Ob", 0, 1), A.is_gt, A.max)
+        winners("r", 6, R("GAr", 0, 96), plain("LVr", 0, 96), "a", "pD", whole=t < NS - 1)
+        if t < NS - 1:
+            mark(6, "a")
+    for a in range(SP, SP + W, 512):
+        flex(R("MB", a, a + 512), R("M", a, a + 512), "VS")
+    for j in range(0, 6, 2):
+        cp(R("MB"), R("ON", 0, 32), scat=R("OFa", j, j + 2))
     ya = R("YA", parts=slice(0, 48))
-    ts(ya, py, -1.0, None, A.max)
+    ts(ya, py, -float(SP), -1.0, A.add, A.max)
     dma("Y", [(T.ya[:], ya[0])], [ya], [], 2000)
-    dma("Y", [(T.yo[:], T.NM[:, SP:SP + L])], [R("NM")], [], 4000)
-    dma("G", [(T.ym[:], T.M[0:128:16, SP:SP + W])], [R("M")], [], 2300)
+    for a in range(0, L, 256):
+        ts(R("NI", a, a + 256), R("NM", SP + a, SP + a + 256), -64.0, None, A.add)
+        cp(R("YO", a, a + 256), R("NI", a, a + 256))
+        if a % 512:
+            dma("Y", [(T.yo[:, a - 256:a + 256], T.YO[:, a - 256:a + 256])], [R("YO", a - 256, a + 256)], [], 3600)
+    dma("Y", [(T.ym[:], T.MB[0:128:16, SP:SP + W])], [R("MB")], [], 2000)
     return ops
 
 
@@ -521,7 +637,8 @@ def depend(ops):
             if ps and o["grp"] is not None and o["first"]:
                 h[:] = []
             h.append((i, r, wr))
-        o["dep"] = sorted(d)
+        o["free"] = set(j for j in d if o["grp"] and ops[j]["grp"]) | (set(o.get("turn", ())) - d)
+        o["dep"] = sorted(d | o["free"])
 
 
 def label(o):
@@ -537,8 +654,8 @@ def schedule(ops):
     lat = K["lat"]
     pr = [0.0] * n
     for i in range(n - 1, -1, -1):
-        c = min(a[1] for a in ops[i]["alts"].values()) + ops[i]["lat"] + ops[i].get("rest", 0.0)
-        pr[i] = c + max([pr[j] + (0 if ops[i]["grp"] and ops[j]["grp"] else lat) for j in succ[i]], default=0.0)
+        c = min(a[1] for a in ops[i]["alts"].values()) + ops[i]["lat"] + ops[i].get("rest", 0.0) + EXTRA.get(label(ops[i]), 0.0)
+        pr[i] = c + max([pr[j] + (0 if i in ops[j]["free"] else lat) for j in succ[i]], default=0.0)
     for i, o in enumerate(ops):
         pr[i] += o.get("boost", 0.0)
     prv = [pr[i] - (K["vpen"] if len(o["alts"]) > 1 else 0.0) for i, o in enumerate(ops)]
@@ -560,10 +677,12 @@ def schedule(ops):
         pe = prv if e == "V" else pr
         best = max((i for i in c if ready[i] <= s), key=lambda i: (pe[i], -i))
         dur = ops[best]["alts"][e][1]
-        soon = [i for i in c if s < ready[i] < s + min(dur, K["look"]) and pe[i] > pe[best] + K["look2"] * dur]
+        soon = [i for i in c if s < ready[i] < s + min(dur - K["tau"], K["look"]) and pe[i] > pe[best] + K["look2"] * dur]
         if soon:
-            best = max(soon, key=lambda i: (pe[i], -i))
-            s = ready[best]
+            nxt = max(soon, key=lambda i: (pe[i], -i))
+            fit = [i for i in c if ready[i] <= s and s + ops[i]["alts"][e][1] - K["tau"] <= ready[nxt]]
+            best = max(fit, key=lambda i: (pe[i], -i)) if fit else nxt
+            s = max(s, ready[best])
             dur = ops[best]["alts"][e][1]
         for e2 in ops[best]["alts"]:
             pool[e2].discard(best)
@@ -571,7 +690,7 @@ def schedule(ops):
         now[e] = s + dur
         end = s + dur + ops[best]["lat"]
         for j in succ[best]:
-            ready[j] = max(ready[j], end + (0 if ops[best]["grp"] and ops[j]["grp"] else lat))
+            ready[j] = max(ready[j], end + (0 if best in ops[j]["free"] else lat))
             left[j] -= 1
             if not left[j]:
                 for e2 in ops[j]["alts"]:
@@ -591,7 +710,7 @@ def times(ops, order, c):
         for e, l in order.items():
             while head[e] < len(l) and all(j in end for j in ops[l[head[e]]]["dep"]):
                 i = l[head[e]]
-                s = max([now[e]] + [end[j] + lt[j] + (0 if ops[i]["grp"] and ops[j]["grp"] else lat) for j in ops[i]["dep"]])
+                s = max([now[e]] + [end[j] + lt[j] + (0 if j in ops[i]["free"] else lat) for j in ops[i]["dep"]])
                 st[i] = s
                 end[i] = now[e] = s + cost[i][e]
                 head[e] += 1
@@ -607,7 +726,7 @@ def fill(ops, seq, pre, c, rev):
         o = ops[i]
         est = lt[i] if rev else 0.0
         for j in pre[i]:
-            x = en[j] + (0 if o["grp"] and ops[j]["grp"] else lat) + (lt[i] if rev else lt[j])
+            x = en[j] + (0 if j in o["free"] or i in ops[j]["free"] else lat) + (lt[i] if rev else lt[j])
             if x > est:
                 est = x
         best = None
@@ -660,6 +779,122 @@ def polish(ops, order, cs, rounds, seed, noise):
     return best[1]
 
 
+def anneal(ops, order, cs, sweeps, tries, width, heat, lam, seed):
+    n = len(ops)
+    E = "VSPGY"
+    st0 = times(ops, order, cs[0])[0]
+    eng = [0] * n
+    for e, l in order.items():
+        for i in l:
+            eng[i] = E.index(e)
+    seq = sorted(range(n), key=lambda i: (st0[i], i))
+    dset, sset = [set(o["dep"]) for o in ops], [set() for o in ops]
+    for i, d in enumerate(dset):
+        for j in d:
+            sset[j].add(i)
+    alts = [[E.index(e) for e in o["alts"]] for o in ops]
+    pull = [K["pull"] if label(o) in PULL else 1.0 for o in ops]
+    mods = []
+    for cost, lt, lat in cs:
+        pre = [[(j, lt[j] + (0 if j in o["free"] else lat)) for j in o["dep"]] for o in ops]
+        mods.append((pre, [[c.get(e, 0.0) for e in E] for c in cost], lt))
+    x = [seed]
+
+    def rnd(k):
+        x[0] = (x[0] * 1103515245 + 12345) % 2147483648
+        return (x[0] >> 8) % k
+    for sw in range(sweeps):
+        hot = heat * (1 - sw / sweeps) ** 2
+        a = -rnd(width // 2)
+        while a < n - 1:
+            a0, b = max(a, 0), min(n, a + width)
+            ctx = []
+            for (pre, cost, lt), wt in zip(mods, K["wt"]):
+                now, en = [0.0] * 5, [0.0] * n
+                for i in seq[:a0]:
+                    en[i] = now[eng[i]] = max([now[eng[i]]] + [en[j] + w for j, w in pre[i]]) + cost[i][eng[i]]
+                qe, cross = [0.0] * 5, list(lt)
+                for i in reversed(seq[b:]):
+                    q = qe[eng[i]] = cost[i][eng[i]] + max(cross[i], qe[eng[i]])
+                    for j, w in pre[i]:
+                        cross[j] = max(cross[j], q + w)
+                ctx.append((pre, cost, qe, cross, wt, [en, [(now, max([en[i] + cross[i] for i in seq[:a0]], default=0.0), 0.0)], 0.0]))
+
+            def worth(win, lo, limit):
+                tot, new = sum(c[5][2] for c in ctx), []
+                for pre, cost, qe, cross, wt, (en, marks, was) in ctx:
+                    en, marks = list(en), marks[:lo // 16 + 1]
+                    now, top, acc = marks[-1]
+                    now = list(now)
+                    for p in range(lo // 16 * 16, len(win), 16):
+                        for i in win[p:p + 16]:
+                            e = eng[i]
+                            s = now[e]
+                            for j, w in pre[i]:
+                                v = en[j] + w
+                                if v > s:
+                                    s = v
+                            s += cost[i][e]
+                            en[i] = now[e] = s
+                            acc += s * pull[i]
+                            s += cross[i]
+                            if s > top:
+                                top = s
+                        marks.append((list(now), top, acc))
+                    v = (max([top] + [u + v for u, v in zip(now, qe)]) + lam * acc / len(win)) / wt
+                    tot += v - was
+                    new.append([en, marks, v])
+                    if tot > limit + 0.001:
+                        return None, None
+                return tot, new
+
+            def keep(new):
+                for c, s in zip(ctx, new):
+                    c[5][:] = s
+            win = seq[a0:b]
+            m = len(win)
+            cur, new = worth(win, 0, 1e9)
+            keep(new)
+            best = (cur, win, [eng[i] for i in win])
+            for it in range(tries):
+                p = rnd(m)
+                i = win[p]
+                kind, old = rnd(8), eng[i]
+                if kind < 2 and len(alts[i]) > 1:
+                    eng[i] = [e for e in alts[i] if e != old][rnd(len(alts[i]) - 1)]
+                    w2, lo = win, p
+                else:
+                    step, hops, q = -1 if kind & 1 else 1, 1 + (rnd(3) * rnd(3) if rnd(6) else rnd(K["far"])), p
+                    while hops and 0 <= q + step < m:
+                        q += step
+                        hops -= eng[win[q]] == old
+                    mv, tie = {i}, sset if step < 0 else dset
+                    for r in range(p + step, q + step, step):
+                        if not mv.isdisjoint(tie[win[r]]):
+                            mv.add(win[r])
+                    if win[q] in mv:
+                        continue
+                    lo, hi = min(p, q), max(p, q) + 1
+                    yes, no = [j for j in win[lo:hi] if j in mv], [j for j in win[lo:hi] if j not in mv]
+                    w2 = win[:lo] + (yes + no if step < 0 else no + yes) + win[hi:]
+                limit = cur + hot * rnd(1000) / 1000.0
+                w, new = worth(w2, lo, limit)
+                if new and w <= limit:
+                    cur, win = w, w2
+                    keep(new)
+                    if w < best[0]:
+                        best = (w, w2, [eng[j] for j in w2])
+                else:
+                    eng[i] = old
+            seq[a0:b] = best[1]
+            for j, e in zip(best[1], best[2]):
+                eng[j] = e
+            a += width // 2
+        st0 = times(ops, {e: [i for i in seq if eng[i] == q] for q, e in enumerate(E)}, cs[0])[0]
+        seq.sort(key=lambda i: st0[i])
+    return {e: [i for i in seq if eng[i] == q] for q, e in enumerate(E)}
+
+
 def emit(g, T, ops, order):
     queue = {"V": g.vector, "S": g.scalar, "P": g.tensor, "G": g, "Y": g.sync}
     eng, pos, last = {}, {}, {}
@@ -680,7 +915,7 @@ def emit(g, T, ops, order):
                 s = seen[e]
                 ws = []
                 for j in sorted(ops[i]["dep"], key=lambda j: -pos[j]):
-                    if e == "P" and eng[j] == "P":
+                    if j in ops[i]["free"]:
                         continue
                     key = ops[j]["sem"][0] if ops[j]["sem"] else eng[j]
                     if s.get(key, -1) >= pos[j]:
@@ -734,7 +969,7 @@ def plan(g, core, T, topo, rank):
         ops = build(g, core, T, topo, rank)
         cs.insert(0, ([{e: a[1] for e, a in o["alts"].items()} for o in ops], [m["rem"] if "sent" in o else o["lat"] for o in ops], m["lat"]))
     depend(ops)
-    return ops, cs, polish(ops, schedule(ops), cs, K["rounds"], K["seed"], K["noise"])
+    return ops, cs, anneal(ops, polish(ops, schedule(ops), cs, K["rounds"], K["seed"], K["noise"]), cs, *K["anneal"])
 
 
 def rank_program(g, core, T, topo):
@@ -743,9 +978,9 @@ def rank_program(g, core, T, topo):
         return
     if "o" not in _CACHE:
         ops, cs, order = plan(g, core, T, topo, rank)
-        _CACHE["o"] = (order, [o["dep"] for o in ops])
+        _CACHE["o"] = (order, [(o["dep"], o["free"]) for o in ops])
     ops = build(g, core, T, topo, rank)
     order, deps = _CACHE["o"]
     for o, d in zip(ops, deps):
-        o["dep"] = d
+        o["dep"], o["free"] = d
     emit(g, T, ops, order)

from concourse.mybir import AluOpType, ActivationFunctionType
A = AluOpType
F = ActivationFunctionType
W, L, NS, CP = 4096, 1024, 3, 96
BF, F32, I32, U16, H16 = "bfloat16", "float32", "int32", "uint16", "float16"
SP = 32
KS = 2.0 ** -17

_S = {
    "x": (W, BF), "M": (W + 2 * SP, F32), "MK": (W, BF), "CT": (512, BF), "NI": (L, I32),
    "NM": (L + 64 + 2 * SP, F32), "DI": (768, I32), "DW": (768, F32),
    "WI": (8, I32), "TI": (8, I32), "PI": (8, I32), "C": (64, F32), "IC": (144, F32), "GC": (128, F32),
    "RC": (128, F32), "OH": (16, F32), "NOH": (16, F32), "EQ": (8, F32), "E8": (8, F32), "Z1": (128, F32), "Z2": (128, F32), "Z3": (128, F32),
    "Wp": (144, BF), "Wn": (144, BF), "Wk0": (144, BF), "Wk1": (144, BF), "Wk2": (144, BF), "Wk3": (144, BF),
    "RZ": (512, BF), "ZR": (1536, BF), "XR": (2560, BF), "MR": (2560, BF), "Y31": (2560, BF), "Y32": (2560, BF), "SC": (128, BF), "PC": (17, F32), "Z5": (4, F32), "HI": (4, F32), "pq": (8, U16), "sel": (128, BF),
    "yU1": (128, BF), "yU2": (128, BF), "Wm": (144, BF), "Wl": (144, BF),
    "WyA": (64, BF), "WyL": (64, BF), "Ib": (128, BF), "Is": (128, BF), "BLK": (128, BF), "TRb": (128, BF), "DLO": (128, BF), "O16": (128, BF),
    "SEL": (128, BF), "SE2": (128, BF), "K5": (32, BF), "KC": (256, BF), "RSx": (256, BF), "RSn": (256, BF),
    "Dp": (128, BF), "Dn": (128, BF), "Dv": (128, BF), "Lp": (128, BF), "Ln": (128, BF), "Lv": (128, BF),
    "J": (288, BF), "RAa0": (256, BF), "RAa1": (256, BF), "RAl0": (256, BF), "RAl1": (256, BF),
    "RBa": (288, BF), "RBl": (288, BF), "aq": (8, BF), "KX": (8, BF),
    "SLT": (96, BF), "Ob": (8, BF), "PT": (256, BF),
    "q2": (16, I32), "q4": (16, F32), "CLn": (32, BF), "CLp": (32, BF), "cT": (16, U16),
    "GAr": (96, BF), "LVr": (96, BF), "LV0": (256, BF), "LV1": (256, BF), "LV2": (256, BF), "ZZ": (128, BF),
    "TH": (16, H16), "Ab": (8, F32), "L0": (32, I32), "GA": (6 * 272, BF), "YA": (256, F32),
    "ny0": (256, BF), "ny1": (256, BF), "NO": (256, F32), "DF": (256, I32), "TT": (256, F32), "NW": (256, F32), "YO": (L, F32),
    "SN": (256, F32), "kn1": (16, I32), "kn2": (16, I32), "kn": (16, U16),
    "RD": (16, BF), "PRE": (32, BF), "NRC": (16, BF), "SL": (16, U16), "ON": (32, BF), "MB": (W + 2 * SP, BF),
}
for _k in ("0", "1", "r"):
    _n = 1536 if _k == "r" else 4096
    _S.update({"mn" + _k: (_n, BF), "G" + _k: (_n, BF), "co" + _k: (256, U16), "SX" + _k: (256, F32),
               "p1" + _k: (16, I32), "p2" + _k: (16, I32), "po" + _k: (16, U16),
               "u1" + _k: (32, I32), "u2" + _k: (32, I32), "u3" + _k: (32, F32), "u4" + _k: (32, F32), "lo" + _k: (32, U16)})
for _k in ("a", "b", "l"):
    _S.update({"DS0" + _k: (256, F32), "DS1" + _k: (256, F32), "SD0" + _k: (256, F32), "SD1" + _k: (256, F32), "OF" + _k: (16, U16)})
for _t in range(NS):
    _S.update({"yr%d" % _t: (4096, BF), "yT%d" % _t: (256, BF), "box%d" % _t: (784, BF), "LB%d" % _t: (112, BF)})
_S.update({"yr1h": (4096, BF), "yP": (256, BF), "nyN": (256, BF), "yrr": (1536, BF), "GFb": (256, F32),
           "GFa": (256, F32), "cN": (16, U16), "Z4": (16, F32), "yQ1": (128, BF), "yQ2": (128, BF)})
_OWN = ("WI", "TI", "YA", "LB0", "LB1", "LB2")
_AT, SCRATCH = {}, {}
for _k, (_n, _d) in _S.items():
    if _n > 288 or _k in _OWN:
        SCRATCH[_k] = ("sbuf", [128, _n], _d)
        _AT[_k] = (_k, 0)
    else:
        _o = SCRATCH.get("pool_" + _d, (0, [0, 0]))[1][1]
        SCRATCH["pool_" + _d] = ("sbuf", [128, _o + (_n + 31) // 32 * 32], _d)
        _AT[_k] = ("pool_" + _d, _o)
_PS = ("pK0", "pK1", "pU", "pA", "pD", "pX", "pS", "pY")
SCRATCH.update({k: ("psum", [128, 512], F32) for k in _PS})
SEMAPHORES = ["V", "S", "P", "G", "sent", "arr0", "arr1", "arr2"] + ["d%d" % i for i in range(12)]

K = {"cyc": 1.0, "g": 1.3, "sc": 3.2, "pe": 0.5, "lat": 100.0, "fix": 30.0, "look": 250.0, "look2": 1.0, "tau": 0.0, "rest": 0.7, "ramp": 0, "vpen": 20000.0,
     "ch0": ([4, 4, 4, 4], [4, 4, 4, 2, 2]), "ch1": ([4, 4, 2, 2, 2, 1, 1],) * 2, "chr": ([8, 4, 4],) * 2, "spr": "VS",
     "ng": 11, "far": 30, "back": 2, "cutl": [96], "parts": [(160, 256), (0, 160)], "soon": 20000.0}
K.update({"wt": (120e3, 110e3, 150e3), "rounds": 30, "seed": 1, "noise": 1000.0, "anneal": (16, 1350, 120, 0.0015, 0.05, 4),
          "ramp": 1, "cutl": [128], "parts": [(128, 256), (0, 128)],
          "soon": 10000.0, "chr": ([4, 4, 4, 2, 2],) * 2,
          "tau": 100.0, "look": 450.0, "vpen": 2000.0, "rest": 1.0,
          "ch0": ([2] * 8, [4, 4, 2, 2, 2, 2]), "ch1": ([2] * 7 + [1, 1], [4, 4, 2, 2, 2, 1, 1])})
MODS = [dict(cyc=.9, g=1.3, sc=3.2, pe=.45, lat=200., rem=3200.), dict(cyc=.83, g=1.0, sc=2.0, pe=.42, lat=170., rem=2800.),
        dict(cyc=1.25, g=2.3, sc=6., pe=.65, lat=260., rem=4000.)]
SILU1 = 1.2784645427610738
EXTRA = {}
PULL = ("NM<NW", "co0<NM", "XR<x", "MR<XR", "mn0<x")
K["pull"] = 10.0
_CACHE = {}


def _clash(a, b):
    if a[1] != b[1] or a[2] >= b[3] or b[2] >= a[3]:
        return False
    if a[4] > 1 and a[4] == b[4] and (a[2] - b[2]) % a[4]:
        return False
    return True


def build(g, core, T, topo, rank):
    ops = []
    cyc = K["cyc"]
    top = slice(0, 8)

    def R(name, a=0, b=None, s=1, parts=None):
        real, o = _AT.get(name, (name, 0))
        b = _S[name][0] if b is None else b
        ps = slice(None) if parts is None else parts
        return (T[real][ps, o + a:o + b:s] if s > 1 else T[real][ps, o + a:o + b], name, a, b, s)

    def cnt(r):
        return (r[3] - r[2] + r[4] - 1) // r[4]

    def two(*rs):
        return all(r[1] in _S and _S[r[1]][1] in (BF, H16, U16) for r in rs)

    def add(alts, reads, writes, **kw):
        o = {"alts": alts, "r": [r for r in reads if isinstance(r, tuple)], "w": list(writes), "grp": None, "sem": None, "lat": 0.0}
        o.update(kw)
        ops.append(o)

    def ap(s):
        return s[0] if isinstance(s, tuple) else s

    def vcost(n, half):
        return K["fix"] + max(64, n * (0.5 if half else 1.0)) * cyc

    def gcost(n, e):
        return (50 if e == "V" else 65) + n * K["g"]

    def ts(out, in0, s1, s2, op0, op1=None, off=None):
        def f(q):
            i = in0[0].indirect(off[0]) if off else in0[0]
            if op1 is None:
                return q.tensor_scalar(out[0], i, ap(s1), None, op0)
            return q.tensor_scalar(out[0], i, ap(s1), ap(s2), op0, op1)
        add({"V": (f, gcost(cnt(out), "V") if off else vcost(cnt(out), two(out, in0)))}, [in0, s1, s2, off], [out])

    def tt(out, in0, in1, op, off=None, scat=None):
        def f(q):
            return q.tensor_tensor(out[0].indirect(scat[0]) if scat else out[0], in0[0].indirect(off[0]) if off else in0[0], in1[0], op)
        if scat:
            c = 50 + cnt(in0) * K["sc"]
        elif off:
            c = gcost(cnt(out), "V")
        else:
            c = vcost(cnt(out) * (1 if in0[1] in _PS or in1[1] in _PS else 2), False)
        add({"V": (f, c)}, [in0, in1, off, scat], [out])

    def cp(out, in_, scat=None):
        def f(q):
            return q.tensor_copy(out[0].indirect(scat[0]) if scat else out[0], in_[0])
        add({"V": (f, 50 + cnt(in_) * K["sc"] if scat else vcost(cnt(out), two(out, in_)))}, [in_, scat], [out])

    def ms(out, v):
        alts = {"V": (lambda q: q.memset(out[0], v), vcost(cnt(out), two(out)))}
        if v == int(v):
            alts["G"] = (lambda q: q.iota(out[0], [[0, cnt(out)]], int(v), 0, allow_small_or_imprecise_dtypes=True), 130 + 2 * cnt(out) * cyc)
        add(alts, [], [out])

    def scan(out, d0, d1, op0, op1):
        add({"V": (lambda q: q.tensor_tensor_scan(out[0], d0[0], d1[0], 0.0, op0, op1), vcost(cnt(out), two(out, d0, d1)))}, [d0, d1], [out])

    def act(out, in_, func=F.Identity, scale=1.0, bias=0.0, off=None, scat=None):
        if scat:
            add({"S": (lambda q: q.activation(out[0].indirect(scat[0]), in_[0], func), 65 + cnt(in_) * K["sc"])}, [in_, scat], [out])
            return

        def f(q):
            return q.activation(out[0], in_[0].indirect(off[0]) if off else in_[0], func, bias=ap(bias), scale=ap(scale))
        add({"S": (f, gcost(cnt(out), "S") if off else vcost(cnt(out), False))}, [in_, scale, bias, off], [out])

    def flex(out, in_, engs, scale=1.0, bias=None, off=None):
        n = cnt(out)
        alts = {}

        def src():
            return in_[0].indirect(off[0]) if off else in_[0]
        if "V" in engs:
            def fv(q):
                if bias is not None:
                    return q.tensor_scalar(out[0], src(), ap(scale), ap(bias), A.mult, A.add)
                if scale != 1.0:
                    return q.tensor_scalar(out[0], src(), ap(scale), None, A.mult)
                return q.tensor_copy(out[0], src())
            alts["V"] = (fv, gcost(n, "V") if off else vcost(n, two(out, in_)))
        if "S" in engs:
            alts["S"] = (lambda q: q.activation(out[0], src(), F.Identity, bias=0.0 if bias is None else ap(bias), scale=ap(scale)),
                         gcost(n, "S") if off else vcost(n, False))
        if "G" in engs:
            alts["G"] = (lambda q: q.affine_select(out[0], in_[0], [[0, n]], A.is_ge, 0.0, 0, 0), 170 + 2 * n * cyc)
        add(alts, [in_, scale, bias, off], [out])

    def square(out, in_):
        n = cnt(out)
        add({"V": (lambda q: q.tensor_tensor(out[0], in_[0], in_[0], A.mult), vcost(2 * n, False)),
             "S": (lambda q: q.activation(out[0], in_[0], F.Square), vcost(n, False))}, [in_], [out])

    def iota(out, pat, base, cm):
        fl = _S[out[1]][1] != I32
        add({"G": (lambda q: q.iota(out[0], pat, base, cm, allow_small_or_imprecise_dtypes=True) if fl else q.iota(out[0], pat, base, cm),
                   130 + 2 * cnt(out) * cyc)}, [], [out])

    turns = {}

    def turn(k):
        if k in turns:
            ops[-1]["turn"] = [turns[k]]
        turns[k] = len(ops) - 1

    gid = [0]

    def group():
        gid[0] += 1
        return [gid[0], True]

    def mm(gr, out, lhsT, rhs):
        mms(gr, [(out, lhsT, rhs)])

    def mms(gr, calls):
        first = gr[1]
        gr[1] = False

        def f(q, stop):
            for j, (out, lhsT, rhs) in enumerate(calls):
                ins = q.matmul(out[0], lhsT[0], rhs[0], first and not j, stop and j == len(calls) - 1)
            return ins
        add({"P": (f, sum(max(64, cnt(c[0])) for c in calls) * K["pe"])},
            [c[j] for j in (1, 2) for c in calls], [c[0] for c in calls], grp=gr[0], first=first)

    nd = [0]

    def dma(e, pairs, reads, writes, ns, boost=0.0):
        s = "d%d" % nd[0]
        nd[0] += 1

        def f(q):
            for o, i in pairs:
                q.dma_start(o, i).then_inc(T.sem[s], 16)
        add({e: (f, (300.0 if e == "G" else 60.0) * len(pairs))}, reads, writes, sem=(s, 16 * len(pairs)), lat=ns, boost=boost)

    def sl(name, j):
        return R(name, 15 - j, 143 - j)

    cols = {}

    def col(name, parts=None):
        j = cols.setdefault(name, len(cols))
        return R("C", j, j + 1, parts=parts)

    def oh(j):
        return R("OH", j, j + 1)

    B0 = W - 256
    dma("Y", [(T.WI[:, 0:1], T.wt[:])], [], [R("WI")], 1900, 6e6)
    dma("Y", [(T.x[:, B0:W], T.xc[:, B0:W])], [], [R("x", B0, W)], 2200, 5e6)
    dma("Y", [(T.MK[0:8, :], T.mk[:])], [], [R("MK")], 2400, 4e6)
    dma("Y", [(T.NI[:], T.oc[:])], [], [R("NI")], 4200, 3e6)
    dma("Y", [(T.x[:, 0:B0], T.xc[:, 0:B0])], [], [R("x", 0, B0)], 6500, 2e6)
    iota(R("PI", 0, 1), [[0, 1]], 0, 1)
    iota(R("IC"), [[1, 144]], 0, 0)
    ts(R("PI", 1, 2), R("PI", 0, 1), 15, None, A.bitwise_and)
    ts(R("PI", 2, 3), R("PI", 0, 1), 112, None, A.bitwise_and)
    p, r, g16 = col("p"), col("r"), col("g16")
    cp(R("C", 0, 3), R("PI", 0, 3))
    ts(col("last"), R("PI", 2, 3), 15.0, None, A.add)
    ts(col("w"), R("WI", 0, 1), 1.0 / W, None, A.mult)
    ts(col("-w"), R("WI", 0, 1), -1.0 / W, None, A.mult)

    def slide(name, c, n=144, at="last"):
        ts(R(name, 0, n), R("IC", 0, n), col(at), c, A.is_equal, A.mult)

    def mix(name, a, v, b):
        flex(col(name), a, "VS", scale=v, bias=b)
        return col(name)
    slide("Wp", col("w"))
    slide("Wn", col("-w"))
    ts(R("OH"), R("IC", 0, 16), r, None, A.is_equal)
    ts(R("Ib"), R("IC", 0, 128), p, None, A.is_equal)
    ms(R("K5"), 592.0 / W)
    flex(col("16r"), r, "VS", scale=16.0)
    iota(R("Z4"), [[1, 2], [2, 8]], 0, 0)
    ts(R("cT"), R("Z4"), col("16r"), None, A.add)
    ts(R("PI", 5, 6), R("PI", 1, 2), 1, None, A.bitwise_and)
    ts(R("PI", 6, 7), R("PI", 1, 2), 14, None, A.bitwise_and)
    ts(col("8b"), R("PI", 6, 7), 8.0, None, A.mult)
    ts(col("at"), R("PI", 5, 6), 128.0, col("8b"), A.mult, A.add)
    ts(R("cN"), R("IC", 0, 16), col("at"), None, A.add)
    mix("pc1", col("at"), 16.0, 255.0)
    keep = mix("keep", oh(1), 1.0, oh(2))
    flex(R("E8"), R("IC", 0, 8), "VS", scale=oh(2), bias=mix("dig", keep, 64.0, oh(3)))
    for j in range(4):
        flex(R("CT", 64 * j, 64 * j + 64), R("IC", 0, 64), "VS", scale=oh(1), bias=R("E8", j, j + 1))
    flex(R("EQ"), R("IC", 0, 8, ), "VS", scale=mix("8hi", oh(2), 8.0, 0.0))
    flex(R("CT", 256, 512), R("CT", 0, 256), "VS", bias=mix("4hi", oh(2), 4.0, 0.0))
    iota(R("Z2", parts=top), [[100, 8], [0, 2], [1, 8]], 0, -100)
    ts(R("SEL", parts=top), R("Z2", parts=top), 0.0, None, A.is_equal)
    for j, bank in enumerate(("pK1", "pA", "pD", "pX", "pS", "pY", "pK0", "pK1")):
        gr = group()
        mm(gr, R(bank, 0, 512), R("Ib"), R("CT"))
        mm(gr, R(bank, 0, 512), R("SEL", parts=top), R("MK", 512 * j, 512 * j + 512, parts=top))
        flex(R("M", SP + 512 * j, SP + 512 * j + 512), R(bank, 0, 512), "VS", bias=R("EQ", j, j + 1))
    dma("Y", [(T.TI[0:8, 0:1], T.th[:])], [], [R("TI")], 2500)
    dma("Y", [(T.DI[j:128:16, :], T.dl[:]) for j in range(16)], [R("x")], [R("DI")], 3500)
    slide("Wk0", 512.0 * KS)
    slide("Wm", mix("m", oh(8), KS, oh(0)))
    ts(R("Is"), R("IC", 0, 128), p, KS, A.is_equal, A.mult)
    iota(R("KC"), [[-32, 16], [0, 16]], 480, 0)
    for nm, a, b in (("RSx", 2.0 * KS, -1e4), ("RSn", -2.0 * KS, 1e4)):
        ms(R(nm), a)
        ms(R(nm, 0, 256, 16), b)
    flex(R("PC"), R("IC", 0, 17), "VS", scale=col("16r"), bias=255.0)
    mix("silu", keep, -SILU1, SILU1)
    ts(col("dead"), oh(3), oh(0), 8192.0, A.subtract, A.mult)
    slide("Wl", col("dead"))
    mix("ya", g16, 0.375, 5.0)
    slide("WyA", mix("slot", oh(3), SP - 4160.0, mix("num", oh(2), 64.0, oh(1))), 64, "ya")
    slide("WyL", mix("live", col("dead"), -1.0, 0.0), 64, "ya")
    iota(R("GC"), [[16, 8], [0, 16]], 0, 0)
    iota(R("RC"), [[0, 8], [1, 16]], 0, 0)
    ts(R("BLK"), R("GC"), g16, None, A.is_equal)
    for k, c in (("D", "slot"), ("L", "dead")):
        flex(R(k + "v"), R("BLK"), "VS", scale=col(c))
        flex(R(k + "p"), R(k + "v"), "VS", scale=2.0 ** 14)
        flex(R(k + "n"), R(k + "v"), "VS", scale=-2.0 ** 14)
    iota(R("J"), [[0, 9], [1, 32]], 0, 0)
    flex(col("15-r"), r, "VS", scale=-1.0, bias=15.0)
    for k, c in (("a", r), ("l", col("15-r"))):
        ts(R("RB" + k), R("J"), c, 1e9, A.is_equal, A.mult)
        for h in (0, 1):
            o = 16 * (h if k == "a" else 1 - h)
            ra = "RA%s%d" % (k, h)
            ts(R(ra), R("J", o, o + 256), c, None, A.not_equal)
            flex(R(ra, 31, 256, 32), R(ra, 31, 256, 32), "VS", scale=2.0 ** -14)
    ms(R("ZZ"), 0.0)
    iota(R("Z5"), [[W - L - 64, 2], [16, 2]], L + 64 + SP, 0)
    flex(R("HI"), R("Z5"), "VS", bias=r)
    mix("r16", r, 1.0, 16.0)
    iota(R("SLT"), [[-1, 6], [-6, 16]], CP, 0)
    iota(R("RZ"), [[0, 32], [128, 16]], 0, 0)
    for a in range(0, 1536, 512):
        ms(R("ZR", a, a + 512), 0.0)
    flex(R("Ob", 0, 1), oh(3), "VS")
    flex(R("NOH"), R("OH"), "VS", scale=-1.0, bias=1.0)
    ts(R("Z1"), R("RC"), r, None, A.is_ge)
    tt(R("TRb"), R("Z1"), R("BLK"), A.mult)
    flex(col("-r"), r, "VS", scale=-1.0)
    flex(R("DLO"), R("Ib"), "VS", scale=col("-r"))
    flex(col("r-1"), r, "VS", bias=-1.0)
    ms(R("O16"), -1.0 / 16)
    ms(R("KX", 0, 1), 8.0 * CP - 12288.0)
    ms(R("ON"), 1.0)
    ms(R("PRE", 0, 1), 0.0)
    iota(R("CLn", 0, 16), [[-16, 16]], -256, 0)
    iota(R("CLp", 0, 16), [[16, 16]], 256, 0)
    iota(R("Z3", 0, 128, parts=top), [[1, 8], [0, 16]], 0, -1)
    ts(R("SE2", parts=top), R("Z3", 0, 128, parts=top), 0.0, 512.0 * KS, A.is_equal, A.mult)
    ts(col("th", top), R("TI", 0, 1, parts=top), -1.0, None, A.add)
    ts(R("TH", parts=top), R("ON", 0, 16, parts=top), col("th", top), None, A.mult)
    for t in range(NS):
        ms(R("box%d" % t, 0, 112), 0.0)
        ts(R("DW", 256 * t, 256 * t + 256), R("DI", 256 * t, 256 * t + 256), 64.0, None, A.add)
    for j in range(4):
        ts(R("NM", SP + 256 * j, SP + 256 * j + 256), R("NI", 256 * j, 256 * j + 256), 64.0, None, A.add)
    names = R("NM", SP, SP + L)
    AB0 = 312 - 0.40625

    def place(k, pu, ab, a=0, out=None):
        u1, u2, u3, u4 = (R("u%d%s" % (j, k), a, a + cnt(pu)) for j in (1, 2, 3, 4))
        ts(u1, pu, -0.5 + 2.0 ** -13 - 592.0 / W, None, A.add)
        tt(u3, pu, u1, A.subtract)
        square(u4, u3)
        ts(u1, u4, 2.0 ** 19, ab, A.mult, A.add)
        ts(out or u2, u1, 1023, None, A.bitwise_and)
        if not out:
            cp(R("lo" + k, a, a + cnt(pu)), u2)

    def umm(o, rhs, wn="Wn"):
        gr = group()
        mm(gr, o, R("Ib"), R("K5", 0, cnt(o)))
        mms(gr, [(o, sl(wn, j), rhs(j)) for j in range(16)])
        return o

    def columns(k, n, t, nm, a=0):
        up = 0 if nm[1] == "NI" else 4 * (15 - t)
        ts(R("co" + k, 16 * a, 16 * (a + n)), nm, (15 - t) / 16.0, -15.0 / 32 - up, A.mult, A.add, off=R("lo" + k, a, a + n))

    def spread(yr, h, src, e, scale=1.0, plus=None, ng=0):
        for k in range(16):
            out = R(yr, 2048 * h + k, 2048 * h + 2048, 16)
            if k < ng:
                flex(out, plus, "G")
            else:
                flex(out, src, e, scale=scale)

    def scores(k, n, B, yr, pk, chunks, c0=0, ramp=None):
        gr = group()
        w, e0 = 16 * n, 256 * c0
        mm(gr, R(pk, 0, w), R("Is"), R("KC", 0, w))
        if ramp:
            for a in range(0, 16, 2):
                j, e = a // 4, 5 * w * (a % 4)
                act(R("XR", e + j, e + 10 * w, 5), R("x", 0, B), scale=2.0 ** j, bias=128.0 * 2 ** j,
                    off=R("co" + k, 16 * c0 + n * a, 16 * c0 + n * (a + 2)))
            for e in (0, 1280):
                scan(R("MR", e, e + 1280), R("XR", e, e + 1280), R(ramp, e, e + 1280), A.max, A.min)
                mms(gr, [(R(pk, 0, w), sl("Wk%d" % (a // 4), a), R("MR", 5 * w * (a % 4) + a // 4, 5 * w * (a % 4 + 1), 5))
                         for a in range(16) if a % 4 // 2 == e // 1280])
        for nm, wn, chs in (("mn", "Wk0", [] if ramp else chunks[0]), ("G", "Wm", chunks[1])):
            a = 0
            for ch in chs:
                o = R("co" + k, 16 * c0 + n * a, 16 * c0 + n * (a + ch))
                out = R(nm + k, e0 + w * a, e0 + w * (a + ch))
                if nm == "mn":
                    tt(out, R("x", 0, B), R(yr, out[2], out[3]), A.min, off=o)
                    turn(k == "r")
                else:
                    flex(out, R("M", SP, SP + B), "VS", off=o)
                    ops[-1]["rest"] = (16 - a - ch) * w * K["g"] * K["rest"]
                mms(gr, [(R(pk, 0, w), sl(wn, 2 * (j % 8) + j // 8 if k == "1" else j), R(nm + k, e0 + w * j, e0 + w * j + w))
                         for j in range(a, a + ch)])
                a += ch

    def best(k, n, pk, pc, c0=0):
        w, e0 = 16 * n, 16 * c0
        scan(R("SX" + k, e0, e0 + w), R("RSx", 0, w), R(pk, 0, w), A.add, A.max)
        p1, p2 = R("p1" + k, c0, c0 + n), R("p2" + k, c0, c0 + n)
        ts(p1, R("SX" + k, e0 + 15, e0 + w, 16), 1 / KS, None, A.mult)
        ts(p2, p1, 1, 255, A.arith_shift_right, A.bitwise_and)
        ts(R("po" + k, c0, c0 + n), p2, -1.0, pc, A.mult, A.add)

    def run(name, f, d, n):
        if d > 0:
            return R(name, f, f + d * (n - 1) + 1, d)
        real, o = _AT[name]
        e = o + f + d * n
        return (T[real][:, o + f:e if e >= 0 else None:d], name, f + d * (n - 1), f + 1, -d)

    def plain(name, f, w):
        return [(0, 1, w, name, f, 1)], (name, f + 31, 32)

    def single(k, tab, w, dig, lv, pd, a=0, cut=[]):
        gr = group()
        for c, (runs, ends) in (("L", lv), ("D", dig)):
            calls = [(R(pd, 0, w), R("Lp"), R("ZZ", 0, w))] if c == "L" and len(runs) > 1 else []
            for o, s, n, nm, f, d in runs:
                calls.append((R(pd, o, o + s * (n - 1) + 1, s), R(c + "p"), run(nm, f, d, n)))
            for o, s, n, nm, f, d in runs:
                if o == 0:
                    o, n, f = s, n - 1, f + d
                calls.append((R(pd, o - 1, o + s * (n - 1), s), R(c + "n"), run(nm, f, d, n)))
            mms(gr, calls)
        mms(group(), [(R(pd, 31, w, 32), R(c + "v"), run(*ends, w // 32)) for c, (runs, ends) in (("L", lv), ("D", dig))])
        for h, u, v in [(h, u, v) for u, v in zip([0] + cut, cut + [w]) for h in (0, 1)]:
            o = u + 16 * (h if tab == "a" else 1 - h)
            ds, sd = R("DS%d%s" % (h, k), a + o, a + v), "SD%d%s" % (h, k)
            scan(ds, R("RA%s%d" % (tab, h), o, v), R(pd, o, v), A.mult, A.add)
            act(ds, ds, F.Abs)
            scan(R(sd, a + o, a + v), R("RB" + tab, 2 * o - u, o + v - u), ds, A.add, A.min)
            ts(R("OF" + k, (a + u) // 16 + h, (a + v) // 16, 2), R(sd, a + u + 31, a + v, 32), col("r16") if h else r,
               R("HI", h + 2 * (tab == "a"), h + 2 * (tab == "a") + 1),
               A.max, A.min)

    def winners(k, n, ga, lv, s, pd, c0=0, whole=True):
        w, e0 = 16 * n, 16 * c0
        act(ga, R("G" + k, 256 * c0, 256 * (c0 + n)), off=R("po" + k, c0, c0 + n))
        if whole:
            flex(R("GF" + s, e0, e0 + w), ga, "SV", scale=col("keep"), bias=col("silu"))
        single(s, "a", w, plain(ga[1], ga[2], w), lv, pd, e0)

    def mark(n, s):
        for j in range(0, n, 2):
            act(R("M"), R("GF" + s, 16 * j, 16 * j + 32), F.Silu, scat=R("OF" + s, j, j + 2))

    early = len(ops)
    for t in range(NS):
        B = W - 256 * (t + 1)
        act(R("yT%d" % t), R("x", B, B + 256), off=R("cT"))
        for h in (0, 1):
            o = 16 * max(t - 1, 0) + 8 * h
            umm(R("pS" if t else "pU", o, o + 8), lambda j: R("x", B + 2 * j + h, B + 256, 32), "Wp")
        if t == 0:
            place("0", R("pU", 0, 16), AB0)
        spread("yr%d" % t, 0, R("x", B, B + 256, 2), "G" if t else "VSG")
        if not (t and K["ramp"]):
            spread("yr%d" % t, 1, R("x", B + 1, B + 256, 2), "G" if t else "VSG")
        else:
            for j in range(4):
                flex(R("yQ%d" % t, 32 * j, 32 * j + 32), R("x", B + 64 * j + 1, B + 64 * j + 64, 2), "VS", scale=2.0 ** j, bias=128.0 * 2 ** j)
            flex(R("yU%d" % t), R("yT%d" % t, 128, 256), "VS", bias=128.0)
            ms(R("Y3%d" % t, 4, 2560, 5), 0.0)
            spread("yr%d" % t, 1, R("yQ%d" % t), "G")
            for j in range(4):
                flex(R("Y3%d" % t, j, 2560, 5), R("yr%d" % t, 2048 + 512 * j, 2560 + 512 * j), "G")
    for o in ops[early:]:
        if list(o["alts"]) == ["G"] or o["w"][0][1][:2] == "yQ":
            o["boost"] = K["soon"]
    if K["ramp"]:
        ms(R("XR", 4, 2560, 5), 0.0)
        for j in (1, 2, 3):
            flex(R("Wk%d" % j), R("Wk0"), "VS", scale=0.5 ** j)
        for j in range(4):
            ms(R("SC", 4 * j, 4 * j + 4), 0.5 ** j)
        for a in (16, 32, 64):
            flex(R("SC", a, 2 * a), R("SC", 0, a), "VSG")
        ts(R("PI", 3, 4), R("PI", 1, 2), 3, None, A.bitwise_and)
        ts(R("PI", 4, 5), R("PI", 1, 2), 2, None, A.arith_shift_right)
        ts(col("q3"), R("PI", 3, 4), 640.0, 1275.0, A.mult, A.add)
        ts(col("pq"), R("PI", 4, 5), col("q3"), None, A.add)
    place("r", R("pS", 0, 32), AB0, out=R("L0"))
    gy = group()
    py = R("pY", 0, 256, parts=slice(0, 48))
    N = len(T.cores)
    for t in range(NS):
        B = W - 256 * (t + 1)
        ab = AB0 if t == 0 else R("Ab", t, t + 1)
        lv = "LV%d" % t
        flex(R(lv, 0, 256), R("M", SP + B, SP + B + 256), "VS")
        if t:
            flex(ab, R("LB%d" % (t - 1), 14, 15), "VS", bias=AB0)
        else:
            columns("0", 16, t, R("NI"))
        for h, pk, pd in ((0, "pK0", "pD"), (1, "pX", "pA")):
            e = 128 * h
            ramp = K["ramp"] and t and h and "Y3%d" % t
            scores("0", 8, B, "yr%d" % t, pk, K["ch0"], 8 * h, ramp)
            best("0", 8, pk, R("PC", 8, 9), 8 * h)
            if ramp:
                ts(R("pq"), R("p20", 8, 16), -5.0, col("pq"), A.mult, A.add)
                tt(R("sel"), R("MR"), R("SC"), A.mult, off=R("pq"))
                tt(R("ny0", e, e + 128), R("sel"), R("yU%d" % t), A.subtract)
            else:
                tt(R("ny0", e, e + 128), R("mn0", 16 * e, 16 * e + 2048), R("yT%d" % t, e, e + 128), A.subtract, off=R("po0", 8 * h, 8 * h + 8))
            place("1", umm(R("pU", 8 * h, 8 * h + 8), lambda j: R("ny0", e + j, e + 128, 16)), ab, 8 * h)
            columns("1", 8, t, names if t else R("NI"), 8 * h)
            winners("0", 8, R("GA", 544 * t + 136 * h, 544 * t + 136 * h + 128),
                    ([(16 * b, 1, 16, lv, 2 * b + h, 16) for b in range(8)], (lv, 242 + h, 4)), "a", pd, 8 * h)
        flex(R("yP", 128, 256), R("ny0", 128, 256), "VS", scale=-1.0)
        act(R("nyN"), R("ny0"), off=R("cN"))
        mark(16, "a")
        spread("yr1h", 0, R("ny0", 0, 128), "VS", -1.0)
        spread("yr1h", 1, R("ny0", 128, 256), "VS", -1.0, R("yP", 128, 256), K["ng"])
        scores("1", 16, B, "yr1h", "pK1", K["ch1"])
        act(R("NO"), names, off=R("lo1", 0, 16))
        act(R("PT"), R("M", SP, SP + L), off=R("lo1", 0, 16))
        for a, b in K["parts"]:
            tt(R("DF", a, b), R("NO"), R("DW", 256 * t + a, 256 * t + b), A.subtract, off=R("cN", a // 16, b // 16))
        single("l", "l", 256, ([(15 - 2 * (j % 8) - j // 8, 16, 16, "PT", 16 * j + 15, -1) for j in range(16)], ("PT", 14, -2)),
               ([(0, 1, 256, lv, 255, -1)], (lv, 224, -32)), "pX", cut=K["cutl"])
        best("1", 16, "pK1", col("pc1"))
        act(R("ny1"), R("mn1"), off=R("po1"))
        box, lb = "box%d" % t, "LB%d" % t
        gr = group()
        mm(gr, R("pS", 0, 16), R("SE2", parts=top), R("TH", parts=top))
        mms(gr, [(R("pS", 0, 16), sl("Wl", j), R(lv, j, 256, 16)) for j in range(16)])
        mms(gr, [(R("pS", 0, 16), sl("Wk0", 2 * (j % 8) + j // 8), R("ny0", 16 * j, 16 * j + 16)) for j in range(16)])
        ts(R("q2"), R("p11", 0, 16), 1, None, A.bitwise_and)
        tt(R("q4"), R("SX1", 15, 256, 16), R("pS", 0, 16), A.add)
        tt(R("RD"), R("q2"), R("q4"), A.is_gt)
        scan(R("PRE", 1, 17), R("ON", 0, 16), R("RD"), A.mult, A.add)
        tt(R("NRC"), R("RD"), R("CLn", 0, 16), A.mult)
        gr = group()
        mm(gr, R("pS", 32, 48), R("Ib"), R("CLp", 0, 16))
        mms(gr, [(R("pS", 32, 48), R("TRb"), R("RD")), (R("pS", 32, 48), R("DLO"), R("RD"))])
        mm(gr, R("pS", 32, 48), R("Ib"), R("NRC"))
        mm(gr, R("pS", 32, 48), R("BLK"), R("PRE", 0, 16))
        ts(R("SL"), R("pS", 32, 48), col("r-1"), None, A.add)
        mm(group(), R("pK0", 0, 1), R("BLK"), R("PRE", 16, 17))
        act(R(box, 15, 16), R("pK0", 0, 1), F.Relu, scale=-1.0, bias=float(CP))
        if t < NS - 1:
            gr = group()
            mm(gr, R("pK0", 1, 2), R("Ib"), R("KX", 0, 1))
            mm(gr, R("pK0", 1, 2), R("O16"), R(box, 15, 16))
            act(R("aq", 0, 1), R("pK0", 1, 2), scale=-1.0, bias=31.5)
            act(R(box, 14, 15), R("pK0", 1, 2), bias=R("aq", 0, 1))
        tt(R(box, 16, 784), R("ny1"), R("nyN"), A.add, scat=R("SL"))
        dst = T.cores[(rank + 1 + t % (N - 1)) % N]
        rid, pid, _se = topo.addr(dst)

        def put(q, box=box, lb=lb, t=t, dst=dst, rid=rid, pid=pid):
            q.remote_dma(T[lb][:], T[box][:, 0:112], T.sem["arr%d" % t], T.sem.sent, pid, rid, topo.mask(core, dst))
        ne = len(topo.engines(core, dst))
        add({"G": (put, 300.0)}, [R(box, 0, 112)], [R(lb)], sem=("arr%d" % t, ne), lat=2800.0, sent=ne)
        scan(R("SN"), R("RSn"), R("pK1", 0, 256), A.add, A.min)
        ts(R("kn1"), R("SN", 15, 256, 16), 1 / KS, 30.0, A.mult, A.add)
        ts(R("kn2"), R("kn1"), 1, 15, A.arith_shift_right, A.bitwise_and)
        cp(R("kn"), R("kn2"))
        for a, b in K["parts"]:
            tt(R("TT", a, b), R("NOH"), R("DF", a, b), A.mult, off=R("kn", a // 16, b // 16))
            tt(R("NW", a, b), R("TT", a, b), R("DW", 256 * t + a, 256 * t + b), A.add)
        for j in range(8):
            a = 224 - 32 * j
            act(R("NM"), R("NW", a, a + 32), F.Silu, scat=R("OFl", 2 * j, 2 * j + 2))
        ga1 = R("GA", 544 * t + 272, 544 * t + 528)
        winners("1", 16, ga1, plain(lv, 0, 256), "b", "pA")
        mark(16, "b")
        for j in (2 * t, 2 * t + 1):
            mm(gy, py, R("WyL", 5 - j, 53 - j), R(lv, 0, 256))
        mm(gy, py, R("WyA", 4 - 2 * t, 52 - 2 * t), ga1)
        for b in range(0, 32, 4):
            mms(gy, [(R("pY", 16 * (a // 2) + a % 2, 16 * (a // 2) + 16, 2, parts=slice(0, 48)), R("WyA", 5 - 2 * t, 53 - 2 * t),
                      R("GA", 544 * t + 136 * (a % 2) + a // 2, 544 * t + 136 * (a % 2) + 128, 16)) for a in range(b, b + 4)])
        if t < NS - 1:
            ts(R("lo0", 0, 16), R("L0", 16 * t, 16 * t + 16), R(lb, 14, 15), None, A.add)
            flex(R("NM", SP + L, SP + L + 64), R("NM", SP, SP + 64), "VS")
            columns("0", 16, t + 1, R("NM", SP, SP + L + 64))
            first = len(ops) - 1
        place("r", umm(R("pU", 64, 70), lambda j: R(lb, 16 + j, 112, 16)), ab)
        columns("r", 6, t, names)
        if t < NS - 1:
            ops[-K["back"]]["turn"] = [first]
        flex(R("ZR", 0, 1536, 16), R(lb, 16, 112), "VS", scale=-1.0)
        for a in range(0, 1536, 512):
            scan(R("yrr", a, a + 512), R("RZ"), R("ZR", a, a + 512), A.min, A.add)
        scores("r", 6, B, "yrr", "pK1", K["chr"])
        best("r", 6, "pK1", R("PC", 6, 7))
        ts(R("LVr", 0, 96), R("SLT"), R(lb, 15, 16), R("Ob", 0, 1), A.is_gt, A.max)
        winners("r", 6, R("GAr", 0, 96), plain("LVr", 0, 96), "a", "pD", whole=t < NS - 1)
        if t < NS - 1:
            mark(6, "a")
    for a in range(SP, SP + W, 512):
        flex(R("MB", a, a + 512), R("M", a, a + 512), "VS")
    for j in range(0, 6, 2):
        cp(R("MB"), R("ON", 0, 32), scat=R("OFa", j, j + 2))
    ya = R("YA", parts=slice(0, 48))
    ts(ya, py, -float(SP), -1.0, A.add, A.max)
    dma("Y", [(T.ya[:], ya[0])], [ya], [], 2000)
    for a in range(0, L, 256):
        ts(R("NI", a, a + 256), R("NM", SP + a, SP + a + 256), -64.0, None, A.add)
        cp(R("YO", a, a + 256), R("NI", a, a + 256))
        if a % 512:
            dma("Y", [(T.yo[:, a - 256:a + 256], T.YO[:, a - 256:a + 256])], [R("YO", a - 256, a + 256)], [], 3600)
    dma("Y", [(T.ym[:], T.MB[0:128:16, SP:SP + W])], [R("MB")], [], 2000)
    return ops


def depend(ops):
    hist = {}
    for i, o in enumerate(ops):
        d = set()
        for r, wr in [(r, False) for r in o["r"]] + [(r, True) for r in o["w"]]:
            ps = r[1] in _PS
            h = hist.setdefault(r[1], [])
            for j, r2, wr2 in h:
                if j == i:
                    continue
                if ps:
                    if o["grp"] is not None and o["grp"] == ops[j]["grp"]:
                        if ops[j]["first"]:
                            d.add(j)
                    elif wr or wr2 or len(o["alts"]) > 1 or set(o["alts"]) != set(ops[j]["alts"]):
                        d.add(j)
                elif (wr or wr2) and _clash(r, r2):
                    d.add(j)
            if wr and r[4] == 1 and not ps:
                h[:] = [e for e in h if not (r[2] <= e[1][2] and e[1][3] <= r[3])]
            if ps and o["grp"] is not None and o["first"]:
                h[:] = []
            h.append((i, r, wr))
        o["free"] = set(j for j in d if o["grp"] and ops[j]["grp"]) | (set(o.get("turn", ())) - d)
        o["dep"] = sorted(d | o["free"])


def label(o):
    return (o["w"][0][1] + "<" + (o["r"][-1 if o["grp"] else 0][1] if o["r"] else "")) if o["w"] else "out"


def schedule(ops):
    n = len(ops)
    succ = [[] for _ in range(n)]
    for i, o in enumerate(ops):
        for j in o["dep"]:
            succ[j].append(i)
    lat = K["lat"]
    pr = [0.0] * n
    for i in range(n - 1, -1, -1):
        c = min(a[1] for a in ops[i]["alts"].values()) + ops[i]["lat"] + ops[i].get("rest", 0.0) + EXTRA.get(label(ops[i]), 0.0)
        pr[i] = c + max([pr[j] + (0 if i in ops[j]["free"] else lat) for j in succ[i]], default=0.0)
    for i, o in enumerate(ops):
        pr[i] += o.get("boost", 0.0)
    prv = [pr[i] - (K["vpen"] if len(o["alts"]) > 1 else 0.0) for i, o in enumerate(ops)]
    left = [len(o["dep"]) for o in ops]
    ready = [0.0] * n
    now = {e: 0.0 for e in "VSPGY"}
    pool = {e: set(i for i in range(n) if not left[i] and e in ops[i]["alts"]) for e in now}
    order = {e: [] for e in now}
    done = 0
    while done < n:
        pick = None
        for e in now:
            if pool[e]:
                s = max(now[e], min(ready[i] for i in pool[e]))
                if pick is None or s < pick[0]:
                    pick = (s, e)
        s, e = pick
        c = pool[e]
        pe = prv if e == "V" else pr
        best = max((i for i in c if ready[i] <= s), key=lambda i: (pe[i], -i))
        dur = ops[best]["alts"][e][1]
        soon = [i for i in c if s < ready[i] < s + min(dur - K["tau"], K["look"]) and pe[i] > pe[best] + K["look2"] * dur]
        if soon:
            nxt = max(soon, key=lambda i: (pe[i], -i))
            fit = [i for i in c if ready[i] <= s and s + ops[i]["alts"][e][1] - K["tau"] <= ready[nxt]]
            best = max(fit, key=lambda i: (pe[i], -i)) if fit else nxt
            s = max(s, ready[best])
            dur = ops[best]["alts"][e][1]
        for e2 in ops[best]["alts"]:
            pool[e2].discard(best)
        order[e].append(best)
        now[e] = s + dur
        end = s + dur + ops[best]["lat"]
        for j in succ[best]:
            ready[j] = max(ready[j], end + (0 if best in ops[j]["free"] else lat))
            left[j] -= 1
            if not left[j]:
                for e2 in ops[j]["alts"]:
                    pool[e2].add(j)
        done += 1
    return order


def times(ops, order, c):
    cost, lt, lat = c
    st, end = {}, {}
    head = {e: 0 for e in order}
    now = {e: 0.0 for e in order}
    moved = True
    while moved:
        moved = False
        for e, l in order.items():
            while head[e] < len(l) and all(j in end for j in ops[l[head[e]]]["dep"]):
                i = l[head[e]]
                s = max([now[e]] + [end[j] + lt[j] + (0 if j in ops[i]["free"] else lat) for j in ops[i]["dep"]])
                st[i] = s
                end[i] = now[e] = s + cost[i][e]
                head[e] += 1
                moved = True
    return st, end


def fill(ops, seq, pre, c, rev):
    cost, lt, lat = c
    busy = {e: ([], []) for e in "VSPGY"}
    st, en, eg = {}, {}, {}
    for i in seq:
        o = ops[i]
        est = lt[i] if rev else 0.0
        for j in pre[i]:
            x = en[j] + (0 if j in o["free"] or i in ops[j]["free"] else lat) + (lt[i] if rev else lt[j])
            if x > est:
                est = x
        best = None
        for e, d in cost[i].items():
            S, E = busy[e]
            a, k = 0, len(E)
            while a < k:
                m = (a + k) // 2
                if E[m] <= est:
                    a = m + 1
                else:
                    k = m
            s = est
            while k < len(S) and S[k] < s + d - 1e-6:
                s = max(s, E[k])
                k += 1
            if best is None or s + d < best[0]:
                best = (s + d, s, e, k)
        f, s, e, k = best
        busy[e][0].insert(k, s)
        busy[e][1].insert(k, f)
        st[i], en[i], eg[i] = s, f, e
    return st, en, eg


def polish(ops, order, cs, rounds, seed, noise):
    n = len(ops)
    pre = [o["dep"] for o in ops]
    suc = [[] for _ in ops]
    for i, o in enumerate(ops):
        for j in o["dep"]:
            suc[j].append(i)

    def worth(od):
        return sum(max(e + c[1][i] for i, e in times(ops, od, c)[1].items()) / w for c, w in zip(cs, K["wt"]))
    best = (worth(order), order, times(ops, order, cs[0])[1])
    x = seed
    for it in range(rounds):
        key = {}
        for i in range(n - 1, -1, -1):
            x = (x * 1103515245 + 12345) % 2147483648
            v = best[2][i] + (noise * (x / 2147483648.0) if it and x % 16 == 0 else 0.0)
            key[i] = min([v] + [key[j] - 1e-3 for j in suc[i]])
        e2 = fill(ops, sorted(range(n), key=lambda i: (-key[i], -i)), suc, cs[0], True)[1]
        st, en, eg = fill(ops, sorted(range(n), key=lambda i: (-e2[i] - ops[i].get("boost", 0.0), i)), pre, cs[0], False)
        od = {e: sorted((i for i in range(n) if eg[i] == e), key=lambda i: (st[i], i)) for e in "VSPGY"}
        w = worth(od)
        if w < best[0]:
            best = (w, od, en)
    return best[1]


def anneal(ops, order, cs, sweeps, tries, width, heat, lam, seed):
    n = len(ops)
    E = "VSPGY"
    st0 = times(ops, order, cs[0])[0]
    eng = [0] * n
    for e, l in order.items():
        for i in l:
            eng[i] = E.index(e)
    seq = sorted(range(n), key=lambda i: (st0[i], i))
    dset, sset = [set(o["dep"]) for o in ops], [set() for o in ops]
    for i, d in enumerate(dset):
        for j in d:
            sset[j].add(i)
    alts = [[E.index(e) for e in o["alts"]] for o in ops]
    pull = [K["pull"] if label(o) in PULL else 1.0 for o in ops]
    mods = []
    for cost, lt, lat in cs:
        pre = [[(j, lt[j] + (0 if j in o["free"] else lat)) for j in o["dep"]] for o in ops]
        mods.append((pre, [[c.get(e, 0.0) for e in E] for c in cost], lt))
    x = [seed]

    def rnd(k):
        x[0] = (x[0] * 1103515245 + 12345) % 2147483648
        return (x[0] >> 8) % k
    for sw in range(sweeps):
        hot = heat * (1 - sw / sweeps) ** 2
        a = -rnd(width // 2)
        while a < n - 1:
            a0, b = max(a, 0), min(n, a + width)
            ctx = []
            for (pre, cost, lt), wt in zip(mods, K["wt"]):
                now, en = [0.0] * 5, [0.0] * n
                for i in seq[:a0]:
                    en[i] = now[eng[i]] = max([now[eng[i]]] + [en[j] + w for j, w in pre[i]]) + cost[i][eng[i]]
                qe, cross = [0.0] * 5, list(lt)
                for i in reversed(seq[b:]):
                    q = qe[eng[i]] = cost[i][eng[i]] + max(cross[i], qe[eng[i]])
                    for j, w in pre[i]:
                        cross[j] = max(cross[j], q + w)
                ctx.append((pre, cost, qe, cross, wt, [en, [(now, max([en[i] + cross[i] for i in seq[:a0]], default=0.0), 0.0)], 0.0]))

            def worth(win, lo, limit):
                tot, new = sum(c[5][2] for c in ctx), []
                for pre, cost, qe, cross, wt, (en, marks, was) in ctx:
                    en, marks = list(en), marks[:lo // 16 + 1]
                    now, top, acc = marks[-1]
                    now = list(now)
                    for p in range(lo // 16 * 16, len(win), 16):
                        for i in win[p:p + 16]:
                            e = eng[i]
                            s = now[e]
                            for j, w in pre[i]:
                                v = en[j] + w
                                if v > s:
                                    s = v
                            s += cost[i][e]
                            en[i] = now[e] = s
                            acc += s * pull[i]
                            s += cross[i]
                            if s > top:
                                top = s
                        marks.append((list(now), top, acc))
                    v = (max([top] + [u + v for u, v in zip(now, qe)]) + lam * acc / len(win)) / wt
                    tot += v - was
                    new.append([en, marks, v])
                    if tot > limit + 0.001:
                        return None, None
                return tot, new

            def keep(new):
                for c, s in zip(ctx, new):
                    c[5][:] = s
            win = seq[a0:b]
            m = len(win)
            cur, new = worth(win, 0, 1e9)
            keep(new)
            best = (cur, win, [eng[i] for i in win])
            for it in range(tries):
                p = rnd(m)
                i = win[p]
                kind, old = rnd(8), eng[i]
                if kind < 2 and len(alts[i]) > 1:
                    eng[i] = [e for e in alts[i] if e != old][rnd(len(alts[i]) - 1)]
                    w2, lo = win, p
                else:
                    step, hops, q = -1 if kind & 1 else 1, 1 + (rnd(3) * rnd(3) if rnd(6) else rnd(K["far"])), p
                    while hops and 0 <= q + step < m:
                        q += step
                        hops -= eng[win[q]] == old
                    mv, tie = {i}, sset if step < 0 else dset
                    for r in range(p + step, q + step, step):
                        if not mv.isdisjoint(tie[win[r]]):
                            mv.add(win[r])
                    if win[q] in mv:
                        continue
                    lo, hi = min(p, q), max(p, q) + 1
                    yes, no = [j for j in win[lo:hi] if j in mv], [j for j in win[lo:hi] if j not in mv]
                    w2 = win[:lo] + (yes + no if step < 0 else no + yes) + win[hi:]
                limit = cur + hot * rnd(1000) / 1000.0
                w, new = worth(w2, lo, limit)
                if new and w <= limit:
                    cur, win = w, w2
                    keep(new)
                    if w < best[0]:
                        best = (w, w2, [eng[j] for j in w2])
                else:
                    eng[i] = old
            seq[a0:b] = best[1]
            for j, e in zip(best[1], best[2]):
                eng[j] = e
            a += width // 2
        st0 = times(ops, {e: [i for i in seq if eng[i] == q] for q, e in enumerate(E)}, cs[0])[0]
        seq.sort(key=lambda i: st0[i])
    return {e: [i for i in seq if eng[i] == q] for q, e in enumerate(E)}


def emit(g, T, ops, order):
    queue = {"V": g.vector, "S": g.scalar, "P": g.tensor, "G": g, "Y": g.sync}
    eng, pos, last = {}, {}, {}
    for e in order:
        for p, i in enumerate(order[e]):
            eng[i], pos[i] = e, p
            if ops[i]["grp"]:
                last[ops[i]["grp"]] = i
    seen = {e: {} for e in order}
    know, waits, need = {}, {}, set()
    head = {e: 0 for e in order}
    moved = True
    while moved:
        moved = False
        for e in order:
            while head[e] < len(order[e]) and all(j in know for j in ops[order[e][head[e]]]["dep"]):
                i = order[e][head[e]]
                s = seen[e]
                ws = []
                for j in sorted(ops[i]["dep"], key=lambda j: -pos[j]):
                    if j in ops[i]["free"]:
                        continue
                    key = ops[j]["sem"][0] if ops[j]["sem"] else eng[j]
                    if s.get(key, -1) >= pos[j]:
                        continue
                    ws.append(j)
                    need.add(j)
                    s[key] = pos[j]
                    for k2, v in know[j].items():
                        if s.get(k2, -1) < v and "sent" not in ops[j]:
                            s[k2] = v
                waits[i] = ws
                know[i] = dict(s)
                head[e] += 1
                moved = True
    count, total = {}, {}
    for e in order:
        c = 0
        for i in order[e]:
            if not ops[i]["sem"] and i in need:
                c += 1
                count[i] = c
        total[e] = c
    sent = 0
    for e in order:
        q = queue[e]
        for i in order[e]:
            o = ops[i]
            for j in waits[i]:
                if ops[j]["sem"]:
                    q.wait_ge(T.sem[ops[j]["sem"][0]], ops[j]["sem"][1])
                else:
                    q.wait_ge(T.sem[eng[j]], count[j])
            f = o["alts"][e][0]
            ins = f(q, last[o["grp"]] == i) if o["grp"] else f(q)
            if i in count:
                ins.then_inc(T.sem[e], 1)
            sent += o.get("sent", 0)
    for e in "VSPG":
        if total[e]:
            g.sync.wait_ge(T.sem[e], total[e])
    for o in ops:
        if o["sem"]:
            g.sync.wait_ge(T.sem[o["sem"][0]], o["sem"][1])
    g.sync.wait_ge(T.sem.sent, sent)


def plan(g, core, T, topo, rank):
    cs = []
    for m in MODS[::-1]:
        K.update(m)
        ops = build(g, core, T, topo, rank)
        cs.insert(0, ([{e: a[1] for e, a in o["alts"].items()} for o in ops], [m["rem"] if "sent" in o else o["lat"] for o in ops], m["lat"]))
    depend(ops)
    return ops, cs, anneal(ops, polish(ops, schedule(ops), cs, K["rounds"], K["seed"], K["noise"]), cs, *K["anneal"])


def rank_program(g, core, T, topo):
    rank = T.rank_of(core)
    if rank is None:
        return
    if "o" not in _CACHE:
        ops, cs, order = plan(g, core, T, topo, rank)
        _CACHE["o"] = (order, [(o["dep"], o["free"]) for o in ops])
    ops = build(g, core, T, topo, rank)
    order, deps = _CACHE["o"]
    for o, d in zip(ops, deps):
        o["dep"], o["free"] = d
    emit(g, T, ops, order)
